import numpy as np
import ml_dtypes


def mxq(x, axis, fmt="e4m3"):
    dtype, down = {"e4m3": (ml_dtypes.float8_e4m3fn, 7), "e5m2": (ml_dtypes.float8_e5m2, 14)}[fmt]
    v = np.moveaxis(np.asarray(x, np.float32).astype(ml_dtypes.bfloat16).astype(np.float64), axis, -1)
    blocks = v.reshape(v.shape[:-1] + (-1, 32))
    amax = np.abs(blocks).max(-1, keepdims=True)
    byte = np.maximum(np.where(amax > 0, np.frexp(amax)[1] - 1 + 127, 0) - down, 1)
    scale = np.exp2(byte - 127.0)
    codes = (blocks / scale).astype(np.float32).astype(dtype).astype(np.float64)
    return np.moveaxis((codes * scale).reshape(v.shape), -1, axis)


WIDE = False


def mx_kscale(k):
    if not WIDE:
        return np.ones(k)
    levels = np.array([24, -24, 12, -12, 0])
    if k % 512:
        return np.exp2(np.random.permutation(np.resize(levels, k // 32))).repeat(32)
    a = np.empty((k // 512, 16))
    for p in range(k // 512):
        a[p, :8] = np.random.permutation(np.resize(levels, 8))
        for g in range(8):
            far = levels[np.abs(levels - a[p, g]) >= 10]
            a[p, g + 8] = far[np.random.randint(len(far))]
    return np.exp2(a.ravel()).repeat(32)


def f64(x):
    return np.asarray(x).astype(np.float64)


def striped(idx):
    return np.tile(idx.reshape(-1, 16).T, (8, 1)).astype(np.uint16)


def unstriped(offs):
    return offs[:16].T.reshape(-1).astype(np.int64)


E2M1 = np.array([0.0, 0.5, 1.0, 1.5, 2.0, 3.0, 4.0, 6.0, -0.0, -0.5, -1.0, -1.5, -2.0, -3.0, -4.0, -6.0])


def pack_weight(w, fmt):
    k, n = w.shape
    w = f64(np.asarray(w, np.float32).astype(ml_dtypes.bfloat16)).reshape(k // 32, 32, n)
    amax = np.abs(w).max(1)
    if fmt == "e4m3":
        byte = np.frexp(amax)[1] - 1 + 127 - 7
    else:
        mant, ex = np.frexp(amax / 6.0)
        byte = np.where(mant > 0.5, ex, ex - 1) + 127
    byte = np.clip(np.where(amax > 0, byte, 1), 1, 254)
    scaled = (w * np.exp2(127.0 - byte)[:, None, :]).reshape(k, n).astype(np.float32)
    by_word = np.ascontiguousarray(scaled.reshape(k // 512, 128, 4, n).transpose(0, 1, 3, 2))
    if fmt == "e4m3":
        words = by_word.astype(ml_dtypes.float8_e4m3fn).view(np.uint8)
    else:
        c = by_word.astype(ml_dtypes.float4_e2m1fn).view(np.uint8) & 0xF
        words = (c[..., 0::2] | (c[..., 1::2] << 4)).reshape(k // 512, 128, 2 * n)
    return np.ascontiguousarray(words), np.ascontiguousarray(byte.astype(np.uint8).reshape(k // 512, 16, n))


def unpack_weight(words, scales, fmt):
    g, _, n = scales.shape
    words = np.ascontiguousarray(words).reshape(g, 128, n, -1)
    if fmt == "e4m3":
        vals = words.view(ml_dtypes.float8_e4m3fn).astype(np.float64)
    else:
        nib = np.empty((g, 128, n, 4), np.uint8)
        nib[..., 0::2] = words & 0xF
        nib[..., 1::2] = words >> 4
        vals = E2M1[nib]
    vals = vals * np.repeat(np.exp2(scales.astype(np.float64) - 127.0), 8, axis=1)[..., None]
    return vals.transpose(0, 1, 3, 2).reshape(g * 512, n)


def pack_table4(v):
    words, scales = pack_weight(v, "e2m1")
    g, t = words.shape[0] // 2, v.shape[1]
    return np.ascontiguousarray(words.reshape(g, 2, 128, t, 2).transpose(0, 2, 3, 1, 4).reshape(g, 128, t, 4)), scales


def unpack_table4(words, scales):
    g, _, t, _ = words.shape
    return unpack_weight(words.reshape(g, 128, t, 2, 2).transpose(0, 3, 1, 2, 4).reshape(2 * g, 128, 2 * t), scales, "e2m1")


K, M, N, J, T = 1024, 512, 512, 1024, 4096


def setup_inputs():
    n = np.random.standard_normal
    s = mx_kscale(K)[:, None]
    u = mx_kscale(J)[:, None]
    al = n((J, N)) / np.sqrt(J) / u
    p_tab = pack_table4(0.5 * n((K, T)) / np.sqrt(K) / s)
    p_al8 = pack_weight(al[:512], "e4m3")
    p_al4 = pack_weight(al[512:], "e2m1")
    return {
        "x": (n((K, M)) * s).astype(np.float32),
        "tab_words": p_tab[0],
        "tab_scales": p_tab[1],
        "cw": (np.random.uniform(0.5, 2.0, J) * u[:, 0]).astype(np.float32),
        "cb": (0.3 * n(J)).astype(np.float32),
        "al8_words": p_al8[0],
        "al8_scales": p_al8[1],
        "al4_words": p_al4[0],
        "al4_scales": p_al4[1],
        "res": (n((N, M))).astype(np.float32),
        "offs": striped(np.random.permutation(T)[:J]),
    }


def reference(x, tab_words, tab_scales, cw, cb, al8_words, al8_scales, al4_words, al4_scales, res, offs):
    idx = unstriped(offs)
    x_ = mxq(f64(x), 0, "e4m3")
    tab_ = unpack_table4(tab_words, tab_scales)[:, idx]
    d = tab_.T @ x_
    h = f64(cw)[:, None] * (d + f64(cb)[:, None]) ** 2
    h_ = mxq(h, 0, "e4m3")
    al8_ = unpack_weight(al8_words, al8_scales, "e4m3")
    al4_ = unpack_weight(al4_words, al4_scales, "e2m1")
    y = al8_.T @ h_[:512] + al4_.T @ h_[512:]
    return f64(res) + y

@@ -1,0 +1,193 @@
+from contextlib import ExitStack
+
+import concourse.mybir as mybir
+
+K, M, N, J, T = 1024, 512, 512, 1024, 4096
+FLOPS = 2 * K * J * M + 2 * J * N * M
+
+F32 = mybir.dt.float32
+BF16 = mybir.dt.bfloat16
+I32 = mybir.dt.int32
+U32 = mybir.dt.uint32
+U16 = mybir.dt.uint16
+U8 = mybir.dt.uint8
+E4M3 = mybir.dt.float8_e4m3fn_x4
+E2M1 = mybir.dt.float4_e2m1fn_x4
+ACT = mybir.ActivationFunctionType
+ALU = mybir.AluOpType
+
+P = 128
+PACK = 4
+HALF = M // 2
+
+
+def tile_list_kernl_poly2_mix_res_kernel(
+    tc, x, tab_words, tab_scales, cw, cb, al8_words, al8_scales, al4_words, al4_scales, res, offs, out
+):
+    nc = tc.nc
+    with ExitStack() as ctx:
+        keep = ctx.enter_context(tc.tile_pool(name="keep", bufs=1))
+        stage = ctx.enter_context(tc.tile_pool(name="stage", bufs=1))
+        psum = ctx.enter_context(tc.psum_pool(name="psum", bufs=1))
+
+        offsets = keep.tile([P, J // 16], U16, name="offsets")
+        nc.sync.dma_start(offsets[:], offs)
+
+        scale_rows = keep.tile([P, T], U8, name="scale_rows", align_bytes=64)
+        nc.sync.dma_start(
+            scale_rows[0:32, :].bitcast(I32), tab_scales.rearrange("a q t -> (a q) t").bitcast(I32)
+        )
+        nc.vector.memset(scale_rows[64:128, :].bitcast(I32), 0)
+        nc.vector.memset(scale_rows[32:64, :].bitcast(I32), 0)
+
+        x_raw = [stage.tile([P, PACK, M], F32, name="x_raw%d" % a, offset=8192 * a, align_bytes=64) for a in range(2)]
+        x_rows = x.rearrange("(a p t) m -> a p t m", a=2, t=PACK)
+        table = keep.tile([P, T], I32, name="table", align_bytes=64)
+        nc.sync.dma_start(table[:], tab_words[0].rearrange("p t f -> p (t f)").bitcast(I32))
+        nc.sync.dma_start(x_raw[0][:], x_rows[0])
+        nc.sync.dma_start(x_raw[1][:], x_rows[1])
+
+        cw_sb = keep.tile([P, 2, PACK], F32, name="cw_sb")
+        cb_sb = keep.tile([P, 2, PACK], F32, name="cb_sb")
+        nc.gpsimd.dma_start(cb_sb[:], cb.rearrange("(b p t) -> p b t", b=2, t=PACK))
+        nc.gpsimd.dma_start(cw_sb[:], cw.rearrange("(b p t) -> p b t", b=2, t=PACK))
+
+        plane1 = keep.tile([P, J], U8, name="plane1", align_bytes=64)
+        nc.gpsimd.memset(plane1[:].bitcast(I32), 0)
+
+        picked_scales = keep.tile([P, J], U8, name="picked_scales", align_bytes=64)
+        nc.vector.tensor_copy(picked_scales[:], scale_rows[:].indirect(offsets[:]))
+        plane0 = keep.tile([P, J], U8, name="plane0", align_bytes=64)
+        nc.vector.tensor_copy(
+            plane0[:].rearrange("p (b t m) -> p b t m", b=2, t=PACK),
+            picked_scales[:].rearrange("p (b m t) -> p b t m", b=2, t=PACK),
+        )
+        for q in range(1, 4):
+            nc.scalar.dma_start(plane0[32 * q : 32 * q + 4, :].bitcast(I32), plane0[4 * q : 4 * q + 4, :].bitcast(I32))
+        for q in range(4):
+            nc.sync.dma_start(
+                plane1[32 * q : 32 * q + 4, :].bitcast(I32), plane0[16 + 4 * q : 20 + 4 * q, :].bitcast(I32)
+            )
+        tab_plane = (plane0, plane1)
+
+        x_codes = [keep.tile([P, M], U32, name="x_codes%d" % a, align_bytes=64) for a in range(2)]
+        x_scale = [keep.tile([P, M], U8, name="x_scale%d" % a, align_bytes=64) for a in range(2)]
+
+        def quantize_x(a, lo, hi, on_vector, tag):
+            grouped = keep.tile([P, hi - lo, PACK], BF16, name="x_grouped%d_%d" % (a, lo), tag=tag, align_bytes=64)
+            dst = grouped[:].rearrange("p (c i) t -> p c t i", i=4)
+            src = x_raw[a][:, :, lo:hi].rearrange("p t (c i) -> p c t i", i=4)
+            if on_vector:
+                nc.vector.tensor_copy(dst, src)
+            else:
+                nc.scalar.activation(dst, src, ACT.Copy)
+            nc.vector.quantize_mx(
+                out=x_codes[a][:, lo:hi].bitcast(E4M3),
+                scales=x_scale[a][:, lo:hi],
+                in_=grouped[:].rearrange("p m t -> p (m t)"),
+            )
+
+        def pick_centres(b, tag):
+            picked = keep.tile([P, 512], U32, name="picked_words%d" % b, tag=tag, align_bytes=64)
+            nc.vector.tensor_copy(
+                picked[:].rearrange("p (t m) -> p m t", t=PACK),
+                table[:].bitcast(U32).indirect(offsets[:, 32 * b : 32 * (b + 1)]),
+            )
+            parted = keep.tile([P, 2, 1024], U8, name="centres%d" % b, align_bytes=64)
+            nc.vector.tensor_copy(
+                parted[:].bitcast(U16).rearrange("p a (c i) -> p c a i", i=8),
+                picked[:].bitcast(U16).rearrange("p (c i a) -> p c a i", i=8, a=2),
+            )
+            return parted
+
+        centres = [pick_centres(0, "pw0")]
+        quantize_x(0, 0, HALF, True, "xg0")
+        quantize_x(0, HALF, M, False, "xg0s")
+        quantize_x(1, 0, HALF, True, "xg1")
+        quantize_x(1, HALF, M, False, "late")
+        centres.append(pick_centres(1, "late"))
+
+        al8 = stage.tile([P, N], I32, name="al8", offset=0, align_bytes=64)
+        nc.sync.dma_start(al8[:], al8_words[0].rearrange("p n f -> p (n f)").bitcast(I32))
+        al4 = stage.tile([P, 2 * N], U8, name="al4", offset=2048, align_bytes=64)
+        nc.sync.dma_start(al4[:].bitcast(I32), al4_words[0].bitcast(I32))
+        al_planes = stage.tile([P, 2, N], U8, name="al_planes", offset=3072, align_bytes=64)
+        nc.gpsimd.memset(al_planes[:].rearrange("p a n -> p (a n)").bitcast(I32), 0)
+        for a, src in enumerate((al8_scales, al4_scales)):
+            for q in range(4):
+                nc.sync.dma_start(
+                    al_planes[32 * q : 32 * q + 4, a, :].bitcast(I32), src[0, 4 * q : 4 * q + 4, :].bitcast(I32)
+                )
+        res_sb = stage.tile([P, 4, M], F32, name="res_sb", offset=8192, align_bytes=64)
+        nc.sync.dma_start(res_sb[:], res.rearrange("(c p) m -> p c m", p=P))
+
+        h_codes, h_scale = [], []
+        for b in range(2):
+            dots = [psum.tile([P, M], F32, name="dot%d_%d" % (b, t), tag="bank%d" % (4 * b + t)) for t in range(PACK)]
+            order = [(a, t) for a in range(2) for t in range(PACK)] if b == 0 else [(a, t) for t in range(PACK) for a in range(2)]
+            for a, t in order:
+                col = 512 * b + P * t
+                nc.tensor.matmul_mx(
+                    out=dots[t][:],
+                    lhsT=centres[b][:, a, 2 * P * t : 2 * P * (t + 1)].bitcast(E2M1),
+                    lhsT_scale=tab_plane[a][:, col : col + P],
+                    rhs=x_codes[a][:].bitcast(E4M3),
+                    rhs_scale=x_scale[a][:],
+                    start=(a == 0),
+                    stop=(a == 1),
+                )
+            codes = keep.tile([P, M], U32, name="h_codes%d" % b, align_bytes=64)
+            scale = keep.tile([P, M], U8, name="h_scale%d" % b, align_bytes=64)
+            grouped = []
+            for half in range(2):
+                grouped.append(
+                    keep.tile([P, HALF, PACK], BF16, name="h_grouped%d_%d" % (b, half), tag="hg%d" % half, align_bytes=64)
+                )
+                cols = slice(HALF * half, HALF * (half + 1))
+                squares = keep.tile([P, PACK, HALF], F32, name="squares%d_%d" % (b, half))
+                for t in range(PACK):
+                    nc.scalar.activation(squares[:, t, :], dots[t][:, cols], ACT.Square, bias=cb_sb[:, b, t : t + 1])
+                nc.vector.tensor_tensor(
+                    grouped[half][:].rearrange("p (c i) t -> p c t i", i=4),
+                    squares[:].rearrange("p t (c i) -> p c t i", i=4),
+                    cw_sb[:, b, :].rearrange("p (o t u) -> p o t u", o=1, u=1).to_broadcast([P, HALF // 4, PACK, 4]),
+                    ALU.mult,
+                )
+            for half in range(2):
+                cols = slice(HALF * half, HALF * (half + 1))
+                nc.vector.quantize_mx(
+                    out=codes[:, cols].bitcast(E4M3),
+                    scales=scale[:, cols],
+                    in_=grouped[half][:].rearrange("p m t -> p (m t)"),
+                )
+            h_codes.append(codes)
+            h_scale.append(scale)
+
+        sums = [psum.tile([P, M], F32, name="sum%d" % c, tag="bank%d" % c) for c in range(4)]
+        for c in range(4):
+            nc.tensor.matmul_mx(
+                out=sums[c][:],
+                lhsT=al8[:, P * c : P * (c + 1)].bitcast(E4M3),
+                lhsT_scale=al_planes[:, 0, P * c : P * (c + 1)],
+                rhs=h_codes[0][:].bitcast(E4M3),
+                rhs_scale=h_scale[0][:],
+                start=True,
+                stop=False,
+            )
+        for half in range(2):
+            for c in range(4):
+                for quarter in range(2 * half, 2 * half + 2):
+                    cols = slice(P * quarter, P * (quarter + 1))
+                    nc.tensor.matmul_mx(
+                        out=sums[c][:, cols],
+                        lhsT=al4[:, 2 * P * c : 2 * P * (c + 1)].bitcast(E2M1),
+                        lhsT_scale=al_planes[:, 1, P * c : P * (c + 1)],
+                        rhs=h_codes[1][:, cols].bitcast(E4M3),
+                        rhs_scale=h_scale[1][:, cols],
+                        start=False,
+                        stop=(quarter == 3),
+                    )
+        for c in range(4):
+            result = keep.tile([P, M], F32, name="result%d" % c)
+            nc.vector.tensor_tensor(result[:], sums[c][:], res_sb[:, c, :], ALU.add)
+            nc.sync.dma_start(out[P * c : P * (c + 1), :], result[:])

@@ -40,12 +40,21 @@ def tile_list_kernl_poly2_mix_res_kernel(
         nc.vector.memset(scale_rows[64:128, :].bitcast(I32), 0)
         nc.vector.memset(scale_rows[32:64, :].bitcast(I32), 0)
 
-        x_raw = [stage.tile([P, PACK, M], F32, name="x_raw%d" % a, offset=8192 * a, align_bytes=64) for a in range(2)]
-        x_rows = x.rearrange("(a p t) m -> a p t m", a=2, t=PACK)
         table = keep.tile([P, T], I32, name="table", align_bytes=64)
         nc.sync.dma_start(table[:], tab_words[0].rearrange("p t f -> p (t f)").bitcast(I32))
-        nc.sync.dma_start(x_raw[0][:], x_rows[0])
-        nc.sync.dma_start(x_raw[1][:], x_rows[1])
+
+        x_rows = x.rearrange("(a p t) m -> a p t m", a=2, t=PACK)
+        x_raw = {}
+
+        def load_x(half, a):
+            raw = stage.tile(
+                [P, PACK, HALF], F32, name="x_raw%d_%d" % (half, a), offset=4096 * (2 * half + a), align_bytes=64
+            )
+            nc.sync.dma_start(raw[:], x_rows[a][:, :, HALF * half : HALF * (half + 1)])
+            x_raw[half, a] = raw
+
+        load_x(0, 0)
+        load_x(0, 1)
 
         cw_sb = keep.tile([P, 2, PACK], F32, name="cw_sb")
         cb_sb = keep.tile([P, 2, PACK], F32, name="cb_sb")
@@ -55,7 +64,7 @@ def tile_list_kernl_poly2_mix_res_kernel(
         plane1 = keep.tile([P, J], U8, name="plane1", align_bytes=64)
         nc.gpsimd.memset(plane1[:].bitcast(I32), 0)
 
-        picked_scales = keep.tile([P, J], U8, name="picked_scales", align_bytes=64)
+        picked_scales = stage.tile([P, J], U8, name="picked_scales", offset=4096 * 3 - 512, align_bytes=64)
         nc.vector.tensor_copy(picked_scales[:], scale_rows[:].indirect(offsets[:]))
         plane0 = keep.tile([P, J], U8, name="plane0", align_bytes=64)
         nc.vector.tensor_copy(
@@ -63,49 +72,53 @@ def tile_list_kernl_poly2_mix_res_kernel(
             picked_scales[:].rearrange("p (b m t) -> p b t m", b=2, t=PACK),
         )
         for q in range(1, 4):
-            nc.scalar.dma_start(plane0[32 * q : 32 * q + 4, :].bitcast(I32), plane0[4 * q : 4 * q + 4, :].bitcast(I32))
+            nc.sync.dma_start(plane0[32 * q : 32 * q + 4, :].bitcast(I32), plane0[4 * q : 4 * q + 4, :].bitcast(I32))
         for q in range(4):
-            nc.sync.dma_start(
+            queue = nc.sync if q < 2 else nc.gpsimd
+            queue.dma_start(
                 plane1[32 * q : 32 * q + 4, :].bitcast(I32), plane0[16 + 4 * q : 20 + 4 * q, :].bitcast(I32)
             )
         tab_plane = (plane0, plane1)
+        load_x(1, 0)
+        load_x(1, 1)
 
-        x_codes = [keep.tile([P, M], U32, name="x_codes%d" % a, align_bytes=64) for a in range(2)]
-        x_scale = [keep.tile([P, M], U8, name="x_scale%d" % a, align_bytes=64) for a in range(2)]
+        x_codes, x_scale = {}, {}
 
-        def quantize_x(a, lo, hi, on_vector, tag):
-            grouped = keep.tile([P, hi - lo, PACK], BF16, name="x_grouped%d_%d" % (a, lo), tag=tag, align_bytes=64)
+        def quantize_x(half, a, on_vector, tag):
+            grouped = keep.tile([P, HALF, PACK], BF16, name="x_grouped%d_%d" % (half, a), tag=tag, align_bytes=64)
             dst = grouped[:].rearrange("p (c i) t -> p c t i", i=4)
-            src = x_raw[a][:, :, lo:hi].rearrange("p t (c i) -> p c t i", i=4)
+            src = x_raw[half, a][:].rearrange("p t (c i) -> p c t i", i=4)
             if on_vector:
                 nc.vector.tensor_copy(dst, src)
             else:
                 nc.scalar.activation(dst, src, ACT.Copy)
+            codes = keep.tile([P, HALF], U32, name="x_codes%d_%d" % (half, a), align_bytes=64)
+            scale = keep.tile([P, HALF], U8, name="x_scale%d_%d" % (half, a), align_bytes=64)
             nc.vector.quantize_mx(
-                out=x_codes[a][:, lo:hi].bitcast(E4M3),
-                scales=x_scale[a][:, lo:hi],
-                in_=grouped[:].rearrange("p m t -> p (m t)"),
+                out=codes[:].bitcast(E4M3), scales=scale[:], in_=grouped[:].rearrange("p m t -> p (m t)")
             )
+            x_codes[half, a] = codes
+            x_scale[half, a] = scale
 
-        def pick_centres(b, tag):
-            picked = keep.tile([P, 512], U32, name="picked_words%d" % b, tag=tag, align_bytes=64)
+        def pick_centres(b, picked_tag, parted_tag):
+            picked = keep.tile([P, 512], U32, name="picked_words%d" % b, tag=picked_tag, align_bytes=64)
             nc.vector.tensor_copy(
                 picked[:].rearrange("p (t m) -> p m t", t=PACK),
                 table[:].bitcast(U32).indirect(offsets[:, 32 * b : 32 * (b + 1)]),
             )
-            parted = keep.tile([P, 2, 1024], U8, name="centres%d" % b, align_bytes=64)
+            parted = keep.tile([P, 2, 1024], U8, name="centres%d" % b, tag=parted_tag, align_bytes=64)
             nc.vector.tensor_copy(
                 parted[:].bitcast(U16).rearrange("p a (c i) -> p c a i", i=8),
                 picked[:].bitcast(U16).rearrange("p (c i a) -> p c a i", i=8, a=2),
             )
             return parted
 
-        centres = [pick_centres(0, "pw0")]
-        quantize_x(0, 0, HALF, True, "xg0")
-        quantize_x(0, HALF, M, False, "xg0s")
-        quantize_x(1, 0, HALF, True, "xg1")
-        quantize_x(1, HALF, M, False, "late")
-        centres.append(pick_centres(1, "late"))
+        centres = [pick_centres(0, "pw0", "c0")]
+        quantize_x(0, 0, False, "xg00")
+        quantize_x(0, 1, False, "xg01")
+        centres.append(pick_centres(1, "xg00", "xg01"))
+        quantize_x(1, 0, False, "xg10")
+        quantize_x(1, 1, True, "hg0")
 
         al8 = stage.tile([P, N], I32, name="al8", offset=0, align_bytes=64)
         nc.sync.dma_start(al8[:], al8_words[0].rearrange("p n f -> p (n f)").bitcast(I32))
@@ -118,76 +131,88 @@ def tile_list_kernl_poly2_mix_res_kernel(
                 nc.sync.dma_start(
                     al_planes[32 * q : 32 * q + 4, a, :].bitcast(I32), src[0, 4 * q : 4 * q + 4, :].bitcast(I32)
                 )
-        res_sb = stage.tile([P, 4, M], F32, name="res_sb", offset=8192, align_bytes=64)
-        nc.sync.dma_start(res_sb[:], res.rearrange("(c p) m -> p c m", p=P))
+        res_rows = res.rearrange("(c p) m -> p c m", p=P)
+        res_sb = []
+        for half in range(2):
+            part = stage.tile([P, 4, HALF], F32, name="res%d" % half, offset=4096 * (1 + half), align_bytes=64)
+            nc.sync.dma_start(part[:], res_rows[:, :, HALF * half : HALF * (half + 1)])
+            res_sb.append(part)
+        out_rows = out.rearrange("(c p) m -> p c m", p=P)
 
-        h_codes, h_scale = [], []
-        for b in range(2):
-            dots = [psum.tile([P, M], F32, name="dot%d_%d" % (b, t), tag="bank%d" % (4 * b + t)) for t in range(PACK)]
-            order = [(a, t) for a in range(2) for t in range(PACK)] if b == 0 else [(a, t) for t in range(PACK) for a in range(2)]
+        h_codes, h_scale = {}, {}
+
+        def kernel_values(half, b):
+            dots = [
+                psum.tile([P, HALF], F32, name="dot%d_%d_%d" % (half, b, t), tag="bank%d" % (4 * b + t))
+                for t in range(PACK)
+            ]
+            if half == 0 and b == 0:
+                order = [(a, t) for a in range(2) for t in range(PACK)]
+            else:
+                order = [(a, t) for t in range(PACK) for a in range(2)]
             for a, t in order:
                 col = 512 * b + P * t
-                nc.tensor.matmul_mx(
-                    out=dots[t][:],
-                    lhsT=centres[b][:, a, 2 * P * t : 2 * P * (t + 1)].bitcast(E2M1),
-                    lhsT_scale=tab_plane[a][:, col : col + P],
-                    rhs=x_codes[a][:].bitcast(E4M3),
-                    rhs_scale=x_scale[a][:],
-                    start=(a == 0),
-                    stop=(a == 1),
-                )
-            codes = keep.tile([P, M], U32, name="h_codes%d" % b, align_bytes=64)
-            scale = keep.tile([P, M], U8, name="h_scale%d" % b, align_bytes=64)
-            grouped = []
-            for half in range(2):
-                grouped.append(
-                    keep.tile([P, HALF, PACK], BF16, name="h_grouped%d_%d" % (b, half), tag="hg%d" % half, align_bytes=64)
-                )
-                cols = slice(HALF * half, HALF * (half + 1))
-                squares = keep.tile([P, PACK, HALF], F32, name="squares%d_%d" % (b, half))
-                for t in range(PACK):
-                    nc.scalar.activation(squares[:, t, :], dots[t][:, cols], ACT.Square, bias=cb_sb[:, b, t : t + 1])
-                nc.vector.tensor_tensor(
-                    grouped[half][:].rearrange("p (c i) t -> p c t i", i=4),
-                    squares[:].rearrange("p t (c i) -> p c t i", i=4),
-                    cw_sb[:, b, :].rearrange("p (o t u) -> p o t u", o=1, u=1).to_broadcast([P, HALF // 4, PACK, 4]),
-                    ALU.mult,
-                )
-            for half in range(2):
-                cols = slice(HALF * half, HALF * (half + 1))
-                nc.vector.quantize_mx(
-                    out=codes[:, cols].bitcast(E4M3),
-                    scales=scale[:, cols],
-                    in_=grouped[half][:].rearrange("p m t -> p (m t)"),
-                )
-            h_codes.append(codes)
-            h_scale.append(scale)
-
-        sums = [psum.tile([P, M], F32, name="sum%d" % c, tag="bank%d" % c) for c in range(4)]
-        for c in range(4):
-            nc.tensor.matmul_mx(
-                out=sums[c][:],
-                lhsT=al8[:, P * c : P * (c + 1)].bitcast(E4M3),
-                lhsT_scale=al_planes[:, 0, P * c : P * (c + 1)],
-                rhs=h_codes[0][:].bitcast(E4M3),
-                rhs_scale=h_scale[0][:],
-                start=True,
-                stop=False,
-            )
-        for half in range(2):
-            for c in range(4):
-                for quarter in range(2 * half, 2 * half + 2):
-                    cols = slice(P * quarter, P * (quarter + 1))
+                for u in range(2):
+                    cols = slice(P * u, P * (u + 1))
                     nc.tensor.matmul_mx(
-                        out=sums[c][:, cols],
-                        lhsT=al4[:, 2 * P * c : 2 * P * (c + 1)].bitcast(E2M1),
-                        lhsT_scale=al_planes[:, 1, P * c : P * (c + 1)],
-                        rhs=h_codes[1][:, cols].bitcast(E4M3),
-                        rhs_scale=h_scale[1][:, cols],
-                        start=False,
-                        stop=(quarter == 3),
+                        out=dots[t][:, cols],
+                        lhsT=centres[b][:, a, 2 * P * t : 2 * P * (t + 1)].bitcast(E2M1),
+                        lhsT_scale=tab_plane[a][:, col : col + P],
+                        rhs=x_codes[half, a][:, cols].bitcast(E4M3),
+                        rhs_scale=x_scale[half, a][:, cols],
+                        start=(a == 0 and u == 0),
+                        stop=(a == 1 and u == 1),
                     )
-        for c in range(4):
-            result = keep.tile([P, M], F32, name="result%d" % c)
-            nc.vector.tensor_tensor(result[:], sums[c][:], res_sb[:, c, :], ALU.add)
-            nc.sync.dma_start(out[P * c : P * (c + 1), :], result[:])
+            squares = keep.tile([P, PACK, HALF], F32, name="squares%d_%d" % (half, b))
+            for t in range(PACK):
+                nc.scalar.activation(squares[:, t, :], dots[t][:], ACT.Square, bias=cb_sb[:, b, t : t + 1])
+            grouped = keep.tile([P, HALF, PACK], BF16, name="h_grouped%d_%d" % (half, b), tag="hg%d" % b, align_bytes=64)
+            nc.vector.tensor_tensor(
+                grouped[:].rearrange("p (c i) t -> p c t i", i=4),
+                squares[:].rearrange("p t (c i) -> p c t i", i=4),
+                cw_sb[:, b, :].rearrange("p (o t u) -> p o t u", o=1, u=1).to_broadcast([P, HALF // 4, PACK, 4]),
+                ALU.mult,
+            )
+            codes = keep.tile([P, HALF], U32, name="h_codes%d_%d" % (half, b), align_bytes=64)
+            scale = keep.tile([P, HALF], U8, name="h_scale%d_%d" % (half, b), align_bytes=64)
+            nc.vector.quantize_mx(
+                out=codes[:].bitcast(E4M3), scales=scale[:], in_=grouped[:].rearrange("p m t -> p (m t)")
+            )
+            h_codes[half, b] = codes
+            h_scale[half, b] = scale
+
+        def outputs(half):
+            for pair in range(2):
+                sums = psum.tile([P, 2, HALF], F32, name="sum%d_%d" % (half, pair), tag="bank%d" % (4 * half + pair))
+                for i in range(2):
+                    c = 2 * pair + i
+                    nc.tensor.matmul_mx(
+                        out=sums[:, i, :],
+                        lhsT=al8[:, P * c : P * (c + 1)].bitcast(E4M3),
+                        lhsT_scale=al_planes[:, 0, P * c : P * (c + 1)],
+                        rhs=h_codes[half, 0][:].bitcast(E4M3),
+                        rhs_scale=h_scale[half, 0][:],
+                        start=True,
+                        stop=False,
+                    )
+                    for u in range(2):
+                        cols = slice(P * u, P * (u + 1))
+                        nc.tensor.matmul_mx(
+                            out=sums[:, i, cols],
+                            lhsT=al4[:, 2 * P * c : 2 * P * (c + 1)].bitcast(E2M1),
+                            lhsT_scale=al_planes[:, 1, P * c : P * (c + 1)],
+                            rhs=h_codes[half, 1][:, cols].bitcast(E4M3),
+                            rhs_scale=h_scale[half, 1][:, cols],
+                            start=False,
+                            stop=(u == 1),
+                        )
+                result = keep.tile([P, 2, HALF], F32, name="result%d_%d" % (half, pair))
+                nc.vector.tensor_tensor(result[:], sums[:], res_sb[half][:, 2 * pair : 2 * pair + 2, :], ALU.add)
+                nc.sync.dma_start(out_rows[:, 2 * pair : 2 * pair + 2, HALF * half : HALF * (half + 1)], result[:])
+
+        kernel_values(0, 0)
+        kernel_values(0, 1)
+        kernel_values(1, 0)
+        kernel_values(1, 1)
+        outputs(0)
+        outputs(1)

@@ -86,8 +86,8 @@ def tile_list_kernl_poly2_mix_res_kernel(
 
         def quantize_x(half, a, on_vector, tag):
             grouped = keep.tile([P, HALF, PACK], BF16, name="x_grouped%d_%d" % (half, a), tag=tag, align_bytes=64)
-            dst = grouped[:].rearrange("p (c i) t -> p c t i", i=4)
-            src = x_raw[half, a][:].rearrange("p t (c i) -> p c t i", i=4)
+            dst = grouped[:].rearrange("p (c i) t -> p c t i", i=2)
+            src = x_raw[half, a][:].rearrange("p t (c i) -> p c t i", i=2)
             if on_vector:
                 nc.vector.tensor_copy(dst, src)
             else:
@@ -108,8 +108,8 @@ def tile_list_kernl_poly2_mix_res_kernel(
             )
             parted = keep.tile([P, 2, 1024], U8, name="centres%d" % b, tag=parted_tag, align_bytes=64)
             nc.vector.tensor_copy(
-                parted[:].bitcast(U16).rearrange("p a (c i) -> p c a i", i=8),
-                picked[:].bitcast(U16).rearrange("p (c i a) -> p c a i", i=8, a=2),
+                parted[:].bitcast(U16),
+                picked[:].bitcast(U16).rearrange("p (c a) -> p a c", a=2),
             )
             return parted
 
@@ -168,9 +168,9 @@ def tile_list_kernl_poly2_mix_res_kernel(
                 nc.scalar.activation(squares[:, t, :], dots[t][:], ACT.Square, bias=cb_sb[:, b, t : t + 1])
             grouped = keep.tile([P, HALF, PACK], BF16, name="h_grouped%d_%d" % (half, b), tag="hg%d" % b, align_bytes=64)
             nc.vector.tensor_tensor(
-                grouped[:].rearrange("p (c i) t -> p c t i", i=4),
-                squares[:].rearrange("p t (c i) -> p c t i", i=4),
-                cw_sb[:, b, :].rearrange("p (o t u) -> p o t u", o=1, u=1).to_broadcast([P, HALF // 4, PACK, 4]),
+                grouped[:].rearrange("p (c i) t -> p c t i", i=2),
+                squares[:].rearrange("p t (c i) -> p c t i", i=2),
+                cw_sb[:, b, :].rearrange("p (o t u) -> p o t u", o=1, u=1).to_broadcast([P, HALF // 2, PACK, 2]),
                 ALU.mult,
             )
             codes = keep.tile([P, HALF], U32, name="h_codes%d_%d" % (half, b), align_bytes=64)
@@ -206,7 +206,8 @@ def tile_list_kernl_poly2_mix_res_kernel(
                             start=False,
                             stop=(u == 1),
                         )
-                result = keep.tile([P, 2, HALF], F32, name="result%d_%d" % (half, pair))
+                tag = "hg1" if (half, pair) == (0, 1) else "result%d_%d" % (half, pair)
+                result = keep.tile([P, 2, HALF], F32, name="result%d_%d" % (half, pair), tag=tag, align_bytes=64)
                 nc.vector.tensor_tensor(result[:], sums[:], res_sb[half][:, 2 * pair : 2 * pair + 2, :], ALU.add)
                 nc.sync.dma_start(out_rows[:, 2 * pair : 2 * pair + 2, HALF * half : HALF * (half + 1)], result[:])
 

@@ -134,7 +134,7 @@ def tile_list_kernl_poly2_mix_res_kernel(
         res_rows = res.rearrange("(c p) m -> p c m", p=P)
         res_sb = []
         for half in range(2):
-            part = stage.tile([P, 4, HALF], F32, name="res%d" % half, offset=4096 * (1 + half), align_bytes=64)
+            part = stage.tile([P, 4, HALF], F32, name="res%d" % half, offset=4096 * (1 + 2 * half), align_bytes=64)
             nc.sync.dma_start(part[:], res_rows[:, :, HALF * half : HALF * (half + 1)])
             res_sb.append(part)
         out_rows = out.rearrange("(c p) m -> p c m", p=P)
@@ -149,7 +149,8 @@ def tile_list_kernl_poly2_mix_res_kernel(
             if half == 0 and b == 0:
                 order = [(a, t) for a in range(2) for t in range(PACK)]
             else:
-                order = [(a, t) for t in range(PACK) for a in range(2)]
+                order = [(a, t) for t in range(PACK) for a in (1, 0)]
+            first = order[0][0]
             for a, t in order:
                 col = 512 * b + P * t
                 for u in range(2):
@@ -160,10 +161,13 @@ def tile_list_kernl_poly2_mix_res_kernel(
                         lhsT_scale=tab_plane[a][:, col : col + P],
                         rhs=x_codes[half, a][:, cols].bitcast(E4M3),
                         rhs_scale=x_scale[half, a][:, cols],
-                        start=(a == 0 and u == 0),
-                        stop=(a == 1 and u == 1),
+                        start=(a == first and u == 0),
+                        stop=(a != first and u == 1),
                     )
-            squares = keep.tile([P, PACK, HALF], F32, name="squares%d_%d" % (half, b))
+            if half == 0 and b == 0:
+                squares = stage.tile([P, PACK, HALF], F32, name="squares0_0", offset=4096 * 2, align_bytes=64)
+            else:
+                squares = keep.tile([P, PACK, HALF], F32, name="squares%d_%d" % (half, b))
             for t in range(PACK):
                 nc.scalar.activation(squares[:, t, :], dots[t][:], ACT.Square, bias=cb_sb[:, b, t : t + 1])
             grouped = keep.tile([P, HALF, PACK], BF16, name="h_grouped%d_%d" % (half, b), tag="hg%d" % b, align_bytes=64)
@@ -208,8 +212,11 @@ def tile_list_kernl_poly2_mix_res_kernel(
                         )
                 tag = "hg1" if (half, pair) == (0, 1) else "result%d_%d" % (half, pair)
                 result = keep.tile([P, 2, HALF], F32, name="result%d_%d" % (half, pair), tag=tag, align_bytes=64)
-                nc.vector.tensor_tensor(result[:], sums[:], res_sb[half][:, 2 * pair : 2 * pair + 2, :], ALU.add)
-                nc.sync.dma_start(out_rows[:, 2 * pair : 2 * pair + 2, HALF * half : HALF * (half + 1)], result[:])
+                pieces = [(0, 1), (1, 2)] if (half, pair) == (1, 1) else [(0, 2)]
+                for lo, hi in pieces:
+                    rows = slice(2 * pair + lo, 2 * pair + hi)
+                    nc.vector.tensor_tensor(result[:, lo:hi, :], sums[:, lo:hi, :], res_sb[half][:, rows, :], ALU.add)
+                    nc.sync.dma_start(out_rows[:, rows, HALF * half : HALF * (half + 1)], result[:, lo:hi, :])
 
         kernel_values(0, 0)
         kernel_values(0, 1)

@@ -18,7 +18,12 @@ ALU = mybir.AluOpType
 
 P = 128
 PACK = 4
+PASS = P * PACK
 HALF = M // 2
+QUADS = 4
+LIST_COLS = PASS // 16
+SLOT = PACK * HALF * 4
+PAIR = 2
 
 
 def tile_list_kernl_poly2_mix_res_kernel(
@@ -34,9 +39,7 @@ def tile_list_kernl_poly2_mix_res_kernel(
         nc.sync.dma_start(offsets[:], offs)
 
         scale_rows = keep.tile([P, T], U8, name="scale_rows", align_bytes=64)
-        nc.sync.dma_start(
-            scale_rows[0:32, :].bitcast(I32), tab_scales.rearrange("a q t -> (a q) t").bitcast(I32)
-        )
+        nc.sync.dma_start(scale_rows[0:32, :].bitcast(I32), tab_scales.rearrange("a q t -> (a q) t").bitcast(I32))
         nc.vector.memset(scale_rows[64:128, :].bitcast(I32), 0)
         nc.vector.memset(scale_rows[32:64, :].bitcast(I32), 0)
 
@@ -48,7 +51,7 @@ def tile_list_kernl_poly2_mix_res_kernel(
 
         def load_x(half, a):
             raw = stage.tile(
-                [P, PACK, HALF], F32, name="x_raw%d_%d" % (half, a), offset=4096 * (2 * half + a), align_bytes=64
+                [P, PACK, HALF], F32, name="x_raw%d_%d" % (half, a), offset=SLOT * (2 * half + a), align_bytes=64
             )
             nc.sync.dma_start(raw[:], x_rows[a][:, :, HALF * half : HALF * (half + 1)])
             x_raw[half, a] = raw
@@ -64,153 +67,159 @@ def tile_list_kernl_poly2_mix_res_kernel(
         plane1 = keep.tile([P, J], U8, name="plane1", align_bytes=64)
         nc.gpsimd.memset(plane1[:].bitcast(I32), 0)
 
-        picked_scales = stage.tile([P, J], U8, name="picked_scales", offset=4096 * 3 - 512, align_bytes=64)
+        picked_scales = stage.tile([P, J], U8, name="picked_scales", offset=SLOT * 3 - J // 2, align_bytes=64)
         nc.vector.tensor_copy(picked_scales[:], scale_rows[:].indirect(offsets[:]))
         plane0 = keep.tile([P, J], U8, name="plane0", align_bytes=64)
         nc.vector.tensor_copy(
             plane0[:].rearrange("p (b t m) -> p b t m", b=2, t=PACK),
             picked_scales[:].rearrange("p (b m t) -> p b t m", b=2, t=PACK),
         )
-        for q in range(1, 4):
-            nc.sync.dma_start(plane0[32 * q : 32 * q + 4, :].bitcast(I32), plane0[4 * q : 4 * q + 4, :].bitcast(I32))
-        for q in range(4):
-            queue = nc.sync if q < 2 else nc.gpsimd
-            queue.dma_start(
-                plane1[32 * q : 32 * q + 4, :].bitcast(I32), plane0[16 + 4 * q : 20 + 4 * q, :].bitcast(I32)
-            )
-        tab_plane = (plane0, plane1)
+
+        def move_scale_rows(plane, a, quad):
+            row = 16 * a + 4 * quad
+            nc.sync.dma_start(plane[32 * quad : 32 * quad + 4, :].bitcast(I32), plane0[row : row + 4, :].bitcast(I32))
+
+        for quad in range(1, QUADS):
+            move_scale_rows(plane0, 0, quad)
+        for quad in range(QUADS // 2):
+            move_scale_rows(plane1, 1, quad)
         load_x(1, 0)
+        for quad in range(QUADS // 2, QUADS):
+            move_scale_rows(plane1, 1, quad)
         load_x(1, 1)
+        tab_plane = (plane0, plane1)
 
-        x_codes, x_scale = {}, {}
+        def as_words(grouped):
+            return grouped[:].rearrange("p (c i) t -> p c t i", i=PAIR)
 
-        def quantize_x(half, a, on_vector, tag):
-            grouped = keep.tile([P, HALF, PACK], BF16, name="x_grouped%d_%d" % (half, a), tag=tag, align_bytes=64)
-            dst = grouped[:].rearrange("p (c i) t -> p c t i", i=2)
-            src = x_raw[half, a][:].rearrange("p t (c i) -> p c t i", i=2)
-            if on_vector:
-                nc.vector.tensor_copy(dst, src)
-            else:
-                nc.scalar.activation(dst, src, ACT.Copy)
-            codes = keep.tile([P, HALF], U32, name="x_codes%d_%d" % (half, a), align_bytes=64)
-            scale = keep.tile([P, HALF], U8, name="x_scale%d_%d" % (half, a), align_bytes=64)
+        def as_rows(rows):
+            return rows[:].rearrange("p t (c i) -> p c t i", i=PAIR)
+
+        def quantize(grouped, name):
+            codes = keep.tile([P, HALF], U32, name=name + "_codes", align_bytes=64)
+            scale = keep.tile([P, HALF], U8, name=name + "_scale", align_bytes=64)
             nc.vector.quantize_mx(
                 out=codes[:].bitcast(E4M3), scales=scale[:], in_=grouped[:].rearrange("p m t -> p (m t)")
             )
-            x_codes[half, a] = codes
-            x_scale[half, a] = scale
+            return codes, scale
+
+        x_mx = {}
+
+        def quantize_x(half, a, on_vector, tag):
+            grouped = keep.tile([P, HALF, PACK], BF16, name="x_grouped%d_%d" % (half, a), tag=tag, align_bytes=64)
+            if on_vector:
+                nc.vector.tensor_copy(as_words(grouped), as_rows(x_raw[half, a]))
+            else:
+                nc.scalar.activation(as_words(grouped), as_rows(x_raw[half, a]), ACT.Copy)
+            x_mx[half, a] = quantize(grouped, "x%d_%d" % (half, a))
 
         def pick_centres(b, picked_tag, parted_tag):
-            picked = keep.tile([P, 512], U32, name="picked_words%d" % b, tag=picked_tag, align_bytes=64)
+            picked = keep.tile([P, PASS], U32, name="picked_words%d" % b, tag=picked_tag, align_bytes=64)
             nc.vector.tensor_copy(
                 picked[:].rearrange("p (t m) -> p m t", t=PACK),
-                table[:].bitcast(U32).indirect(offsets[:, 32 * b : 32 * (b + 1)]),
+                table[:].bitcast(U32).indirect(offsets[:, LIST_COLS * b : LIST_COLS * (b + 1)]),
             )
-            parted = keep.tile([P, 2, 1024], U8, name="centres%d" % b, tag=parted_tag, align_bytes=64)
-            nc.vector.tensor_copy(
-                parted[:].bitcast(U16),
-                picked[:].bitcast(U16).rearrange("p (c a) -> p a c", a=2),
-            )
+            parted = keep.tile([P, 2, 2 * PASS], U8, name="centres%d" % b, tag=parted_tag, align_bytes=64)
+            nc.vector.tensor_copy(parted[:].bitcast(U16), picked[:].bitcast(U16).rearrange("p (c a) -> p a c", a=2))
             return parted
 
-        centres = [pick_centres(0, "pw0", "c0")]
-        quantize_x(0, 0, False, "xg00")
-        quantize_x(0, 1, False, "xg01")
-        centres.append(pick_centres(1, "xg00", "xg01"))
-        quantize_x(1, 0, False, "xg10")
-        quantize_x(1, 1, True, "hg0")
+        centres = [pick_centres(0, "picked0", "centres0")]
+        quantize_x(0, 0, False, "x_grouped00")
+        quantize_x(0, 1, False, "x_grouped01")
+        centres.append(pick_centres(1, "x_grouped00", "x_grouped01"))
+        quantize_x(1, 0, False, "x_grouped10")
+        quantize_x(1, 1, True, "h_grouped0")
 
         al8 = stage.tile([P, N], I32, name="al8", offset=0, align_bytes=64)
         nc.sync.dma_start(al8[:], al8_words[0].rearrange("p n f -> p (n f)").bitcast(I32))
-        al4 = stage.tile([P, 2 * N], U8, name="al4", offset=2048, align_bytes=64)
+        al4 = stage.tile([P, 2 * N], U8, name="al4", offset=4 * N, align_bytes=64)
         nc.sync.dma_start(al4[:].bitcast(I32), al4_words[0].bitcast(I32))
-        al_planes = stage.tile([P, 2, N], U8, name="al_planes", offset=3072, align_bytes=64)
-        nc.gpsimd.memset(al_planes[:].rearrange("p a n -> p (a n)").bitcast(I32), 0)
-        for a, src in enumerate((al8_scales, al4_scales)):
-            for q in range(4):
+        al_planes = stage.tile([P, 2, N], U8, name="al_planes", offset=6 * N, align_bytes=64)
+        nc.gpsimd.memset(al_planes[:].rearrange("p b n -> p (b n)").bitcast(I32), 0)
+        for b, scales in enumerate((al8_scales, al4_scales)):
+            for quad in range(QUADS):
                 nc.sync.dma_start(
-                    al_planes[32 * q : 32 * q + 4, a, :].bitcast(I32), src[0, 4 * q : 4 * q + 4, :].bitcast(I32)
+                    al_planes[32 * quad : 32 * quad + 4, b, :].bitcast(I32),
+                    scales[0, 4 * quad : 4 * quad + 4, :].bitcast(I32),
                 )
         res_rows = res.rearrange("(c p) m -> p c m", p=P)
         res_sb = []
         for half in range(2):
-            part = stage.tile([P, 4, HALF], F32, name="res%d" % half, offset=4096 * (1 + 2 * half), align_bytes=64)
+            part = stage.tile([P, N // P, HALF], F32, name="res%d" % half, offset=SLOT * (1 + 2 * half), align_bytes=64)
             nc.sync.dma_start(part[:], res_rows[:, :, HALF * half : HALF * (half + 1)])
             res_sb.append(part)
         out_rows = out.rearrange("(c p) m -> p c m", p=P)
 
-        h_codes, h_scale = {}, {}
+        h_mx = {}
 
         def kernel_values(half, b):
+            is_first = (half, b) == (0, 0)
             dots = [
-                psum.tile([P, HALF], F32, name="dot%d_%d_%d" % (half, b, t), tag="bank%d" % (4 * b + t))
+                psum.tile([P, HALF], F32, name="dot%d_%d_%d" % (half, b, t), tag="bank%d" % (PACK * b + t))
                 for t in range(PACK)
             ]
-            if half == 0 and b == 0:
+            if is_first:
                 order = [(a, t) for a in range(2) for t in range(PACK)]
             else:
                 order = [(a, t) for t in range(PACK) for a in (1, 0)]
-            first = order[0][0]
+            opening = order[0][0]
             for a, t in order:
-                col = 512 * b + P * t
-                for u in range(2):
+                col = PASS * b + P * t
+                codes, scale = x_mx[half, a]
+                for u in range(HALF // P):
                     cols = slice(P * u, P * (u + 1))
                     nc.tensor.matmul_mx(
                         out=dots[t][:, cols],
                         lhsT=centres[b][:, a, 2 * P * t : 2 * P * (t + 1)].bitcast(E2M1),
                         lhsT_scale=tab_plane[a][:, col : col + P],
-                        rhs=x_codes[half, a][:, cols].bitcast(E4M3),
-                        rhs_scale=x_scale[half, a][:, cols],
-                        start=(a == first and u == 0),
-                        stop=(a != first and u == 1),
+                        rhs=codes[:, cols].bitcast(E4M3),
+                        rhs_scale=scale[:, cols],
+                        start=(a == opening and u == 0),
+                        stop=(a != opening and u == HALF // P - 1),
                     )
-            if half == 0 and b == 0:
-                squares = stage.tile([P, PACK, HALF], F32, name="squares0_0", offset=4096 * 2, align_bytes=64)
+            if is_first:
+                squares = stage.tile([P, PACK, HALF], F32, name="squares0_0", offset=SLOT * 2, align_bytes=64)
             else:
                 squares = keep.tile([P, PACK, HALF], F32, name="squares%d_%d" % (half, b))
             for t in range(PACK):
                 nc.scalar.activation(squares[:, t, :], dots[t][:], ACT.Square, bias=cb_sb[:, b, t : t + 1])
-            grouped = keep.tile([P, HALF, PACK], BF16, name="h_grouped%d_%d" % (half, b), tag="hg%d" % b, align_bytes=64)
+            grouped = keep.tile(
+                [P, HALF, PACK], BF16, name="h_grouped%d_%d" % (half, b), tag="h_grouped%d" % b, align_bytes=64
+            )
+            weights = cw_sb[:, b, :].rearrange("p (c t i) -> p c t i", c=1, i=1)
             nc.vector.tensor_tensor(
-                grouped[:].rearrange("p (c i) t -> p c t i", i=2),
-                squares[:].rearrange("p t (c i) -> p c t i", i=2),
-                cw_sb[:, b, :].rearrange("p (o t u) -> p o t u", o=1, u=1).to_broadcast([P, HALF // 2, PACK, 2]),
-                ALU.mult,
+                as_words(grouped), as_rows(squares), weights.to_broadcast([P, HALF // PAIR, PACK, PAIR]), ALU.mult
             )
-            codes = keep.tile([P, HALF], U32, name="h_codes%d_%d" % (half, b), align_bytes=64)
-            scale = keep.tile([P, HALF], U8, name="h_scale%d_%d" % (half, b), align_bytes=64)
-            nc.vector.quantize_mx(
-                out=codes[:].bitcast(E4M3), scales=scale[:], in_=grouped[:].rearrange("p m t -> p (m t)")
-            )
-            h_codes[half, b] = codes
-            h_scale[half, b] = scale
+            h_mx[half, b] = quantize(grouped, "h%d_%d" % (half, b))
 
         def outputs(half):
+            codes8, scale8 = h_mx[half, 0]
+            codes4, scale4 = h_mx[half, 1]
             for pair in range(2):
-                sums = psum.tile([P, 2, HALF], F32, name="sum%d_%d" % (half, pair), tag="bank%d" % (4 * half + pair))
+                sums = psum.tile([P, 2, HALF], F32, name="sum%d_%d" % (half, pair), tag="bank%d" % (PACK * half + pair))
                 for i in range(2):
                     c = 2 * pair + i
                     nc.tensor.matmul_mx(
                         out=sums[:, i, :],
                         lhsT=al8[:, P * c : P * (c + 1)].bitcast(E4M3),
                         lhsT_scale=al_planes[:, 0, P * c : P * (c + 1)],
-                        rhs=h_codes[half, 0][:].bitcast(E4M3),
-                        rhs_scale=h_scale[half, 0][:],
+                        rhs=codes8[:].bitcast(E4M3),
+                        rhs_scale=scale8[:],
                         start=True,
                         stop=False,
                     )
-                    for u in range(2):
+                    for u in range(HALF // P):
                         cols = slice(P * u, P * (u + 1))
                         nc.tensor.matmul_mx(
                             out=sums[:, i, cols],
                             lhsT=al4[:, 2 * P * c : 2 * P * (c + 1)].bitcast(E2M1),
                             lhsT_scale=al_planes[:, 1, P * c : P * (c + 1)],
-                            rhs=h_codes[half, 1][:, cols].bitcast(E4M3),
-                            rhs_scale=h_scale[half, 1][:, cols],
+                            rhs=codes4[:, cols].bitcast(E4M3),
+                            rhs_scale=scale4[:, cols],
                             start=False,
-                            stop=(u == 1),
+                            stop=(u == HALF // P - 1),
                         )
-                tag = "hg1" if (half, pair) == (0, 1) else "result%d_%d" % (half, pair)
+                tag = "h_grouped1" if (half, pair) == (0, 1) else "result%d_%d" % (half, pair)
                 result = keep.tile([P, 2, HALF], F32, name="result%d_%d" % (half, pair), tag=tag, align_bytes=64)
                 pieces = [(0, 1), (1, 2)] if (half, pair) == (1, 1) else [(0, 2)]
                 for lo, hi in pieces:
@@ -218,9 +227,8 @@ def tile_list_kernl_poly2_mix_res_kernel(
                     nc.vector.tensor_tensor(result[:, lo:hi, :], sums[:, lo:hi, :], res_sb[half][:, rows, :], ALU.add)
                     nc.sync.dma_start(out_rows[:, rows, HALF * half : HALF * (half + 1)], result[:, lo:hi, :])
 
-        kernel_values(0, 0)
-        kernel_values(0, 1)
-        kernel_values(1, 0)
-        kernel_values(1, 1)
-        outputs(0)
-        outputs(1)
+        for half in range(2):
+            for b in range(2):
+                kernel_values(half, b)
+        for half in range(2):
+            outputs(half)

@@ -24,6 +24,9 @@ QUADS = 4
 LIST_COLS = PASS // 16
 SLOT = PACK * HALF * 4
 PAIR = 2
+ROW = J + N
+TINY = 1e-36
+CHAIN = 6 * SLOT
 
 
 def tile_list_kernl_poly2_mix_res_kernel(
@@ -36,12 +39,20 @@ def tile_list_kernl_poly2_mix_res_kernel(
         psum = ctx.enter_context(tc.psum_pool(name="psum", bufs=1))
 
         offsets = keep.tile([P, J // 16], U16, name="offsets")
-        nc.sync.dma_start(offsets[:], offs)
 
         scale_rows = keep.tile([P, T], U8, name="scale_rows", align_bytes=64)
-        nc.sync.dma_start(scale_rows[0:32, :].bitcast(I32), tab_scales.rearrange("a q t -> (a q) t").bitcast(I32))
+        nc.sync.dma_start(scale_rows[0:32, :].bitcast(I32), tab_scales.rearrange("a q t -> q a t").bitcast(I32))
+        nc.sync.dma_start(offsets[:], offs)
         nc.vector.memset(scale_rows[64:128, :].bitcast(I32), 0)
         nc.vector.memset(scale_rows[32:64, :].bitcast(I32), 0)
+
+        staged = stage.tile([P, ROW], U8, name="staged", offset=2048 + 4 * SLOT, align_bytes=64)
+        for b, scales in enumerate((al8_scales, al4_scales)):
+            lo = J + b * (N // 2)
+            nc.scalar.dma_start(
+                staged[0:32, lo : lo + N // 2].bitcast(I32),
+                scales[0].rearrange("q (a n) -> (q a) n", a=2).bitcast(I32),
+            )
 
         table = keep.tile([P, T], I32, name="table", align_bytes=64)
         nc.sync.dma_start(table[:], tab_words[0].rearrange("p t f -> p (t f)").bitcast(I32))
@@ -59,176 +70,253 @@ def tile_list_kernl_poly2_mix_res_kernel(
         load_x(0, 0)
         load_x(0, 1)
 
-        cw_sb = keep.tile([P, 2, PACK], F32, name="cw_sb")
-        cb_sb = keep.tile([P, 2, PACK], F32, name="cb_sb")
-        nc.gpsimd.dma_start(cb_sb[:], cb.rearrange("(b p t) -> p b t", b=2, t=PACK))
-        nc.gpsimd.dma_start(cw_sb[:], cw.rearrange("(b p t) -> p b t", b=2, t=PACK))
+        cw_sb = keep.tile([P, 2 * PACK], F32, name="cw_sb")
+        cb_sb = keep.tile([P, 2 * PACK], F32, name="cb_sb")
+        nc.scalar.dma_start(cw_sb[:].rearrange("p (b t) -> p b t", b=2), cw.rearrange("(b p t) -> p b t", b=2, t=PACK))
+        nc.gpsimd.dma_start(cb_sb[:].rearrange("p (b t) -> p b t", b=2), cb.rearrange("(b p t) -> p b t", b=2, t=PACK))
 
-        plane1 = keep.tile([P, J], U8, name="plane1", align_bytes=64)
-        nc.gpsimd.memset(plane1[:].bitcast(I32), 0)
+        planes = keep.tile([P, 2, ROW], U8, name="planes", align_bytes=64)
+        nc.gpsimd.memset(planes[:].rearrange("p a n -> p (a n)").bitcast(I32), 0)
 
-        picked_scales = stage.tile([P, J], U8, name="picked_scales", offset=SLOT * 3 - J // 2, align_bytes=64)
+        def small(name, dtype=F32):
+            return keep.tile([P, 2 * PACK], dtype, name=name)
+
+        guess = small("guess")
+        nc.scalar.activation(guess[:], cw_sb[:], ACT.Abs_reciprocal_sqrt, bias=TINY)
+        size = small("size")
+        nc.scalar.activation(size[:], cw_sb[:], ACT.Abs)
+        sign = small("sign", BF16)
+        nc.scalar.activation(sign[:], cw_sb[:], ACT.Sign)
+        rough = small("rough")
+        nc.gpsimd.tensor_tensor(rough[:], size[:], guess[:], ALU.mult)
+        near_one = small("near_one")
+        nc.gpsimd.tensor_tensor(near_one[:], rough[:], guess[:], ALU.mult)
+        factor = small("factor")
+        nc.gpsimd.tensor_scalar(factor[:], near_one[:], -0.5, 1.5, ALU.mult, ALU.add)
+        root = small("root")
+        nc.gpsimd.tensor_tensor(root[:], rough[:], factor[:], ALU.mult)
+        shift = small("shift")
+        nc.gpsimd.tensor_tensor(shift[:], root[:], cb_sb[:], ALU.mult)
+
+        picked_scales = stage.tile([P, J], U8, name="picked_scales", offset=3 * SLOT - J // 2, align_bytes=64)
         nc.vector.tensor_copy(picked_scales[:], scale_rows[:].indirect(offsets[:]))
-        plane0 = keep.tile([P, J], U8, name="plane0", align_bytes=64)
         nc.vector.tensor_copy(
-            plane0[:].rearrange("p (b t m) -> p b t m", b=2, t=PACK),
+            staged[:, 0:J].rearrange("p (b t m) -> p b t m", b=2, t=PACK),
             picked_scales[:].rearrange("p (b m t) -> p b t m", b=2, t=PACK),
         )
-
-        def move_scale_rows(plane, a, quad):
-            row = 16 * a + 4 * quad
-            nc.sync.dma_start(plane[32 * quad : 32 * quad + 4, :].bitcast(I32), plane0[row : row + 4, :].bitcast(I32))
-
-        for quad in range(1, QUADS):
-            move_scale_rows(plane0, 0, quad)
-        for quad in range(QUADS // 2):
-            move_scale_rows(plane1, 1, quad)
+        for quad in range(QUADS):
+            nc.sync.dma_start(
+                planes[32 * quad : 32 * quad + 4].rearrange("p a n -> p (a n)").bitcast(I32),
+                staged[8 * quad : 8 * quad + 8, :].bitcast(I32),
+            )
         load_x(1, 0)
-        for quad in range(QUADS // 2, QUADS):
-            move_scale_rows(plane1, 1, quad)
         load_x(1, 1)
-        tab_plane = (plane0, plane1)
 
         def as_words(grouped):
-            return grouped[:].rearrange("p (c i) t -> p c t i", i=PAIR)
+            return grouped.rearrange("p (c i) t -> p c t i", i=PAIR)
 
         def as_rows(rows):
-            return rows[:].rearrange("p t (c i) -> p c t i", i=PAIR)
+            return rows.rearrange("p t (c i) -> p c t i", i=PAIR)
 
         def quantize(grouped, name):
-            codes = keep.tile([P, HALF], U32, name=name + "_codes", align_bytes=64)
-            scale = keep.tile([P, HALF], U8, name=name + "_scale", align_bytes=64)
+            width = grouped.shape[1]
+            if name == "none":
+                codes = stage.tile([P, width], U32, name=name + "_codes", offset=CHAIN + 2048, align_bytes=64)
+            else:
+                codes = keep.tile([P, width], U32, name=name + "_codes", align_bytes=64)
+            scale = keep.tile([P, width], U8, name=name + "_scale", align_bytes=64)
             nc.vector.quantize_mx(
                 out=codes[:].bitcast(E4M3), scales=scale[:], in_=grouped[:].rearrange("p m t -> p (m t)")
             )
             return codes, scale
 
         x_mx = {}
+        x_grouped = {}
 
-        def quantize_x(half, a, on_vector, tag):
-            grouped = keep.tile([P, HALF, PACK], BF16, name="x_grouped%d_%d" % (half, a), tag=tag, align_bytes=64)
-            if on_vector:
-                nc.vector.tensor_copy(as_words(grouped), as_rows(x_raw[half, a]))
+        def interleave_x(half, a, split):
+            if (half, a) == (1, 1):
+                grouped = stage.tile([P, HALF, PACK], BF16, name="x_grouped_last", offset=CHAIN + 1024, align_bytes=64)
             else:
-                nc.scalar.activation(as_words(grouped), as_rows(x_raw[half, a]), ACT.Copy)
-            x_mx[half, a] = quantize(grouped, "x%d_%d" % (half, a))
+                grouped = keep.tile([P, HALF, PACK], BF16, name="x_grouped%d_%d" % (half, a), tag="grouped%d" % (2 * half + a), align_bytes=64)
+            raw = x_raw[half, a]
+            if split > 0:
+                nc.scalar.activation(as_words(grouped[:, :split, :]), as_rows(raw[:, :, :split]), ACT.Copy)
+            if split < HALF:
+                nc.vector.tensor_copy(as_words(grouped[:, split:, :]), as_rows(raw[:, :, split:]))
+            x_grouped[half, a] = grouped
 
-        def pick_centres(b, picked_tag, parted_tag):
-            picked = keep.tile([P, PASS], U32, name="picked_words%d" % b, tag=picked_tag, align_bytes=64)
+        def quantize_x(half, a):
+            x_mx[half, a] = quantize(x_grouped[half, a], "x%d_%d" % (half, a))
+
+        def pick_words(b, picked):
             nc.vector.tensor_copy(
                 picked[:].rearrange("p (t m) -> p m t", t=PACK),
                 table[:].bitcast(U32).indirect(offsets[:, LIST_COLS * b : LIST_COLS * (b + 1)]),
             )
-            parted = keep.tile([P, 2, 2 * PASS], U8, name="centres%d" % b, tag=parted_tag, align_bytes=64)
+            return picked
+
+        def part_words(picked, parted):
             nc.vector.tensor_copy(parted[:].bitcast(U16), picked[:].bitcast(U16).rearrange("p (c a) -> p a c", a=2))
-            return parted
 
-        centres = [pick_centres(0, "picked0", "centres0")]
-        quantize_x(0, 0, False, "x_grouped00")
-        quantize_x(0, 1, False, "x_grouped01")
-        centres.append(pick_centres(1, "x_grouped00", "x_grouped01"))
-        quantize_x(1, 0, False, "x_grouped10")
-        quantize_x(1, 1, True, "h_grouped0")
+        picked = [keep.tile([P, PASS], U32, name="picked%d" % b, align_bytes=64) for b in range(2)]
+        for b in range(2):
+            pick_words(b, picked[b])
+        centres = [keep.tile([P, 2, 2 * PASS], U8, name="centres0", align_bytes=64)]
+        part_words(picked[0], centres[0])
+        interleave_x(0, 0, HALF)
+        interleave_x(0, 1, HALF)
+        quantize_x(0, 0)
+        quantize_x(0, 1)
+        centres.append(keep.tile([P, 2, 2 * PASS], U8, name="centres1", tag="grouped0", align_bytes=64))
+        part_words(picked[1], centres[1])
+        interleave_x(1, 0, 0)
+        interleave_x(1, 1, 0)
+        quantize_x(1, 0)
+        quantize_x(1, 1)
 
-        al8 = stage.tile([P, N], I32, name="al8", offset=0, align_bytes=64)
+        al8 = stage.tile([P, N], I32, name="al8", offset=2048 + 4 * SLOT + 2 * N, align_bytes=64)
         nc.sync.dma_start(al8[:], al8_words[0].rearrange("p n f -> p (n f)").bitcast(I32))
-        al4 = stage.tile([P, 2 * N], U8, name="al4", offset=4 * N, align_bytes=64)
+        al4 = stage.tile([P, 2 * N], U8, name="al4", offset=2048 + 4 * SLOT, align_bytes=64)
         nc.sync.dma_start(al4[:].bitcast(I32), al4_words[0].bitcast(I32))
-        al_planes = stage.tile([P, 2, N], U8, name="al_planes", offset=6 * N, align_bytes=64)
-        nc.gpsimd.memset(al_planes[:].rearrange("p b n -> p (b n)").bitcast(I32), 0)
-        for b, scales in enumerate((al8_scales, al4_scales)):
-            for quad in range(QUADS):
-                nc.sync.dma_start(
-                    al_planes[32 * quad : 32 * quad + 4, b, :].bitcast(I32),
-                    scales[0, 4 * quad : 4 * quad + 4, :].bitcast(I32),
-                )
         res_rows = res.rearrange("(c p) m -> p c m", p=P)
         res_sb = []
         for half in range(2):
-            part = stage.tile([P, N // P, HALF], F32, name="res%d" % half, offset=SLOT * (1 + 2 * half), align_bytes=64)
+            part = stage.tile([P, N // P, HALF], F32, name="res%d" % half, offset=(SLOT * 3 + 2048) * half, align_bytes=64)
             nc.sync.dma_start(part[:], res_rows[:, :, HALF * half : HALF * (half + 1)])
             res_sb.append(part)
         out_rows = out.rearrange("(c p) m -> p c m", p=P)
 
-        h_mx = {}
+        def product_pass(dst, b, t, a, codes, scale, start, stop):
+            col = PASS * b + P * t
+            nc.tensor.matmul_mx(
+                out=dst,
+                lhsT=centres[b][:, a, 2 * P * t : 2 * P * (t + 1)].bitcast(E2M1),
+                lhsT_scale=planes[:, a, col : col + P],
+                rhs=codes.bitcast(E4M3),
+                rhs_scale=scale,
+                start=start,
+                stop=stop,
+            )
 
-        def kernel_values(half, b):
-            is_first = (half, b) == (0, 0)
-            dots = [
-                psum.tile([P, HALF], F32, name="dot%d_%d_%d" % (half, b, t), tag="bank%d" % (PACK * b + t))
-                for t in range(PACK)
+        def first_product(half, b, width, first_bank):
+            banks = [
+                psum.tile([P, width, HALF], F32, name="dot%d_%d_%d" % (half, b, u), tag="bank%d" % (first_bank + u))
+                for u in range(PACK // width)
             ]
-            if is_first:
-                order = [(a, t) for a in range(2) for t in range(PACK)]
+            if (half, b) == (0, 0):
+                order = [(u, a) for a in range(2) for u in range(len(banks))]
             else:
-                order = [(a, t) for t in range(PACK) for a in (1, 0)]
-            opening = order[0][0]
-            for a, t in order:
-                col = PASS * b + P * t
+                order = [(u, a) for u in range(len(banks)) for a in (1, 0)]
+            opening = order[0][1]
+            for u, a in order:
                 codes, scale = x_mx[half, a]
-                for u in range(HALF // P):
-                    cols = slice(P * u, P * (u + 1))
-                    nc.tensor.matmul_mx(
-                        out=dots[t][:, cols],
-                        lhsT=centres[b][:, a, 2 * P * t : 2 * P * (t + 1)].bitcast(E2M1),
-                        lhsT_scale=tab_plane[a][:, col : col + P],
-                        rhs=codes[:, cols].bitcast(E4M3),
-                        rhs_scale=scale[:, cols],
-                        start=(a == opening and u == 0),
-                        stop=(a != opening and u == HALF // P - 1),
-                    )
-            if is_first:
-                squares = stage.tile([P, PACK, HALF], F32, name="squares0_0", offset=SLOT * 2, align_bytes=64)
-            else:
-                squares = keep.tile([P, PACK, HALF], F32, name="squares%d_%d" % (half, b))
-            for t in range(PACK):
-                nc.scalar.activation(squares[:, t, :], dots[t][:], ACT.Square, bias=cb_sb[:, b, t : t + 1])
-            grouped = keep.tile(
-                [P, HALF, PACK], BF16, name="h_grouped%d_%d" % (half, b), tag="h_grouped%d" % b, align_bytes=64
-            )
-            weights = cw_sb[:, b, :].rearrange("p (c t i) -> p c t i", c=1, i=1)
-            nc.vector.tensor_tensor(
-                as_words(grouped), as_rows(squares), weights.to_broadcast([P, HALF // PAIR, PACK, PAIR]), ALU.mult
-            )
-            h_mx[half, b] = quantize(grouped, "h%d_%d" % (half, b))
-
-        def outputs(half):
-            codes8, scale8 = h_mx[half, 0]
-            codes4, scale4 = h_mx[half, 1]
-            for pair in range(2):
-                sums = psum.tile([P, 2, HALF], F32, name="sum%d_%d" % (half, pair), tag="bank%d" % (PACK * half + pair))
-                for i in range(2):
-                    c = 2 * pair + i
-                    nc.tensor.matmul_mx(
-                        out=sums[:, i, :],
-                        lhsT=al8[:, P * c : P * (c + 1)].bitcast(E4M3),
-                        lhsT_scale=al_planes[:, 0, P * c : P * (c + 1)],
-                        rhs=codes8[:].bitcast(E4M3),
-                        rhs_scale=scale8[:],
-                        start=True,
-                        stop=False,
-                    )
-                    for u in range(HALF // P):
-                        cols = slice(P * u, P * (u + 1))
-                        nc.tensor.matmul_mx(
-                            out=sums[:, i, cols],
-                            lhsT=al4[:, 2 * P * c : 2 * P * (c + 1)].bitcast(E2M1),
-                            lhsT_scale=al_planes[:, 1, P * c : P * (c + 1)],
-                            rhs=codes4[:, cols].bitcast(E4M3),
-                            rhs_scale=scale4[:, cols],
-                            start=False,
-                            stop=(u == HALF // P - 1),
+                for i in range(width):
+                    for g in range(HALF // P):
+                        cols = slice(P * g, P * (g + 1))
+                        product_pass(
+                            banks[u][:, i, cols], b, width * u + i, a, codes[:, cols], scale[:, cols],
+                            a == opening and i == 0 and g == 0, a != opening and i == width - 1 and g == HALF // P - 1,
                         )
-                tag = "h_grouped1" if (half, pair) == (0, 1) else "result%d_%d" % (half, pair)
-                result = keep.tile([P, 2, HALF], F32, name="result%d_%d" % (half, pair), tag=tag, align_bytes=64)
-                pieces = [(0, 1), (1, 2)] if (half, pair) == (1, 1) else [(0, 2)]
-                for lo, hi in pieces:
-                    rows = slice(2 * pair + lo, 2 * pair + hi)
-                    nc.vector.tensor_tensor(result[:, lo:hi, :], sums[:, lo:hi, :], res_sb[half][:, rows, :], ALU.add)
-                    nc.sync.dma_start(out_rows[:, rows, HALF * half : HALF * (half + 1)], result[:, lo:hi, :])
+            return [banks[t // width][:, t % width, :] for t in range(PACK)]
 
-        for half in range(2):
-            for b in range(2):
-                kernel_values(half, b)
-        for half in range(2):
-            outputs(half)
+        def first_product_quarter(half, b, g, bank_no):
+            bank = psum.tile([P, PACK, P], F32, name="dotq%d" % g, tag="bank%d" % bank_no)
+            cols = slice(P * g, P * (g + 1))
+            for a in (1, 0):
+                codes, scale = x_mx[half, a]
+                for t in range(PACK):
+                    product_pass(
+                        bank[:, t, :], b, t, a, codes[:, cols], scale[:, cols], a == 1 and t == 0, a == 0 and t == PACK - 1
+                    )
+            return [bank[:, t, :] for t in range(PACK)]
+
+        def place(shape, dtype, name, offset, tag=None):
+            if offset is None:
+                return keep.tile(shape, dtype, name=name, tag=tag or name, align_bytes=64)
+            return stage.tile(shape, dtype, name=name, offset=offset, align_bytes=64)
+
+        def weighted_on_vector(dots, b, name, sq_offset=None, tag=None, offset=None):
+            width = dots[0].shape[1]
+            squares = place([P, PACK, width], F32, "squares" + name, sq_offset)
+            for t in range(PACK):
+                col = PACK * b + t
+                nc.scalar.activation(squares[:, t, :], dots[t], ACT.Square, bias=cb_sb[:, col : col + 1])
+            grouped = place([P, width, PACK], BF16, "h_grouped" + name, offset, tag)
+            weights = cw_sb[:, PACK * b : PACK * (b + 1)].rearrange("p (c t i) -> p c t i", c=1, i=1)
+            nc.vector.tensor_tensor(
+                as_words(grouped[:]), as_rows(squares[:]), weights.to_broadcast([P, width // PAIR, PACK, PAIR]), ALU.mult
+            )
+            return quantize(grouped, "h" + name)
+
+        def weighted_on_scalar(dots, b, name, sq_offset=None, tag=None, offset=None):
+            width = dots[0].shape[1]
+            pairs = place([P, 2, width, 2], BF16, "pairs" + name, sq_offset)
+            for t in range(PACK):
+                col = PACK * b + t
+                nc.scalar.activation(
+                    pairs[:, t // 2, :, t % 2],
+                    dots[t],
+                    ACT.Square,
+                    bias=shift[:, col : col + 1],
+                    scale=root[:, col : col + 1],
+                )
+            grouped = place([P, width, PACK], BF16, "h_grouped" + name, offset, tag)
+            signs = sign[:, PACK * b : PACK * (b + 1)].rearrange("p (m u e) -> p m u e", m=1, u=2)
+            nc.vector.tensor_tensor(
+                grouped[:].rearrange("p m (u e) -> p m u e", u=2),
+                pairs[:].rearrange("p u m e -> p m u e"),
+                signs.to_broadcast([P, width, 2, 2]),
+                ALU.mult,
+            )
+            return quantize(grouped, "h" + name)
+
+        def second_pass(dst, b, c, codes, scale, start, stop):
+            lo = J + b * (N // 2) + P * (c % 2)
+            if b == 0:
+                weights = al8[:, P * c : P * (c + 1)].bitcast(E4M3)
+            else:
+                weights = al4[:, 2 * P * c : 2 * P * (c + 1)].bitcast(E2M1)
+            nc.tensor.matmul_mx(
+                out=dst,
+                lhsT=weights,
+                lhsT_scale=planes[:, c // 2, lo : lo + P],
+                rhs=codes.bitcast(E4M3),
+                rhs_scale=scale,
+                start=start,
+                stop=stop,
+            )
+
+        def finish(sums, name, rows, half, lo, width):
+            count = rows.stop - rows.start
+            result = keep.tile([P, count, width], F32, name="result" + name, align_bytes=64)
+            nc.vector.tensor_tensor(result[:], sums, res_sb[half][:, rows, lo : lo + width], ALU.add)
+            nc.sync.dma_start(out_rows[:, rows, HALF * half + lo : HALF * half + lo + width], result[:])
+
+        dots00 = first_product(0, 0, 1, 0)
+        h00 = weighted_on_vector(dots00, 0, "00", offset=CHAIN)
+        dots01 = first_product(0, 1, 2, 4)
+        dots10 = first_product(1, 0, 2, 0)
+        h01 = weighted_on_scalar(dots01, 1, "01", offset=CHAIN + 2048)
+        dots11 = [first_product_quarter(1, 1, g, 4 + g) for g in range(2)]
+        sums0 = [psum.tile([P, 2, HALF], F32, name="sum0_%d" % pair, tag="bank%d" % (6 + pair)) for pair in range(2)]
+        for c in range(4):
+            second_pass(sums0[c // 2][:, c % 2, :], 0, c, h00[0][:], h00[1][:], c % 2 == 0, False)
+        for c in range(4):
+            for g in range(2):
+                cols = slice(P * g, P * (g + 1))
+                second_pass(sums0[c // 2][:, c % 2, cols], 1, c, h01[0][:, cols], h01[1][:, cols], False, c % 2 == 1 and g == 1)
+        h10 = weighted_on_scalar(dots10, 0, "10")
+        sums1 = [psum.tile([P, 4, P], F32, name="sum1_%d" % g, tag="bank%d" % (2 + g)) for g in range(2)]
+        for g in range(2):
+            cols = slice(P * g, P * (g + 1))
+            for c in range(4):
+                second_pass(sums1[g][:, c, :], 0, c, h10[0][:, cols], h10[1][:, cols], c == 0, False)
+        for pair in range(2):
+            finish(sums0[pair][:], "0_%d" % pair, slice(2 * pair, 2 * pair + 2), 0, 0, HALF)
+        for g in range(2):
+            h11 = weighted_on_scalar(dots11[g], 1, "11_%d" % g, offset=None)
+            for c in range(4):
+                second_pass(sums1[g][:, c, :], 1, c, h11[0][:], h11[1][:], False, c == 3)
+        finish(sums1[0][:], "1_0", slice(0, 4), 1, 0, P)
+        for pair in range(2):
+            finish(sums1[1][:, 2 * pair : 2 * pair + 2, :], "1_1_%d" % pair, slice(2 * pair, 2 * pair + 2), 1, P, P)

@@ -169,7 +169,7 @@ def tile_list_kernl_poly2_mix_res_kernel(
         quantize_x(0, 1)
         centres.append(keep.tile([P, 2, 2 * PASS], U8, name="centres1", tag="grouped0", align_bytes=64))
         part_words(picked[1], centres[1])
-        interleave_x(1, 0, 0)
+        interleave_x(1, 0, HALF)
         interleave_x(1, 1, 0)
         quantize_x(1, 0)
         quantize_x(1, 1)
@@ -293,10 +293,10 @@ def tile_list_kernl_poly2_mix_res_kernel(
             nc.sync.dma_start(out_rows[:, rows, HALF * half + lo : HALF * half + lo + width], result[:])
 
         dots00 = first_product(0, 0, 1, 0)
-        h00 = weighted_on_vector(dots00, 0, "00", offset=CHAIN)
+        h00 = weighted_on_vector(dots00, 0, "00", sq_offset=2 * SLOT - 2048, offset=CHAIN)
         dots01 = first_product(0, 1, 2, 4)
         dots10 = first_product(1, 0, 2, 0)
-        h01 = weighted_on_scalar(dots01, 1, "01", offset=CHAIN + 2048)
+        h01 = weighted_on_vector(dots01, 1, "01", sq_offset=2 * SLOT + 2048, offset=CHAIN + 2048)
         dots11 = [first_product_quarter(1, 1, g, 4 + g) for g in range(2)]
         sums0 = [psum.tile([P, 2, HALF], F32, name="sum0_%d" % pair, tag="bank%d" % (6 + pair)) for pair in range(2)]
         for c in range(4):

@@ -150,13 +150,16 @@ def tile_list_kernl_poly2_mix_res_kernel(
 
         def pick_words(b, picked):
             nc.vector.tensor_copy(
-                picked[:].rearrange("p (t m) -> p m t", t=PACK),
+                picked[:],
                 table[:].bitcast(U32).indirect(offsets[:, LIST_COLS * b : LIST_COLS * (b + 1)]),
             )
             return picked
 
         def part_words(picked, parted):
-            nc.vector.tensor_copy(parted[:].bitcast(U16), picked[:].bitcast(U16).rearrange("p (c a) -> p a c", a=2))
+            nc.vector.tensor_copy(
+                parted[:].bitcast(U16).rearrange("p a (t c i) -> p a c t i", t=PACK, i=4),
+                picked[:].bitcast(U16).rearrange("p (c i t a) -> p a c t i", i=4, t=PACK, a=2),
+            )
 
         picked = [keep.tile([P, PASS], U32, name="picked%d" % b, align_bytes=64) for b in range(2)]
         for b in range(2):

@@ -22,10 +22,14 @@ PASS = P * PACK
 HALF = M // 2
 QUADS = 4
 LIST_COLS = PASS // 16
-SLOT = PACK * HALF * 4
 PAIR = 2
+RUN = 4
 ROW = J + N
 TINY = 1e-36
+
+SLOT = PACK * HALF * 4
+GROUP = PACK * HALF * 2
+WEIGHTS = 4 * SLOT + GROUP
 CHAIN = 6 * SLOT
 
 
@@ -46,7 +50,10 @@ def tile_list_kernl_poly2_mix_res_kernel(
         nc.vector.memset(scale_rows[64:128, :].bitcast(I32), 0)
         nc.vector.memset(scale_rows[32:64, :].bitcast(I32), 0)
 
-        staged = stage.tile([P, ROW], U8, name="staged", offset=2048 + 4 * SLOT, align_bytes=64)
+        cw_sb = keep.tile([P, 2 * PACK], F32, name="cw_sb")
+        nc.scalar.dma_start(cw_sb[:].rearrange("p (b t) -> p b t", b=2), cw.rearrange("(b p t) -> p b t", b=2, t=PACK))
+
+        staged = stage.tile([P, ROW], U8, name="staged", offset=WEIGHTS, align_bytes=64)
         for b, scales in enumerate((al8_scales, al4_scales)):
             lo = J + b * (N // 2)
             nc.scalar.dma_start(
@@ -70,13 +77,11 @@ def tile_list_kernl_poly2_mix_res_kernel(
         load_x(0, 0)
         load_x(0, 1)
 
-        cw_sb = keep.tile([P, 2 * PACK], F32, name="cw_sb")
         cb_sb = keep.tile([P, 2 * PACK], F32, name="cb_sb")
-        nc.scalar.dma_start(cw_sb[:].rearrange("p (b t) -> p b t", b=2), cw.rearrange("(b p t) -> p b t", b=2, t=PACK))
         nc.gpsimd.dma_start(cb_sb[:].rearrange("p (b t) -> p b t", b=2), cb.rearrange("(b p t) -> p b t", b=2, t=PACK))
 
-        planes = keep.tile([P, 2, ROW], U8, name="planes", align_bytes=64)
-        nc.gpsimd.memset(planes[:].rearrange("p a n -> p (a n)").bitcast(I32), 0)
+        placed = keep.tile([P, 2, ROW], U8, name="placed", align_bytes=64)
+        nc.gpsimd.memset(placed[:].rearrange("p a n -> p (a n)").bitcast(I32), 0)
 
         def small(name, dtype=F32):
             return keep.tile([P, 2 * PACK], dtype, name=name)
@@ -106,102 +111,84 @@ def tile_list_kernl_poly2_mix_res_kernel(
         )
         for quad in range(QUADS):
             nc.sync.dma_start(
-                planes[32 * quad : 32 * quad + 4].rearrange("p a n -> p (a n)").bitcast(I32),
+                placed[32 * quad : 32 * quad + 4].rearrange("p a n -> p (a n)").bitcast(I32),
                 staged[8 * quad : 8 * quad + 8, :].bitcast(I32),
             )
         load_x(1, 0)
         load_x(1, 1)
 
         def as_words(grouped):
-            return grouped.rearrange("p (c i) t -> p c t i", i=PAIR)
+            return grouped[:].rearrange("p (c i) t -> p c t i", i=PAIR)
 
         def as_rows(rows):
-            return rows.rearrange("p t (c i) -> p c t i", i=PAIR)
+            return rows[:].rearrange("p t (c i) -> p c t i", i=PAIR)
 
         def quantize(grouped, name):
             width = grouped.shape[1]
-            if name == "none":
-                codes = stage.tile([P, width], U32, name=name + "_codes", offset=CHAIN + 2048, align_bytes=64)
-            else:
-                codes = keep.tile([P, width], U32, name=name + "_codes", align_bytes=64)
+            codes = keep.tile([P, width], U32, name=name + "_codes", align_bytes=64)
             scale = keep.tile([P, width], U8, name=name + "_scale", align_bytes=64)
             nc.vector.quantize_mx(
                 out=codes[:].bitcast(E4M3), scales=scale[:], in_=grouped[:].rearrange("p m t -> p (m t)")
             )
             return codes, scale
 
-        x_mx = {}
-        x_grouped = {}
+        def interleave_on_scalar(half, a):
+            name = "x_grouped%d_%d" % (half, a)
+            grouped = keep.tile([P, HALF, PACK], BF16, name=name, tag=name, align_bytes=64)
+            nc.scalar.activation(as_words(grouped), as_rows(x_raw[half, a]), ACT.Copy)
+            return grouped
 
-        def interleave_x(half, a, split):
-            if (half, a) == (1, 1):
-                grouped = stage.tile([P, HALF, PACK], BF16, name="x_grouped_last", offset=CHAIN + 1024, align_bytes=64)
-            else:
-                grouped = keep.tile([P, HALF, PACK], BF16, name="x_grouped%d_%d" % (half, a), tag="grouped%d" % (2 * half + a), align_bytes=64)
-            raw = x_raw[half, a]
-            if split > 0:
-                nc.scalar.activation(as_words(grouped[:, :split, :]), as_rows(raw[:, :, :split]), ACT.Copy)
-            if split < HALF:
-                nc.vector.tensor_copy(as_words(grouped[:, split:, :]), as_rows(raw[:, :, split:]))
-            x_grouped[half, a] = grouped
-
-        def quantize_x(half, a):
-            x_mx[half, a] = quantize(x_grouped[half, a], "x%d_%d" % (half, a))
-
-        def pick_words(b, picked):
+        def part_words(words, parted):
             nc.vector.tensor_copy(
-                picked[:],
-                table[:].bitcast(U32).indirect(offsets[:, LIST_COLS * b : LIST_COLS * (b + 1)]),
-            )
-            return picked
-
-        def part_words(picked, parted):
-            nc.vector.tensor_copy(
-                parted[:].bitcast(U16).rearrange("p a (t c i) -> p a c t i", t=PACK, i=4),
-                picked[:].bitcast(U16).rearrange("p (c i t a) -> p a c t i", i=4, t=PACK, a=2),
+                parted[:].bitcast(U16).rearrange("p a (t c i) -> p a c t i", t=PACK, i=RUN),
+                words[:].bitcast(U16).rearrange("p (c i t a) -> p a c t i", i=RUN, t=PACK, a=2),
             )
 
         picked = [keep.tile([P, PASS], U32, name="picked%d" % b, align_bytes=64) for b in range(2)]
         for b in range(2):
-            pick_words(b, picked[b])
+            nc.vector.tensor_copy(
+                picked[b][:], table[:].bitcast(U32).indirect(offsets[:, LIST_COLS * b : LIST_COLS * (b + 1)])
+            )
+
+        x_mx = {}
         centres = [keep.tile([P, 2, 2 * PASS], U8, name="centres0", align_bytes=64)]
         part_words(picked[0], centres[0])
-        interleave_x(0, 0, HALF)
-        interleave_x(0, 1, HALF)
-        quantize_x(0, 0)
-        quantize_x(0, 1)
-        centres.append(keep.tile([P, 2, 2 * PASS], U8, name="centres1", tag="grouped0", align_bytes=64))
+        first_half = [interleave_on_scalar(0, a) for a in range(2)]
+        for a in range(2):
+            x_mx[0, a] = quantize(first_half[a], "x0_%d" % a)
+        centres.append(keep.tile([P, 2, 2 * PASS], U8, name="centres1", tag="x_grouped0_0", align_bytes=64))
         part_words(picked[1], centres[1])
-        interleave_x(1, 0, HALF)
-        interleave_x(1, 1, 0)
-        quantize_x(1, 0)
-        quantize_x(1, 1)
+        third = interleave_on_scalar(1, 0)
+        last = stage.tile([P, HALF, PACK], BF16, name="x_grouped1_1", offset=CHAIN + GROUP // 2, align_bytes=64)
+        nc.vector.tensor_copy(as_words(last), as_rows(x_raw[1, 1]))
+        x_mx[1, 0] = quantize(third, "x1_0")
+        x_mx[1, 1] = quantize(last, "x1_1")
 
-        al8 = stage.tile([P, N], I32, name="al8", offset=2048 + 4 * SLOT + 2 * N, align_bytes=64)
+        al8 = stage.tile([P, N], I32, name="al8", offset=WEIGHTS + 2 * N, align_bytes=64)
         nc.sync.dma_start(al8[:], al8_words[0].rearrange("p n f -> p (n f)").bitcast(I32))
-        al4 = stage.tile([P, 2 * N], U8, name="al4", offset=2048 + 4 * SLOT, align_bytes=64)
+        al4 = stage.tile([P, 2 * N], U8, name="al4", offset=WEIGHTS, align_bytes=64)
         nc.sync.dma_start(al4[:].bitcast(I32), al4_words[0].bitcast(I32))
         res_rows = res.rearrange("(c p) m -> p c m", p=P)
         res_sb = []
-        for half in range(2):
-            part = stage.tile([P, N // P, HALF], F32, name="res%d" % half, offset=(SLOT * 3 + 2048) * half, align_bytes=64)
-            nc.sync.dma_start(part[:], res_rows[:, :, HALF * half : HALF * (half + 1)])
-            res_sb.append(part)
+        for half, offset in enumerate((0, WEIGHTS - SLOT)):
+            rows = stage.tile([P, N // P, HALF], F32, name="res%d" % half, offset=offset, align_bytes=64)
+            nc.sync.dma_start(rows[:], res_rows[:, :, HALF * half : HALF * (half + 1)])
+            res_sb.append(rows)
         out_rows = out.rearrange("(c p) m -> p c m", p=P)
 
-        def product_pass(dst, b, t, a, codes, scale, start, stop):
+        def dot_pass(dst, b, t, a, codes, scale, start, stop):
             col = PASS * b + P * t
             nc.tensor.matmul_mx(
                 out=dst,
                 lhsT=centres[b][:, a, 2 * P * t : 2 * P * (t + 1)].bitcast(E2M1),
-                lhsT_scale=planes[:, a, col : col + P],
+                lhsT_scale=placed[:, a, col : col + P],
                 rhs=codes.bitcast(E4M3),
                 rhs_scale=scale,
                 start=start,
                 stop=stop,
             )
 
-        def first_product(half, b, width, first_bank):
+        def dots_of_part(half, b, width, first_bank):
             banks = [
                 psum.tile([P, width, HALF], F32, name="dot%d_%d_%d" % (half, b, u), tag="bank%d" % (first_bank + u))
                 for u in range(PACK // width)
@@ -216,44 +203,40 @@ def tile_list_kernl_poly2_mix_res_kernel(
                 for i in range(width):
                     for g in range(HALF // P):
                         cols = slice(P * g, P * (g + 1))
-                        product_pass(
-                            banks[u][:, i, cols], b, width * u + i, a, codes[:, cols], scale[:, cols],
-                            a == opening and i == 0 and g == 0, a != opening and i == width - 1 and g == HALF // P - 1,
-                        )
+                        start = a == opening and i == 0 and g == 0
+                        stop = a != opening and i == width - 1 and g == HALF // P - 1
+                        dot_pass(banks[u][:, i, cols], b, width * u + i, a, codes[:, cols], scale[:, cols], start, stop)
             return [banks[t // width][:, t % width, :] for t in range(PACK)]
 
-        def first_product_quarter(half, b, g, bank_no):
+        def dots_of_quarter(g, bank_no):
             bank = psum.tile([P, PACK, P], F32, name="dotq%d" % g, tag="bank%d" % bank_no)
             cols = slice(P * g, P * (g + 1))
             for a in (1, 0):
-                codes, scale = x_mx[half, a]
+                codes, scale = x_mx[1, a]
                 for t in range(PACK):
-                    product_pass(
-                        bank[:, t, :], b, t, a, codes[:, cols], scale[:, cols], a == 1 and t == 0, a == 0 and t == PACK - 1
-                    )
+                    start, stop = a == 1 and t == 0, a == 0 and t == PACK - 1
+                    dot_pass(bank[:, t, :], 1, t, a, codes[:, cols], scale[:, cols], start, stop)
             return [bank[:, t, :] for t in range(PACK)]
 
-        def place(shape, dtype, name, offset, tag=None):
-            if offset is None:
-                return keep.tile(shape, dtype, name=name, tag=tag or name, align_bytes=64)
-            return stage.tile(shape, dtype, name=name, offset=offset, align_bytes=64)
-
-        def weighted_on_vector(dots, b, name, sq_offset=None, tag=None, offset=None):
-            width = dots[0].shape[1]
-            squares = place([P, PACK, width], F32, "squares" + name, sq_offset)
+        def weighted_on_vector(dots, b):
+            squares = stage.tile(
+                [P, PACK, HALF], F32, name="squares%d" % b, offset=SLOT * (2 + b) - SLOT // 2, align_bytes=64
+            )
             for t in range(PACK):
                 col = PACK * b + t
                 nc.scalar.activation(squares[:, t, :], dots[t], ACT.Square, bias=cb_sb[:, col : col + 1])
-            grouped = place([P, width, PACK], BF16, "h_grouped" + name, offset, tag)
+            grouped = stage.tile(
+                [P, HALF, PACK], BF16, name="h_grouped0%d" % b, offset=CHAIN + GROUP * b, align_bytes=64
+            )
             weights = cw_sb[:, PACK * b : PACK * (b + 1)].rearrange("p (c t i) -> p c t i", c=1, i=1)
             nc.vector.tensor_tensor(
-                as_words(grouped[:]), as_rows(squares[:]), weights.to_broadcast([P, width // PAIR, PACK, PAIR]), ALU.mult
+                as_words(grouped), as_rows(squares), weights.to_broadcast([P, HALF // PAIR, PACK, PAIR]), ALU.mult
             )
-            return quantize(grouped, "h" + name)
+            return quantize(grouped, "h0%d" % b)
 
-        def weighted_on_scalar(dots, b, name, sq_offset=None, tag=None, offset=None):
+        def weighted_on_scalar(dots, b, name):
             width = dots[0].shape[1]
-            pairs = place([P, 2, width, 2], BF16, "pairs" + name, sq_offset)
+            pairs = keep.tile([P, 2, width, 2], BF16, name="pairs" + name, align_bytes=64)
             for t in range(PACK):
                 col = PACK * b + t
                 nc.scalar.activation(
@@ -263,7 +246,7 @@ def tile_list_kernl_poly2_mix_res_kernel(
                     bias=shift[:, col : col + 1],
                     scale=root[:, col : col + 1],
                 )
-            grouped = place([P, width, PACK], BF16, "h_grouped" + name, offset, tag)
+            grouped = keep.tile([P, width, PACK], BF16, name="h_grouped" + name, align_bytes=64)
             signs = sign[:, PACK * b : PACK * (b + 1)].rearrange("p (m u e) -> p m u e", m=1, u=2)
             nc.vector.tensor_tensor(
                 grouped[:].rearrange("p m (u e) -> p m u e", u=2),
@@ -273,7 +256,7 @@ def tile_list_kernl_poly2_mix_res_kernel(
             )
             return quantize(grouped, "h" + name)
 
-        def second_pass(dst, b, c, codes, scale, start, stop):
+        def sum_pass(dst, b, c, codes, scale, start, stop):
             lo = J + b * (N // 2) + P * (c % 2)
             if b == 0:
                 weights = al8[:, P * c : P * (c + 1)].bitcast(E4M3)
@@ -282,7 +265,7 @@ def tile_list_kernl_poly2_mix_res_kernel(
             nc.tensor.matmul_mx(
                 out=dst,
                 lhsT=weights,
-                lhsT_scale=planes[:, c // 2, lo : lo + P],
+                lhsT_scale=placed[:, c // 2, lo : lo + P],
                 rhs=codes.bitcast(E4M3),
                 rhs_scale=scale,
                 start=start,
@@ -290,36 +273,40 @@ def tile_list_kernl_poly2_mix_res_kernel(
             )
 
         def finish(sums, name, rows, half, lo, width):
-            count = rows.stop - rows.start
-            result = keep.tile([P, count, width], F32, name="result" + name, align_bytes=64)
+            result = keep.tile([P, rows.stop - rows.start, width], F32, name="result" + name, align_bytes=64)
             nc.vector.tensor_tensor(result[:], sums, res_sb[half][:, rows, lo : lo + width], ALU.add)
             nc.sync.dma_start(out_rows[:, rows, HALF * half + lo : HALF * half + lo + width], result[:])
 
-        dots00 = first_product(0, 0, 1, 0)
-        h00 = weighted_on_vector(dots00, 0, "00", sq_offset=2 * SLOT - 2048, offset=CHAIN)
-        dots01 = first_product(0, 1, 2, 4)
-        dots10 = first_product(1, 0, 2, 0)
-        h01 = weighted_on_vector(dots01, 1, "01", sq_offset=2 * SLOT + 2048, offset=CHAIN + 2048)
-        dots11 = [first_product_quarter(1, 1, g, 4 + g) for g in range(2)]
+        tiles = N // P
+        dots00 = dots_of_part(0, 0, 1, 0)
+        codes00, scale00 = weighted_on_vector(dots00, 0)
+        dots01 = dots_of_part(0, 1, 2, 4)
+        dots10 = dots_of_part(1, 0, 2, 0)
+        codes01, scale01 = weighted_on_vector(dots01, 1)
+        dots11 = [dots_of_quarter(g, 4 + g) for g in range(2)]
+
         sums0 = [psum.tile([P, 2, HALF], F32, name="sum0_%d" % pair, tag="bank%d" % (6 + pair)) for pair in range(2)]
-        for c in range(4):
-            second_pass(sums0[c // 2][:, c % 2, :], 0, c, h00[0][:], h00[1][:], c % 2 == 0, False)
-        for c in range(4):
+        for c in range(tiles):
+            sum_pass(sums0[c // 2][:, c % 2, :], 0, c, codes00[:], scale00[:], c % 2 == 0, False)
+        for c in range(tiles):
             for g in range(2):
                 cols = slice(P * g, P * (g + 1))
-                second_pass(sums0[c // 2][:, c % 2, cols], 1, c, h01[0][:, cols], h01[1][:, cols], False, c % 2 == 1 and g == 1)
-        h10 = weighted_on_scalar(dots10, 0, "10")
-        sums1 = [psum.tile([P, 4, P], F32, name="sum1_%d" % g, tag="bank%d" % (2 + g)) for g in range(2)]
+                stop = c % 2 == 1 and g == 1
+                sum_pass(sums0[c // 2][:, c % 2, cols], 1, c, codes01[:, cols], scale01[:, cols], False, stop)
+
+        codes10, scale10 = weighted_on_scalar(dots10, 0, "10")
+        sums1 = [psum.tile([P, tiles, P], F32, name="sum1_%d" % g, tag="bank%d" % (2 + g)) for g in range(2)]
         for g in range(2):
             cols = slice(P * g, P * (g + 1))
-            for c in range(4):
-                second_pass(sums1[g][:, c, :], 0, c, h10[0][:, cols], h10[1][:, cols], c == 0, False)
+            for c in range(tiles):
+                sum_pass(sums1[g][:, c, :], 0, c, codes10[:, cols], scale10[:, cols], c == 0, False)
         for pair in range(2):
             finish(sums0[pair][:], "0_%d" % pair, slice(2 * pair, 2 * pair + 2), 0, 0, HALF)
         for g in range(2):
-            h11 = weighted_on_scalar(dots11[g], 1, "11_%d" % g, offset=None)
-            for c in range(4):
-                second_pass(sums1[g][:, c, :], 1, c, h11[0][:], h11[1][:], False, c == 3)
-        finish(sums1[0][:], "1_0", slice(0, 4), 1, 0, P)
+            codes11, scale11 = weighted_on_scalar(dots11[g], 1, "11_%d" % g)
+            for c in range(tiles):
+                sum_pass(sums1[g][:, c, :], 1, c, codes11[:], scale11[:], False, c == tiles - 1)
+        finish(sums1[0][:], "1_0", slice(0, tiles), 1, 0, P)
         for pair in range(2):
-            finish(sums1[1][:, 2 * pair : 2 * pair + 2, :], "1_1_%d" % pair, slice(2 * pair, 2 * pair + 2), 1, P, P)
+            rows = slice(2 * pair, 2 * pair + 2)
+            finish(sums1[1][:, rows, :], "1_1_%d" % pair, rows, 1, P, P)

@@ -24,12 +24,12 @@ QUADS = 4
 LIST_COLS = PASS // 16
 PAIR = 2
 RUN = 4
-ROW = J + N
+BLOCK = 8
 TINY = 1e-36
 
 SLOT = PACK * HALF * 4
 GROUP = PACK * HALF * 2
-WEIGHTS = 4 * SLOT + GROUP
+WEIGHTS = 5 * SLOT
 CHAIN = 6 * SLOT
 
 
@@ -50,16 +50,10 @@ def tile_list_kernl_poly2_mix_res_kernel(
         nc.vector.memset(scale_rows[64:128, :].bitcast(I32), 0)
         nc.vector.memset(scale_rows[32:64, :].bitcast(I32), 0)
 
-        cw_sb = keep.tile([P, 2 * PACK], F32, name="cw_sb")
-        nc.scalar.dma_start(cw_sb[:].rearrange("p (b t) -> p b t", b=2), cw.rearrange("(b p t) -> p b t", b=2, t=PACK))
-
-        staged = stage.tile([P, ROW], U8, name="staged", offset=WEIGHTS, align_bytes=64)
-        for b, scales in enumerate((al8_scales, al4_scales)):
-            lo = J + b * (N // 2)
-            nc.scalar.dma_start(
-                staged[0:32, lo : lo + N // 2].bitcast(I32),
-                scales[0].rearrange("q (a n) -> (q a) n", a=2).bitcast(I32),
-            )
+        cw_sb = keep.tile([P, 2, BLOCK], F32, name="cw_sb")
+        nc.scalar.dma_start(cw_sb[:, :, 0:PACK], cw.rearrange("(b p t) -> p b t", b=2, t=PACK))
+        cb_sb = keep.tile([P, 2, BLOCK], F32, name="cb_sb")
+        nc.scalar.dma_start(cb_sb[:, :, 0:PACK], cb.rearrange("(b p t) -> p b t", b=2, t=PACK))
 
         table = keep.tile([P, T], I32, name="table", align_bytes=64)
         nc.sync.dma_start(table[:], tab_words[0].rearrange("p t f -> p (t f)").bitcast(I32))
@@ -77,21 +71,20 @@ def tile_list_kernl_poly2_mix_res_kernel(
         load_x(0, 0)
         load_x(0, 1)
 
-        cb_sb = keep.tile([P, 2 * PACK], F32, name="cb_sb")
-        nc.gpsimd.dma_start(cb_sb[:].rearrange("p (b t) -> p b t", b=2), cb.rearrange("(b p t) -> p b t", b=2, t=PACK))
-
-        placed = keep.tile([P, 2, ROW], U8, name="placed", align_bytes=64)
+        placed = keep.tile([P, 2, J], U8, name="placed", align_bytes=64)
         nc.gpsimd.memset(placed[:].rearrange("p a n -> p (a n)").bitcast(I32), 0)
+        al_placed = keep.tile([P, 2, N], U8, name="al_placed", align_bytes=64)
+        nc.gpsimd.memset(al_placed[:].rearrange("p a n -> p (a n)").bitcast(I32), 0)
 
         def small(name, dtype=F32):
-            return keep.tile([P, 2 * PACK], dtype, name=name)
+            return keep.tile([P, 2, PACK], dtype, name=name)
 
         guess = small("guess")
-        nc.scalar.activation(guess[:], cw_sb[:], ACT.Abs_reciprocal_sqrt, bias=TINY)
+        nc.scalar.activation(guess[:], cw_sb[:, :, 0:PACK], ACT.Abs_reciprocal_sqrt, bias=TINY)
         size = small("size")
-        nc.scalar.activation(size[:], cw_sb[:], ACT.Abs)
+        nc.scalar.activation(size[:], cw_sb[:, :, 0:PACK], ACT.Abs)
         sign = small("sign", BF16)
-        nc.scalar.activation(sign[:], cw_sb[:], ACT.Sign)
+        nc.scalar.activation(sign[:], cw_sb[:, :, 0:PACK], ACT.Sign)
         rough = small("rough")
         nc.gpsimd.tensor_tensor(rough[:], size[:], guess[:], ALU.mult)
         near_one = small("near_one")
@@ -101,19 +94,24 @@ def tile_list_kernl_poly2_mix_res_kernel(
         root = small("root")
         nc.gpsimd.tensor_tensor(root[:], rough[:], factor[:], ALU.mult)
         shift = small("shift")
-        nc.gpsimd.tensor_tensor(shift[:], root[:], cb_sb[:], ALU.mult)
+        nc.gpsimd.tensor_tensor(shift[:], root[:], cb_sb[:, :, 0:PACK], ALU.mult)
 
         picked_scales = stage.tile([P, J], U8, name="picked_scales", offset=3 * SLOT - J // 2, align_bytes=64)
+        staged = stage.tile([P, J], U8, name="staged", offset=WEIGHTS, align_bytes=64)
         nc.vector.tensor_copy(picked_scales[:], scale_rows[:].indirect(offsets[:]))
         nc.vector.tensor_copy(
-            staged[:, 0:J].rearrange("p (b t m) -> p b t m", b=2, t=PACK),
+            staged[:].rearrange("p (b t m) -> p b t m", b=2, t=PACK),
             picked_scales[:].rearrange("p (b m t) -> p b t m", b=2, t=PACK),
         )
-        for quad in range(QUADS):
-            nc.sync.dma_start(
-                placed[32 * quad : 32 * quad + 4].rearrange("p a n -> p (a n)").bitcast(I32),
-                staged[8 * quad : 8 * quad + 8, :].bitcast(I32),
-            )
+
+        def place_rows(dst, src):
+            for quad in (0, 2, 1, 3):
+                nc.sync.dma_start(
+                    dst[32 * quad : 32 * quad + 4].rearrange("p a n -> p (a n)").bitcast(I32),
+                    src[8 * quad : 8 * quad + 8, :].bitcast(I32),
+                )
+
+        place_rows(placed, staged)
         load_x(1, 0)
         load_x(1, 1)
 
@@ -164,13 +162,17 @@ def tile_list_kernl_poly2_mix_res_kernel(
         x_mx[1, 0] = quantize(third, "x1_0")
         x_mx[1, 1] = quantize(last, "x1_1")
 
-        al8 = stage.tile([P, N], I32, name="al8", offset=WEIGHTS + 2 * N, align_bytes=64)
+        al_staged = stage.tile([P, N], U8, name="al_staged", offset=WEIGHTS + N // 2, align_bytes=64)
+        for a, scales in enumerate((al8_scales, al4_scales)):
+            nc.sync.dma_start(al_staged[a:32:2, :].bitcast(I32), scales[0].bitcast(I32))
+        al8 = stage.tile([P, N], I32, name="al8", offset=WEIGHTS + 3 * N // 2, align_bytes=64)
         nc.sync.dma_start(al8[:], al8_words[0].rearrange("p n f -> p (n f)").bitcast(I32))
-        al4 = stage.tile([P, 2 * N], U8, name="al4", offset=WEIGHTS, align_bytes=64)
+        al4 = stage.tile([P, 2 * N], U8, name="al4", offset=WEIGHTS - 3 * N // 2, align_bytes=64)
         nc.sync.dma_start(al4[:].bitcast(I32), al4_words[0].bitcast(I32))
+        place_rows(al_placed, al_staged)
         res_rows = res.rearrange("(c p) m -> p c m", p=P)
         res_sb = []
-        for half, offset in enumerate((0, WEIGHTS - SLOT)):
+        for half, offset in enumerate((0, 3 * SLOT + GROUP)):
             rows = stage.tile([P, N // P, HALF], F32, name="res%d" % half, offset=offset, align_bytes=64)
             nc.sync.dma_start(rows[:], res_rows[:, :, HALF * half : HALF * (half + 1)])
             res_sb.append(rows)
@@ -223,12 +225,11 @@ def tile_list_kernl_poly2_mix_res_kernel(
                 [P, PACK, HALF], F32, name="squares%d" % b, offset=SLOT * (2 + b) - SLOT // 2, align_bytes=64
             )
             for t in range(PACK):
-                col = PACK * b + t
-                nc.scalar.activation(squares[:, t, :], dots[t], ACT.Square, bias=cb_sb[:, col : col + 1])
+                nc.scalar.activation(squares[:, t, :], dots[t], ACT.Square, bias=cb_sb[:, b, t : t + 1])
             grouped = stage.tile(
                 [P, HALF, PACK], BF16, name="h_grouped0%d" % b, offset=CHAIN + GROUP * b, align_bytes=64
             )
-            weights = cw_sb[:, PACK * b : PACK * (b + 1)].rearrange("p (c t i) -> p c t i", c=1, i=1)
+            weights = cw_sb[:, b, 0:PACK].rearrange("p (c t i) -> p c t i", c=1, i=1)
             nc.vector.tensor_tensor(
                 as_words(grouped), as_rows(squares), weights.to_broadcast([P, HALF // PAIR, PACK, PAIR]), ALU.mult
             )
@@ -238,16 +239,15 @@ def tile_list_kernl_poly2_mix_res_kernel(
             width = dots[0].shape[1]
             pairs = keep.tile([P, 2, width, 2], BF16, name="pairs" + name, align_bytes=64)
             for t in range(PACK):
-                col = PACK * b + t
                 nc.scalar.activation(
                     pairs[:, t // 2, :, t % 2],
                     dots[t],
                     ACT.Square,
-                    bias=shift[:, col : col + 1],
-                    scale=root[:, col : col + 1],
+                    bias=shift[:, b, t : t + 1],
+                    scale=root[:, b, t : t + 1],
                 )
             grouped = keep.tile([P, width, PACK], BF16, name="h_grouped" + name, align_bytes=64)
-            signs = sign[:, PACK * b : PACK * (b + 1)].rearrange("p (m u e) -> p m u e", m=1, u=2)
+            signs = sign[:, b, :].rearrange("p (m u e) -> p m u e", m=1, u=2)
             nc.vector.tensor_tensor(
                 grouped[:].rearrange("p m (u e) -> p m u e", u=2),
                 pairs[:].rearrange("p u m e -> p m u e"),
@@ -257,7 +257,6 @@ def tile_list_kernl_poly2_mix_res_kernel(
             return quantize(grouped, "h" + name)
 
         def sum_pass(dst, b, c, codes, scale, start, stop):
-            lo = J + b * (N // 2) + P * (c % 2)
             if b == 0:
                 weights = al8[:, P * c : P * (c + 1)].bitcast(E4M3)
             else:
@@ -265,7 +264,7 @@ def tile_list_kernl_poly2_mix_res_kernel(
             nc.tensor.matmul_mx(
                 out=dst,
                 lhsT=weights,
-                lhsT_scale=placed[:, c // 2, lo : lo + P],
+                lhsT_scale=al_placed[:, b, P * c : P * (c + 1)],
                 rhs=codes.bitcast(E4M3),
                 rhs_scale=scale,
                 start=start,

@@ -29,8 +29,10 @@ TINY = 1e-36
 
 SLOT = PACK * HALF * 4
 GROUP = PACK * HALF * 2
-WEIGHTS = 5 * SLOT
-CHAIN = 6 * SLOT
+X_AT = {(0, 0): 0, (0, 1): SLOT, (1, 0): 2 * SLOT + GROUP, (1, 1): 3 * SLOT + GROUP + N}
+STAGED = 6 * SLOT
+CODES = STAGED + J
+LATE = 8 * SLOT
 
 
 def tile_list_kernl_poly2_mix_res_kernel(
@@ -63,7 +65,7 @@ def tile_list_kernl_poly2_mix_res_kernel(
 
         def load_x(half, a):
             raw = stage.tile(
-                [P, PACK, HALF], F32, name="x_raw%d_%d" % (half, a), offset=SLOT * (2 * half + a), align_bytes=64
+                [P, PACK, HALF], F32, name="x_raw%d_%d" % (half, a), offset=X_AT[half, a], align_bytes=64
             )
             nc.sync.dma_start(raw[:], x_rows[a][:, :, HALF * half : HALF * (half + 1)])
             x_raw[half, a] = raw
@@ -96,8 +98,8 @@ def tile_list_kernl_poly2_mix_res_kernel(
         shift = small("shift")
         nc.gpsimd.tensor_tensor(shift[:], root[:], cb_sb[:, :, 0:PACK], ALU.mult)
 
-        picked_scales = stage.tile([P, J], U8, name="picked_scales", offset=3 * SLOT - J // 2, align_bytes=64)
-        staged = stage.tile([P, J], U8, name="staged", offset=WEIGHTS, align_bytes=64)
+        picked_scales = stage.tile([P, J], U8, name="picked_scales", offset=X_AT[1, 1] - N - N // 2, align_bytes=64)
+        staged = stage.tile([P, J], U8, name="staged", offset=STAGED, align_bytes=64)
         nc.vector.tensor_copy(picked_scales[:], scale_rows[:].indirect(offsets[:]))
         nc.vector.tensor_copy(
             staged[:].rearrange("p (b t m) -> p b t m", b=2, t=PACK),
@@ -114,6 +116,9 @@ def tile_list_kernl_poly2_mix_res_kernel(
         place_rows(placed, staged)
         load_x(1, 0)
         load_x(1, 1)
+        al_staged = stage.tile([P, N], U8, name="al_staged", offset=X_AT[1, 1] - N, align_bytes=64)
+        for a, scales in enumerate((al8_scales, al4_scales)):
+            nc.sync.dma_start(al_staged[a:32:2, :].bitcast(I32), scales[0].bitcast(I32))
 
         def as_words(grouped):
             return grouped[:].rearrange("p (c i) t -> p c t i", i=PAIR)
@@ -121,9 +126,12 @@ def tile_list_kernl_poly2_mix_res_kernel(
         def as_rows(rows):
             return rows[:].rearrange("p t (c i) -> p c t i", i=PAIR)
 
-        def quantize(grouped, name):
+        def quantize(grouped, name, offset=None):
             width = grouped.shape[1]
-            codes = keep.tile([P, width], U32, name=name + "_codes", align_bytes=64)
+            if offset is None:
+                codes = keep.tile([P, width], U32, name=name + "_codes", align_bytes=64)
+            else:
+                codes = stage.tile([P, width], U32, name=name + "_codes", offset=offset, align_bytes=64)
             scale = keep.tile([P, width], U8, name=name + "_scale", align_bytes=64)
             nc.vector.quantize_mx(
                 out=codes[:].bitcast(E4M3), scales=scale[:], in_=grouped[:].rearrange("p m t -> p (m t)")
@@ -142,10 +150,27 @@ def tile_list_kernl_poly2_mix_res_kernel(
                 words[:].bitcast(U16).rearrange("p (c i t a) -> p a c t i", i=RUN, t=PACK, a=2),
             )
 
+        idle = keep.tile([P, HALF, PACK], BF16, name="idle", align_bytes=64)
+        nc.gpsimd.memset(idle[:], 0.0)
+        idle_codes, idle_scale = quantize(idle, "idle")
+
         picked = [keep.tile([P, PASS], U32, name="picked%d" % b, align_bytes=64) for b in range(2)]
         for b in range(2):
             nc.vector.tensor_copy(
                 picked[b][:], table[:].bitcast(U32).indirect(offsets[:, LIST_COLS * b : LIST_COLS * (b + 1)])
+            )
+
+        warm = psum.tile([P, HALF], F32, name="warm", tag="bank7")
+        widths = (HALF, HALF, HALF, HALF, P)
+        for i, width in enumerate(widths):
+            nc.tensor.matmul_mx(
+                out=warm[:, 0:width],
+                lhsT=picked[0][:, 0 : P // 2].bitcast(U8).bitcast(E2M1),
+                lhsT_scale=staged[:, 0:P],
+                rhs=idle_codes[:, 0:width].bitcast(E4M3),
+                rhs_scale=idle_scale[:, 0:width],
+                start=i == 0,
+                stop=i == len(widths) - 1,
             )
 
         x_mx = {}
@@ -156,26 +181,24 @@ def tile_list_kernl_poly2_mix_res_kernel(
             x_mx[0, a] = quantize(first_half[a], "x0_%d" % a)
         centres.append(keep.tile([P, 2, 2 * PASS], U8, name="centres1", tag="x_grouped0_0", align_bytes=64))
         part_words(picked[1], centres[1])
-        third = interleave_on_scalar(1, 0)
-        last = stage.tile([P, HALF, PACK], BF16, name="x_grouped1_1", offset=CHAIN + GROUP // 2, align_bytes=64)
-        nc.vector.tensor_copy(as_words(last), as_rows(x_raw[1, 1]))
-        x_mx[1, 0] = quantize(third, "x1_0")
-        x_mx[1, 1] = quantize(last, "x1_1")
+        for a in range(2):
+            grouped = stage.tile([P, HALF, PACK], BF16, name="x_grouped1_%d" % a, offset=LATE + GROUP * a, align_bytes=64)
+            nc.vector.tensor_copy(as_words(grouped), as_rows(x_raw[1, a]))
+            x_mx[1, a] = quantize(grouped, "x1_%d" % a)
 
-        al_staged = stage.tile([P, N], U8, name="al_staged", offset=WEIGHTS + N // 2, align_bytes=64)
-        for a, scales in enumerate((al8_scales, al4_scales)):
-            nc.sync.dma_start(al_staged[a:32:2, :].bitcast(I32), scales[0].bitcast(I32))
-        al8 = stage.tile([P, N], I32, name="al8", offset=WEIGHTS + 3 * N // 2, align_bytes=64)
+        res_rows = res.rearrange("(c p) m -> p c m", p=P)
+        res_first = []
+        for pair in range(2):
+            rows = stage.tile([P, 2, HALF], F32, name="res0_%d" % pair, offset=pair * SLOT // 2, align_bytes=64)
+            nc.sync.dma_start(rows[:], res_rows[:, 2 * pair : 2 * pair + 2, 0:HALF])
+            res_first.append(rows)
+        al8 = stage.tile([P, N], I32, name="al8", offset=SLOT, align_bytes=64)
         nc.sync.dma_start(al8[:], al8_words[0].rearrange("p n f -> p (n f)").bitcast(I32))
-        al4 = stage.tile([P, 2 * N], U8, name="al4", offset=WEIGHTS - 3 * N // 2, align_bytes=64)
+        al4 = stage.tile([P, 2 * N], U8, name="al4", offset=SLOT + 4 * N, align_bytes=64)
         nc.sync.dma_start(al4[:].bitcast(I32), al4_words[0].bitcast(I32))
         place_rows(al_placed, al_staged)
-        res_rows = res.rearrange("(c p) m -> p c m", p=P)
-        res_sb = []
-        for half, offset in enumerate((0, 3 * SLOT + GROUP)):
-            rows = stage.tile([P, N // P, HALF], F32, name="res%d" % half, offset=offset, align_bytes=64)
-            nc.sync.dma_start(rows[:], res_rows[:, :, HALF * half : HALF * (half + 1)])
-            res_sb.append(rows)
+        res_second = stage.tile([P, N // P, HALF], F32, name="res1", offset=LATE + GROUP, align_bytes=64)
+        nc.sync.dma_start(res_second[:], res_rows[:, :, HALF:M])
         out_rows = out.rearrange("(c p) m -> p c m", p=P)
 
         def dot_pass(dst, b, t, a, codes, scale, start, stop):
@@ -203,11 +226,9 @@ def tile_list_kernl_poly2_mix_res_kernel(
             for u, a in order:
                 codes, scale = x_mx[half, a]
                 for i in range(width):
-                    for g in range(HALF // P):
-                        cols = slice(P * g, P * (g + 1))
-                        start = a == opening and i == 0 and g == 0
-                        stop = a != opening and i == width - 1 and g == HALF // P - 1
-                        dot_pass(banks[u][:, i, cols], b, width * u + i, a, codes[:, cols], scale[:, cols], start, stop)
+                    start = a == opening and i == 0
+                    stop = a != opening and i == width - 1
+                    dot_pass(banks[u][:, i, :], b, width * u + i, a, codes[:], scale[:], start, stop)
             return [banks[t // width][:, t % width, :] for t in range(PACK)]
 
         def dots_of_quarter(g, bank_no):
@@ -221,21 +242,19 @@ def tile_list_kernl_poly2_mix_res_kernel(
             return [bank[:, t, :] for t in range(PACK)]
 
         def weighted_on_vector(dots, b):
-            squares = stage.tile(
-                [P, PACK, HALF], F32, name="squares%d" % b, offset=SLOT * (2 + b) - SLOT // 2, align_bytes=64
-            )
+            squares = keep.tile([P, PACK, HALF], F32, name="squares%d" % b, align_bytes=64)
             for t in range(PACK):
                 nc.scalar.activation(squares[:, t, :], dots[t], ACT.Square, bias=cb_sb[:, b, t : t + 1])
             grouped = stage.tile(
-                [P, HALF, PACK], BF16, name="h_grouped0%d" % b, offset=CHAIN + GROUP * b, align_bytes=64
+                [P, HALF, PACK], BF16, name="h_grouped0%d" % b, offset=X_AT[1, 1], align_bytes=64
             )
             weights = cw_sb[:, b, 0:PACK].rearrange("p (c t i) -> p c t i", c=1, i=1)
             nc.vector.tensor_tensor(
                 as_words(grouped), as_rows(squares), weights.to_broadcast([P, HALF // PAIR, PACK, PAIR]), ALU.mult
             )
-            return quantize(grouped, "h0%d" % b)
+            return grouped
 
-        def weighted_on_scalar(dots, b, name):
+        def weighted_on_scalar(dots, b, name, offset):
             width = dots[0].shape[1]
             pairs = keep.tile([P, 2, width, 2], BF16, name="pairs" + name, align_bytes=64)
             for t in range(PACK):
@@ -246,7 +265,7 @@ def tile_list_kernl_poly2_mix_res_kernel(
                     bias=shift[:, b, t : t + 1],
                     scale=root[:, b, t : t + 1],
                 )
-            grouped = keep.tile([P, width, PACK], BF16, name="h_grouped" + name, align_bytes=64)
+            grouped = stage.tile([P, width, PACK], BF16, name="h_grouped" + name, offset=offset, align_bytes=64)
             signs = sign[:, b, :].rearrange("p (m u e) -> p m u e", m=1, u=2)
             nc.vector.tensor_tensor(
                 grouped[:].rearrange("p m (u e) -> p m u e", u=2),
@@ -254,7 +273,7 @@ def tile_list_kernl_poly2_mix_res_kernel(
                 signs.to_broadcast([P, width, 2, 2]),
                 ALU.mult,
             )
-            return quantize(grouped, "h" + name)
+            return grouped
 
         def sum_pass(dst, b, c, codes, scale, start, stop):
             if b == 0:
@@ -271,41 +290,42 @@ def tile_list_kernl_poly2_mix_res_kernel(
                 stop=stop,
             )
 
-        def finish(sums, name, rows, half, lo, width):
-            result = keep.tile([P, rows.stop - rows.start, width], F32, name="result" + name, align_bytes=64)
-            nc.vector.tensor_tensor(result[:], sums, res_sb[half][:, rows, lo : lo + width], ALU.add)
-            nc.sync.dma_start(out_rows[:, rows, HALF * half + lo : HALF * half + lo + width], result[:])
+        def finish(sums, residual, name, rows, cols):
+            result = keep.tile([P, rows.stop - rows.start, cols.stop - cols.start], F32, name="result" + name)
+            nc.vector.tensor_tensor(result[:], sums, residual, ALU.add)
+            nc.sync.dma_start(out_rows[:, rows, cols], result[:])
 
         tiles = N // P
+        free = CODES + 4 * HALF
         dots00 = dots_of_part(0, 0, 1, 0)
-        codes00, scale00 = weighted_on_vector(dots00, 0)
+        grouped00 = weighted_on_vector(dots00, 0)
         dots01 = dots_of_part(0, 1, 2, 4)
         dots10 = dots_of_part(1, 0, 2, 0)
-        codes01, scale01 = weighted_on_vector(dots01, 1)
+        grouped01 = weighted_on_scalar(dots01, 1, "01", X_AT[1, 1] + GROUP)
+        codes00, scale00 = quantize(grouped00, "h00")
+        codes01, scale01 = quantize(grouped01, "h01", CODES)
         dots11 = [dots_of_quarter(g, 4 + g) for g in range(2)]
 
         sums0 = [psum.tile([P, 2, HALF], F32, name="sum0_%d" % pair, tag="bank%d" % (6 + pair)) for pair in range(2)]
-        for c in range(tiles):
-            sum_pass(sums0[c // 2][:, c % 2, :], 0, c, codes00[:], scale00[:], c % 2 == 0, False)
-        for c in range(tiles):
-            for g in range(2):
-                cols = slice(P * g, P * (g + 1))
-                stop = c % 2 == 1 and g == 1
-                sum_pass(sums0[c // 2][:, c % 2, cols], 1, c, codes01[:, cols], scale01[:, cols], False, stop)
+        for b, (codes, scale) in enumerate(((codes00, scale00), (codes01, scale01))):
+            for c in range(tiles):
+                sum_pass(sums0[c // 2][:, c % 2, :], b, c, codes[:], scale[:], b == 0 and c % 2 == 0, b == 1 and c % 2 == 1)
 
-        codes10, scale10 = weighted_on_scalar(dots10, 0, "10")
+        grouped10 = weighted_on_scalar(dots10, 0, "10", free)
+        finish(sums0[0][:], res_first[0][:], "0_0", slice(0, 2), slice(0, HALF))
+        codes10, scale10 = quantize(grouped10, "h10", CODES)
         sums1 = [psum.tile([P, tiles, P], F32, name="sum1_%d" % g, tag="bank%d" % (2 + g)) for g in range(2)]
         for g in range(2):
             cols = slice(P * g, P * (g + 1))
             for c in range(tiles):
                 sum_pass(sums1[g][:, c, :], 0, c, codes10[:, cols], scale10[:, cols], c == 0, False)
-        for pair in range(2):
-            finish(sums0[pair][:], "0_%d" % pair, slice(2 * pair, 2 * pair + 2), 0, 0, HALF)
+        grouped11 = [weighted_on_scalar(dots11[g], 1, "11_%d" % g, g * GROUP // 2) for g in range(2)]
         for g in range(2):
-            codes11, scale11 = weighted_on_scalar(dots11[g], 1, "11_%d" % g)
+            codes11, scale11 = quantize(grouped11[g], "h11_%d" % g)
             for c in range(tiles):
                 sum_pass(sums1[g][:, c, :], 1, c, codes11[:], scale11[:], False, c == tiles - 1)
-        finish(sums1[0][:], "1_0", slice(0, tiles), 1, 0, P)
+        finish(sums0[1][:], res_first[1][:], "0_1", slice(2, 4), slice(0, HALF))
+        finish(sums1[0][:], res_second[:, :, 0:P], "1_0", slice(0, tiles), slice(HALF, HALF + P))
         for pair in range(2):
             rows = slice(2 * pair, 2 * pair + 2)
-            finish(sums1[1][:, rows, :], "1_1_%d" % pair, rows, 1, P, P)
+            finish(sums1[1][:, rows, :], res_second[:, rows, P:HALF], "1_1_%d" % pair, rows, slice(HALF + P, M))

@@ -241,12 +241,12 @@ def tile_list_kernl_poly2_mix_res_kernel(
                     dot_pass(bank[:, t, :], 1, t, a, codes[:, cols], scale[:, cols], start, stop)
             return [bank[:, t, :] for t in range(PACK)]
 
-        def weighted_on_vector(dots, b):
+        def weighted_on_vector(dots, b, offset):
             squares = keep.tile([P, PACK, HALF], F32, name="squares%d" % b, align_bytes=64)
             for t in range(PACK):
                 nc.scalar.activation(squares[:, t, :], dots[t], ACT.Square, bias=cb_sb[:, b, t : t + 1])
             grouped = stage.tile(
-                [P, HALF, PACK], BF16, name="h_grouped0%d" % b, offset=X_AT[1, 1], align_bytes=64
+                [P, HALF, PACK], BF16, name="h_grouped0%d" % b, offset=offset, align_bytes=64
             )
             weights = cw_sb[:, b, 0:PACK].rearrange("p (c t i) -> p c t i", c=1, i=1)
             nc.vector.tensor_tensor(
@@ -298,10 +298,10 @@ def tile_list_kernl_poly2_mix_res_kernel(
         tiles = N // P
         free = CODES + 4 * HALF
         dots00 = dots_of_part(0, 0, 1, 0)
-        grouped00 = weighted_on_vector(dots00, 0)
+        grouped00 = weighted_on_vector(dots00, 0, X_AT[1, 1])
         dots01 = dots_of_part(0, 1, 2, 4)
         dots10 = dots_of_part(1, 0, 2, 0)
-        grouped01 = weighted_on_scalar(dots01, 1, "01", X_AT[1, 1] + GROUP)
+        grouped01 = weighted_on_vector(dots01, 1, X_AT[1, 1] + GROUP)
         codes00, scale00 = quantize(grouped00, "h00")
         codes01, scale01 = quantize(grouped01, "h01", CODES)
         dots11 = [dots_of_quarter(g, 4 + g) for g in range(2)]

@@ -181,10 +181,23 @@ def tile_list_kernl_poly2_mix_res_kernel(
             x_mx[0, a] = quantize(first_half[a], "x0_%d" % a)
         centres.append(keep.tile([P, 2, 2 * PASS], U8, name="centres1", tag="x_grouped0_0", align_bytes=64))
         part_words(picked[1], centres[1])
-        for a in range(2):
-            grouped = stage.tile([P, HALF, PACK], BF16, name="x_grouped1_%d" % a, offset=LATE + GROUP * a, align_bytes=64)
-            nc.vector.tensor_copy(as_words(grouped), as_rows(x_raw[1, a]))
-            x_mx[1, a] = quantize(grouped, "x1_%d" % a)
+        third = stage.tile([P, HALF, PACK], BF16, name="x_grouped1_0", offset=LATE, align_bytes=64)
+        nc.vector.tensor_copy(as_words(third), as_rows(x_raw[1, 0]))
+        x_mx[1, 0] = quantize(third, "x1_0")
+        last = stage.tile([P, HALF, PACK], BF16, name="x_grouped1_1", offset=LATE + GROUP, align_bytes=64)
+        last_codes = keep.tile([P, HALF], U32, name="x1_1_codes", align_bytes=64)
+        last_scale = keep.tile([P, HALF], U8, name="x1_1_scale", align_bytes=64)
+        for g in range(2):
+            pairs = slice(g * P // PAIR, (g + 1) * P // PAIR)
+            nc.vector.tensor_copy(as_words(last)[:, pairs], as_rows(x_raw[1, 1])[:, pairs])
+        for g in range(2):
+            cols = slice(P * g, P * (g + 1))
+            nc.vector.quantize_mx(
+                out=last_codes[:, cols].bitcast(E4M3),
+                scales=last_scale[:, cols],
+                in_=last[:, cols, :].rearrange("p m t -> p (m t)"),
+            )
+        x_mx[1, 1] = last_codes, last_scale
 
         res_rows = res.rearrange("(c p) m -> p c m", p=P)
         res_first = []
@@ -218,7 +231,7 @@ def tile_list_kernl_poly2_mix_res_kernel(
                 psum.tile([P, width, HALF], F32, name="dot%d_%d_%d" % (half, b, u), tag="bank%d" % (first_bank + u))
                 for u in range(PACK // width)
             ]
-            if (half, b) == (0, 0):
+            if b == 0:
                 order = [(u, a) for a in range(2) for u in range(len(banks))]
             else:
                 order = [(u, a) for u in range(len(banks)) for a in (1, 0)]
@@ -300,16 +313,17 @@ def tile_list_kernl_poly2_mix_res_kernel(
         dots00 = dots_of_part(0, 0, 1, 0)
         grouped00 = weighted_on_vector(dots00, 0, X_AT[1, 1])
         dots01 = dots_of_part(0, 1, 2, 4)
-        dots10 = dots_of_part(1, 0, 2, 0)
+        dots10 = dots_of_part(1, 0, 1, 0)
         grouped01 = weighted_on_vector(dots01, 1, X_AT[1, 1] + GROUP)
         codes00, scale00 = quantize(grouped00, "h00")
         codes01, scale01 = quantize(grouped01, "h01", CODES)
         dots11 = [dots_of_quarter(g, 4 + g) for g in range(2)]
 
         sums0 = [psum.tile([P, 2, HALF], F32, name="sum0_%d" % pair, tag="bank%d" % (6 + pair)) for pair in range(2)]
-        for b, (codes, scale) in enumerate(((codes00, scale00), (codes01, scale01))):
-            for c in range(tiles):
-                sum_pass(sums0[c // 2][:, c % 2, :], b, c, codes[:], scale[:], b == 0 and c % 2 == 0, b == 1 and c % 2 == 1)
+        for pair in range(2):
+            for b, (codes, scale) in enumerate(((codes00, scale00), (codes01, scale01))):
+                for i in range(2):
+                    sum_pass(sums0[pair][:, i, :], b, 2 * pair + i, codes[:], scale[:], b == 0 and i == 0, b == 1 and i == 1)
 
         grouped10 = weighted_on_scalar(dots10, 0, "10", free)
         finish(sums0[0][:], res_first[0][:], "0_0", slice(0, 2), slice(0, HALF))

@@ -187,10 +187,10 @@ def tile_list_kernl_poly2_mix_res_kernel(
         last = stage.tile([P, HALF, PACK], BF16, name="x_grouped1_1", offset=LATE + GROUP, align_bytes=64)
         last_codes = keep.tile([P, HALF], U32, name="x1_1_codes", align_bytes=64)
         last_scale = keep.tile([P, HALF], U8, name="x1_1_scale", align_bytes=64)
-        for g in range(2):
+        for g in (1, 0):
             pairs = slice(g * P // PAIR, (g + 1) * P // PAIR)
             nc.vector.tensor_copy(as_words(last)[:, pairs], as_rows(x_raw[1, 1])[:, pairs])
-        for g in range(2):
+        for g in (1, 0):
             cols = slice(P * g, P * (g + 1))
             nc.vector.quantize_mx(
                 out=last_codes[:, cols].bitcast(E4M3),
@@ -317,7 +317,7 @@ def tile_list_kernl_poly2_mix_res_kernel(
         grouped01 = weighted_on_vector(dots01, 1, X_AT[1, 1] + GROUP)
         codes00, scale00 = quantize(grouped00, "h00")
         codes01, scale01 = quantize(grouped01, "h01", CODES)
-        dots11 = [dots_of_quarter(g, 4 + g) for g in range(2)]
+        dots11 = [dots_of_quarter(g, bank_no) for g, bank_no in enumerate((4, 0))]
 
         sums0 = [psum.tile([P, 2, HALF], F32, name="sum0_%d" % pair, tag="bank%d" % (6 + pair)) for pair in range(2)]
         for pair in range(2):

@@ -20,18 +20,21 @@ P = 128
 PACK = 4
 PASS = P * PACK
 HALF = M // 2
-QUADS = 4
 LIST_COLS = PASS // 16
 PAIR = 2
 RUN = 4
 BLOCK = 8
 TINY = 1e-36
 
+WARM_UP = (HALF, HALF, HALF, HALF, P)
+
 SLOT = PACK * HALF * 4
 GROUP = PACK * HALF * 2
 X_AT = {(0, 0): 0, (0, 1): SLOT, (1, 0): 2 * SLOT + GROUP, (1, 1): 3 * SLOT + GROUP + N}
+AL_STAGED = X_AT[1, 1] - N
 STAGED = 6 * SLOT
 CODES = STAGED + J
+THIRD_PART = CODES + 4 * HALF
 LATE = 8 * SLOT
 
 
@@ -98,7 +101,7 @@ def tile_list_kernl_poly2_mix_res_kernel(
         shift = small("shift")
         nc.gpsimd.tensor_tensor(shift[:], root[:], cb_sb[:, :, 0:PACK], ALU.mult)
 
-        picked_scales = stage.tile([P, J], U8, name="picked_scales", offset=X_AT[1, 1] - N - N // 2, align_bytes=64)
+        picked_scales = stage.tile([P, J], U8, name="picked_scales", offset=AL_STAGED - N // 2, align_bytes=64)
         staged = stage.tile([P, J], U8, name="staged", offset=STAGED, align_bytes=64)
         nc.vector.tensor_copy(picked_scales[:], scale_rows[:].indirect(offsets[:]))
         nc.vector.tensor_copy(
@@ -116,7 +119,7 @@ def tile_list_kernl_poly2_mix_res_kernel(
         place_rows(placed, staged)
         load_x(1, 0)
         load_x(1, 1)
-        al_staged = stage.tile([P, N], U8, name="al_staged", offset=X_AT[1, 1] - N, align_bytes=64)
+        al_staged = stage.tile([P, N], U8, name="al_staged", offset=AL_STAGED, align_bytes=64)
         for a, scales in enumerate((al8_scales, al4_scales)):
             nc.sync.dma_start(al_staged[a:32:2, :].bitcast(I32), scales[0].bitcast(I32))
 
@@ -151,7 +154,7 @@ def tile_list_kernl_poly2_mix_res_kernel(
             )
 
         idle = keep.tile([P, HALF, PACK], BF16, name="idle", align_bytes=64)
-        nc.gpsimd.memset(idle[:], 0.0)
+        nc.vector.memset(idle[:].rearrange("p m t -> p (m t)").bitcast(I32), 0)
         idle_codes, idle_scale = quantize(idle, "idle")
 
         picked = [keep.tile([P, PASS], U32, name="picked%d" % b, align_bytes=64) for b in range(2)]
@@ -161,8 +164,7 @@ def tile_list_kernl_poly2_mix_res_kernel(
             )
 
         warm = psum.tile([P, HALF], F32, name="warm", tag="bank7")
-        widths = (HALF, HALF, HALF, HALF, P)
-        for i, width in enumerate(widths):
+        for i, width in enumerate(WARM_UP):
             nc.tensor.matmul_mx(
                 out=warm[:, 0:width],
                 lhsT=picked[0][:, 0 : P // 2].bitcast(U8).bitcast(E2M1),
@@ -170,7 +172,7 @@ def tile_list_kernl_poly2_mix_res_kernel(
                 rhs=idle_codes[:, 0:width].bitcast(E4M3),
                 rhs_scale=idle_scale[:, 0:width],
                 start=i == 0,
-                stop=i == len(widths) - 1,
+                stop=i == len(WARM_UP) - 1,
             )
 
         x_mx = {}
@@ -258,34 +260,35 @@ def tile_list_kernl_poly2_mix_res_kernel(
             squares = keep.tile([P, PACK, HALF], F32, name="squares%d" % b, align_bytes=64)
             for t in range(PACK):
                 nc.scalar.activation(squares[:, t, :], dots[t], ACT.Square, bias=cb_sb[:, b, t : t + 1])
-            grouped = stage.tile(
-                [P, HALF, PACK], BF16, name="h_grouped0%d" % b, offset=offset, align_bytes=64
-            )
+            grouped = stage.tile([P, HALF, PACK], BF16, name="h_grouped0%d" % b, offset=offset, align_bytes=64)
             weights = cw_sb[:, b, 0:PACK].rearrange("p (c t i) -> p c t i", c=1, i=1)
             nc.vector.tensor_tensor(
                 as_words(grouped), as_rows(squares), weights.to_broadcast([P, HALF // PAIR, PACK, PAIR]), ALU.mult
             )
             return grouped
 
-        def weighted_on_scalar(dots, b, name, offset):
+        def weighted_on_scalar(dots, b, name, offset, steps=1):
             width = dots[0].shape[1]
-            pairs = keep.tile([P, 2, width, 2], BF16, name="pairs" + name, align_bytes=64)
-            for t in range(PACK):
-                nc.scalar.activation(
-                    pairs[:, t // 2, :, t % 2],
-                    dots[t],
-                    ACT.Square,
-                    bias=shift[:, b, t : t + 1],
-                    scale=root[:, b, t : t + 1],
-                )
             grouped = stage.tile([P, width, PACK], BF16, name="h_grouped" + name, offset=offset, align_bytes=64)
             signs = sign[:, b, :].rearrange("p (m u e) -> p m u e", m=1, u=2)
-            nc.vector.tensor_tensor(
-                grouped[:].rearrange("p m (u e) -> p m u e", u=2),
-                pairs[:].rearrange("p u m e -> p m u e"),
-                signs.to_broadcast([P, width, 2, 2]),
-                ALU.mult,
-            )
+            run = width // steps
+            for step in range(steps):
+                cols = slice(run * step, run * (step + 1))
+                pairs = keep.tile([P, 2, run, 2], BF16, name="pairs%s_%d" % (name, step), align_bytes=64)
+                for t in range(PACK):
+                    nc.scalar.activation(
+                        pairs[:, t // 2, :, t % 2],
+                        dots[t][:, cols],
+                        ACT.Square,
+                        bias=shift[:, b, t : t + 1],
+                        scale=root[:, b, t : t + 1],
+                    )
+                nc.vector.tensor_tensor(
+                    grouped[:, cols, :].rearrange("p m (u e) -> p m u e", u=2),
+                    pairs[:].rearrange("p u m e -> p m u e"),
+                    signs.to_broadcast([P, run, 2, 2]),
+                    ALU.mult,
+                )
             return grouped
 
         def sum_pass(dst, b, c, codes, scale, start, stop):
@@ -309,12 +312,11 @@ def tile_list_kernl_poly2_mix_res_kernel(
             nc.sync.dma_start(out_rows[:, rows, cols], result[:])
 
         tiles = N // P
-        free = CODES + 4 * HALF
         dots00 = dots_of_part(0, 0, 1, 0)
         grouped00 = weighted_on_vector(dots00, 0, X_AT[1, 1])
         dots01 = dots_of_part(0, 1, 2, 4)
         dots10 = dots_of_part(1, 0, 1, 0)
-        grouped01 = weighted_on_vector(dots01, 1, X_AT[1, 1] + GROUP)
+        grouped01 = weighted_on_scalar(dots01, 1, "01", X_AT[1, 1] + GROUP)
         codes00, scale00 = quantize(grouped00, "h00")
         codes01, scale01 = quantize(grouped01, "h01", CODES)
         dots11 = [dots_of_quarter(g, bank_no) for g, bank_no in enumerate((4, 0))]
@@ -323,9 +325,10 @@ def tile_list_kernl_poly2_mix_res_kernel(
         for pair in range(2):
             for b, (codes, scale) in enumerate(((codes00, scale00), (codes01, scale01))):
                 for i in range(2):
-                    sum_pass(sums0[pair][:, i, :], b, 2 * pair + i, codes[:], scale[:], b == 0 and i == 0, b == 1 and i == 1)
+                    start, stop = b == 0 and i == 0, b == 1 and i == 1
+                    sum_pass(sums0[pair][:, i, :], b, 2 * pair + i, codes[:], scale[:], start, stop)
 
-        grouped10 = weighted_on_scalar(dots10, 0, "10", free)
+        grouped10 = weighted_on_scalar(dots10, 0, "10", THIRD_PART, 2)
         finish(sums0[0][:], res_first[0][:], "0_0", slice(0, 2), slice(0, HALF))
         codes10, scale10 = quantize(grouped10, "h10", CODES)
         sums1 = [psum.tile([P, tiles, P], F32, name="sum1_%d" % g, tag="bank%d" % (2 + g)) for g in range(2)]

@@ -20,6 +20,7 @@ P = 128
 PACK = 4
 PASS = P * PACK
 HALF = M // 2
+TILES = N // P
 LIST_COLS = PASS // 16
 PAIR = 2
 RUN = 4
@@ -30,12 +31,12 @@ WARM_UP = (HALF, HALF, HALF, HALF, P)
 
 SLOT = PACK * HALF * 4
 GROUP = PACK * HALF * 2
-X_AT = {(0, 0): 0, (0, 1): SLOT, (1, 0): 2 * SLOT + GROUP, (1, 1): 3 * SLOT + GROUP + N}
+X_AT = {(0, 0): 0, (0, 1): SLOT, (1, 0): 2 * SLOT, (1, 1): 3 * SLOT + N}
 AL_STAGED = X_AT[1, 1] - N
-STAGED = 6 * SLOT
+STAGED = 5 * SLOT
 CODES = STAGED + J
-THIRD_PART = CODES + 4 * HALF
-LATE = 8 * SLOT
+LATE = 6 * SLOT
+LAST_PART = SLOT // 2
 
 
 def tile_list_kernl_poly2_mix_res_kernel(
@@ -47,38 +48,43 @@ def tile_list_kernl_poly2_mix_res_kernel(
         stage = ctx.enter_context(tc.tile_pool(name="stage", bufs=1))
         psum = ctx.enter_context(tc.psum_pool(name="psum", bufs=1))
 
-        offsets = keep.tile([P, J // 16], U16, name="offsets")
+        def kept(name, shape, dtype):
+            return keep.tile([P] + shape, dtype, name=name, align_bytes=64)
 
-        scale_rows = keep.tile([P, T], U8, name="scale_rows", align_bytes=64)
+        def laid(name, shape, dtype, offset):
+            return stage.tile([P] + shape, dtype, name=name, offset=offset, align_bytes=64)
+
+        def bank(name, shape, number):
+            return psum.tile([P] + shape, F32, name=name, tag="bank%d" % number)
+
+        offsets = keep.tile([P, J // 16], U16, name="offsets")
+        scale_rows = kept("scale_rows", [T], U8)
         nc.sync.dma_start(scale_rows[0:32, :].bitcast(I32), tab_scales.rearrange("a q t -> q a t").bitcast(I32))
         nc.sync.dma_start(offsets[:], offs)
         nc.vector.memset(scale_rows[64:128, :].bitcast(I32), 0)
         nc.vector.memset(scale_rows[32:64, :].bitcast(I32), 0)
 
-        cw_sb = keep.tile([P, 2, BLOCK], F32, name="cw_sb")
+        cw_sb = kept("cw_sb", [2, BLOCK], F32)
         nc.scalar.dma_start(cw_sb[:, :, 0:PACK], cw.rearrange("(b p t) -> p b t", b=2, t=PACK))
-        cb_sb = keep.tile([P, 2, BLOCK], F32, name="cb_sb")
+        cb_sb = kept("cb_sb", [2, BLOCK], F32)
         nc.scalar.dma_start(cb_sb[:, :, 0:PACK], cb.rearrange("(b p t) -> p b t", b=2, t=PACK))
 
-        table = keep.tile([P, T], I32, name="table", align_bytes=64)
+        table = kept("table", [T], I32)
         nc.sync.dma_start(table[:], tab_words[0].rearrange("p t f -> p (t f)").bitcast(I32))
 
         x_rows = x.rearrange("(a p t) m -> a p t m", a=2, t=PACK)
         x_raw = {}
 
         def load_x(half, a):
-            raw = stage.tile(
-                [P, PACK, HALF], F32, name="x_raw%d_%d" % (half, a), offset=X_AT[half, a], align_bytes=64
-            )
-            nc.sync.dma_start(raw[:], x_rows[a][:, :, HALF * half : HALF * (half + 1)])
-            x_raw[half, a] = raw
+            x_raw[half, a] = laid("x_raw%d_%d" % (half, a), [PACK, HALF], F32, X_AT[half, a])
+            nc.sync.dma_start(x_raw[half, a][:], x_rows[a][:, :, HALF * half : HALF * (half + 1)])
 
         load_x(0, 0)
         load_x(0, 1)
 
-        placed = keep.tile([P, 2, J], U8, name="placed", align_bytes=64)
+        placed = kept("placed", [2, J], U8)
         nc.gpsimd.memset(placed[:].rearrange("p a n -> p (a n)").bitcast(I32), 0)
-        al_placed = keep.tile([P, 2, N], U8, name="al_placed", align_bytes=64)
+        al_placed = kept("al_placed", [2, N], U8)
         nc.gpsimd.memset(al_placed[:].rearrange("p a n -> p (a n)").bitcast(I32), 0)
 
         def small(name, dtype=F32):
@@ -101,8 +107,8 @@ def tile_list_kernl_poly2_mix_res_kernel(
         shift = small("shift")
         nc.gpsimd.tensor_tensor(shift[:], root[:], cb_sb[:, :, 0:PACK], ALU.mult)
 
-        picked_scales = stage.tile([P, J], U8, name="picked_scales", offset=AL_STAGED - N // 2, align_bytes=64)
-        staged = stage.tile([P, J], U8, name="staged", offset=STAGED, align_bytes=64)
+        picked_scales = laid("picked_scales", [J], U8, AL_STAGED - N // 2)
+        staged = laid("staged", [J], U8, STAGED)
         nc.vector.tensor_copy(picked_scales[:], scale_rows[:].indirect(offsets[:]))
         nc.vector.tensor_copy(
             staged[:].rearrange("p (b t m) -> p b t m", b=2, t=PACK),
@@ -119,33 +125,25 @@ def tile_list_kernl_poly2_mix_res_kernel(
         place_rows(placed, staged)
         load_x(1, 0)
         load_x(1, 1)
-        al_staged = stage.tile([P, N], U8, name="al_staged", offset=AL_STAGED, align_bytes=64)
+        al_staged = laid("al_staged", [N], U8, AL_STAGED)
         for a, scales in enumerate((al8_scales, al4_scales)):
             nc.sync.dma_start(al_staged[a:32:2, :].bitcast(I32), scales[0].bitcast(I32))
 
         def as_words(grouped):
-            return grouped[:].rearrange("p (c i) t -> p c t i", i=PAIR)
+            return grouped.rearrange("p (c i) t -> p c t i", i=PAIR)
 
         def as_rows(rows):
-            return rows[:].rearrange("p t (c i) -> p c t i", i=PAIR)
+            return rows.rearrange("p t (c i) -> p c t i", i=PAIR)
 
         def quantize(grouped, name, offset=None):
             width = grouped.shape[1]
             if offset is None:
-                codes = keep.tile([P, width], U32, name=name + "_codes", align_bytes=64)
+                codes = kept(name + "_codes", [width], U32)
             else:
-                codes = stage.tile([P, width], U32, name=name + "_codes", offset=offset, align_bytes=64)
-            scale = keep.tile([P, width], U8, name=name + "_scale", align_bytes=64)
-            nc.vector.quantize_mx(
-                out=codes[:].bitcast(E4M3), scales=scale[:], in_=grouped[:].rearrange("p m t -> p (m t)")
-            )
+                codes = laid(name + "_codes", [width], U32, offset)
+            scale = kept(name + "_scale", [width], U8)
+            nc.vector.quantize_mx(out=codes[:].bitcast(E4M3), scales=scale[:], in_=grouped.rearrange("p m t -> p (m t)"))
             return codes, scale
-
-        def interleave_on_scalar(half, a):
-            name = "x_grouped%d_%d" % (half, a)
-            grouped = keep.tile([P, HALF, PACK], BF16, name=name, tag=name, align_bytes=64)
-            nc.scalar.activation(as_words(grouped), as_rows(x_raw[half, a]), ACT.Copy)
-            return grouped
 
         def part_words(words, parted):
             nc.vector.tensor_copy(
@@ -153,17 +151,17 @@ def tile_list_kernl_poly2_mix_res_kernel(
                 words[:].bitcast(U16).rearrange("p (c i t a) -> p a c t i", i=RUN, t=PACK, a=2),
             )
 
-        idle = keep.tile([P, HALF, PACK], BF16, name="idle", align_bytes=64)
+        idle = kept("idle", [HALF, PACK], BF16)
         nc.vector.memset(idle[:].rearrange("p m t -> p (m t)").bitcast(I32), 0)
-        idle_codes, idle_scale = quantize(idle, "idle")
+        idle_codes, idle_scale = quantize(idle[:], "idle")
 
-        picked = [keep.tile([P, PASS], U32, name="picked%d" % b, align_bytes=64) for b in range(2)]
+        picked = [kept("picked%d" % b, [PASS], U32) for b in range(2)]
         for b in range(2):
             nc.vector.tensor_copy(
                 picked[b][:], table[:].bitcast(U32).indirect(offsets[:, LIST_COLS * b : LIST_COLS * (b + 1)])
             )
 
-        warm = psum.tile([P, HALF], F32, name="warm", tag="bank7")
+        warm = bank("warm", [HALF], 7)
         for i, width in enumerate(WARM_UP):
             nc.tensor.matmul_mx(
                 out=warm[:, 0:width],
@@ -175,44 +173,44 @@ def tile_list_kernl_poly2_mix_res_kernel(
                 stop=i == len(WARM_UP) - 1,
             )
 
-        x_mx = {}
-        centres = [keep.tile([P, 2, 2 * PASS], U8, name="centres0", align_bytes=64)]
+        centres = [kept("centres0", [2, 2 * PASS], U8)]
         part_words(picked[0], centres[0])
-        first_half = [interleave_on_scalar(0, a) for a in range(2)]
+        first = [kept("x_grouped0_%d" % a, [HALF, PACK], BF16) for a in range(2)]
         for a in range(2):
-            x_mx[0, a] = quantize(first_half[a], "x0_%d" % a)
-        centres.append(keep.tile([P, 2, 2 * PASS], U8, name="centres1", tag="x_grouped0_0", align_bytes=64))
+            nc.scalar.activation(as_words(first[a][:]), as_rows(x_raw[0, a][:]), ACT.Copy)
+        x_first = [quantize(first[0][:], "x0_0")]
+        centres.append(laid("centres1", [2, 2 * PASS], U8, X_AT[0, 0]))
         part_words(picked[1], centres[1])
-        third = stage.tile([P, HALF, PACK], BF16, name="x_grouped1_0", offset=LATE, align_bytes=64)
-        nc.vector.tensor_copy(as_words(third), as_rows(x_raw[1, 0]))
-        x_mx[1, 0] = quantize(third, "x1_0")
-        last = stage.tile([P, HALF, PACK], BF16, name="x_grouped1_1", offset=LATE + GROUP, align_bytes=64)
-        last_codes = keep.tile([P, HALF], U32, name="x1_1_codes", align_bytes=64)
-        last_scale = keep.tile([P, HALF], U8, name="x1_1_scale", align_bytes=64)
-        for g in (1, 0):
-            pairs = slice(g * P // PAIR, (g + 1) * P // PAIR)
-            nc.vector.tensor_copy(as_words(last)[:, pairs], as_rows(x_raw[1, 1])[:, pairs])
-        for g in (1, 0):
-            cols = slice(P * g, P * (g + 1))
+        x_first.append(quantize(first[1][:], "x0_1"))
+
+        third = laid("x_grouped1_0", [HALF, PACK], BF16, LATE)
+        nc.vector.tensor_copy(as_words(third[:]), as_rows(x_raw[1, 0][:]))
+        third_mx = quantize(third[:], "x1_0")
+        last = laid("x_grouped1_1", [HALF, PACK], BF16, LATE + GROUP)
+        quarters = [slice(P * g, P * (g + 1)) for g in range(2)]
+        for cols in reversed(quarters):
+            nc.vector.tensor_copy(as_words(last[:, cols, :]), as_rows(x_raw[1, 1][:, :, cols]))
+        last_codes = kept("x1_1_codes", [HALF], U32)
+        last_scale = kept("x1_1_scale", [HALF], U8)
+        for cols in reversed(quarters):
             nc.vector.quantize_mx(
                 out=last_codes[:, cols].bitcast(E4M3),
                 scales=last_scale[:, cols],
                 in_=last[:, cols, :].rearrange("p m t -> p (m t)"),
             )
-        x_mx[1, 1] = last_codes, last_scale
 
         res_rows = res.rearrange("(c p) m -> p c m", p=P)
         res_first = []
         for pair in range(2):
-            rows = stage.tile([P, 2, HALF], F32, name="res0_%d" % pair, offset=pair * SLOT // 2, align_bytes=64)
+            rows = laid("res0_%d" % pair, [2, HALF], F32, SLOT // 2 + pair * SLOT)
             nc.sync.dma_start(rows[:], res_rows[:, 2 * pair : 2 * pair + 2, 0:HALF])
             res_first.append(rows)
-        al8 = stage.tile([P, N], I32, name="al8", offset=SLOT, align_bytes=64)
+        al8 = laid("al8", [N], I32, SLOT)
         nc.sync.dma_start(al8[:], al8_words[0].rearrange("p n f -> p (n f)").bitcast(I32))
-        al4 = stage.tile([P, 2 * N], U8, name="al4", offset=SLOT + 4 * N, align_bytes=64)
+        al4 = laid("al4", [2 * N], U8, X_AT[1, 0])
         nc.sync.dma_start(al4[:].bitcast(I32), al4_words[0].bitcast(I32))
         place_rows(al_placed, al_staged)
-        res_second = stage.tile([P, N // P, HALF], F32, name="res1", offset=LATE + GROUP, align_bytes=64)
+        res_second = laid("res1", [TILES, HALF], F32, LATE + GROUP)
         nc.sync.dma_start(res_second[:], res_rows[:, :, HALF:M])
         out_rows = out.rearrange("(c p) m -> p c m", p=P)
 
@@ -228,70 +226,7 @@ def tile_list_kernl_poly2_mix_res_kernel(
                 stop=stop,
             )
 
-        def dots_of_part(half, b, width, first_bank):
-            banks = [
-                psum.tile([P, width, HALF], F32, name="dot%d_%d_%d" % (half, b, u), tag="bank%d" % (first_bank + u))
-                for u in range(PACK // width)
-            ]
-            if b == 0:
-                order = [(u, a) for a in range(2) for u in range(len(banks))]
-            else:
-                order = [(u, a) for u in range(len(banks)) for a in (1, 0)]
-            opening = order[0][1]
-            for u, a in order:
-                codes, scale = x_mx[half, a]
-                for i in range(width):
-                    start = a == opening and i == 0
-                    stop = a != opening and i == width - 1
-                    dot_pass(banks[u][:, i, :], b, width * u + i, a, codes[:], scale[:], start, stop)
-            return [banks[t // width][:, t % width, :] for t in range(PACK)]
-
-        def dots_of_quarter(g, bank_no):
-            bank = psum.tile([P, PACK, P], F32, name="dotq%d" % g, tag="bank%d" % bank_no)
-            cols = slice(P * g, P * (g + 1))
-            for a in (1, 0):
-                codes, scale = x_mx[1, a]
-                for t in range(PACK):
-                    start, stop = a == 1 and t == 0, a == 0 and t == PACK - 1
-                    dot_pass(bank[:, t, :], 1, t, a, codes[:, cols], scale[:, cols], start, stop)
-            return [bank[:, t, :] for t in range(PACK)]
-
-        def weighted_on_vector(dots, b, offset):
-            squares = keep.tile([P, PACK, HALF], F32, name="squares%d" % b, align_bytes=64)
-            for t in range(PACK):
-                nc.scalar.activation(squares[:, t, :], dots[t], ACT.Square, bias=cb_sb[:, b, t : t + 1])
-            grouped = stage.tile([P, HALF, PACK], BF16, name="h_grouped0%d" % b, offset=offset, align_bytes=64)
-            weights = cw_sb[:, b, 0:PACK].rearrange("p (c t i) -> p c t i", c=1, i=1)
-            nc.vector.tensor_tensor(
-                as_words(grouped), as_rows(squares), weights.to_broadcast([P, HALF // PAIR, PACK, PAIR]), ALU.mult
-            )
-            return grouped
-
-        def weighted_on_scalar(dots, b, name, offset, steps=1):
-            width = dots[0].shape[1]
-            grouped = stage.tile([P, width, PACK], BF16, name="h_grouped" + name, offset=offset, align_bytes=64)
-            signs = sign[:, b, :].rearrange("p (m u e) -> p m u e", m=1, u=2)
-            run = width // steps
-            for step in range(steps):
-                cols = slice(run * step, run * (step + 1))
-                pairs = keep.tile([P, 2, run, 2], BF16, name="pairs%s_%d" % (name, step), align_bytes=64)
-                for t in range(PACK):
-                    nc.scalar.activation(
-                        pairs[:, t // 2, :, t % 2],
-                        dots[t][:, cols],
-                        ACT.Square,
-                        bias=shift[:, b, t : t + 1],
-                        scale=root[:, b, t : t + 1],
-                    )
-                nc.vector.tensor_tensor(
-                    grouped[:, cols, :].rearrange("p m (u e) -> p m u e", u=2),
-                    pairs[:].rearrange("p u m e -> p m u e"),
-                    signs.to_broadcast([P, run, 2, 2]),
-                    ALU.mult,
-                )
-            return grouped
-
-        def sum_pass(dst, b, c, codes, scale, start, stop):
+        def sum_pass(dst, b, c, mx, start, stop):
             if b == 0:
                 weights = al8[:, P * c : P * (c + 1)].bitcast(E4M3)
             else:
@@ -300,49 +235,112 @@ def tile_list_kernl_poly2_mix_res_kernel(
                 out=dst,
                 lhsT=weights,
                 lhsT_scale=al_placed[:, b, P * c : P * (c + 1)],
-                rhs=codes.bitcast(E4M3),
-                rhs_scale=scale,
+                rhs=mx[0][:].bitcast(E4M3),
+                rhs_scale=mx[1][:],
                 start=start,
                 stop=stop,
             )
 
-        def finish(sums, residual, name, rows, cols):
-            result = keep.tile([P, rows.stop - rows.start, cols.stop - cols.start], F32, name="result" + name)
+        def square(dots, b, name):
+            width = dots[0].shape[1]
+            pairs = kept("pairs" + name, [2, width, 2], BF16)
+            for t in range(PACK):
+                nc.scalar.activation(
+                    pairs[:, t // 2, :, t % 2],
+                    dots[t],
+                    ACT.Square,
+                    bias=shift[:, b, t : t + 1],
+                    scale=root[:, b, t : t + 1],
+                )
+            return pairs
+
+        def weave(pairs, b, grouped):
+            width = pairs.shape[2]
+            signs = sign[:, b, :].rearrange("p (m u e) -> p m u e", m=1, u=2)
+            nc.vector.tensor_tensor(
+                grouped.rearrange("p m (u e) -> p m u e", u=2),
+                pairs[:].rearrange("p u m e -> p m u e"),
+                signs.to_broadcast([P, width, 2, 2]),
+                ALU.mult,
+            )
+            return grouped
+
+        def finish(sums, residual, name, rows, cols, offset=None):
+            shape = [rows.stop - rows.start, cols.stop - cols.start]
+            if offset is None:
+                result = kept("result" + name, shape, F32)
+            else:
+                result = laid("result" + name, shape, F32, offset)
             nc.vector.tensor_tensor(result[:], sums, residual, ALU.add)
             nc.sync.dma_start(out_rows[:, rows, cols], result[:])
 
-        tiles = N // P
-        dots00 = dots_of_part(0, 0, 1, 0)
-        grouped00 = weighted_on_vector(dots00, 0, X_AT[1, 1])
-        dots01 = dots_of_part(0, 1, 2, 4)
-        dots10 = dots_of_part(1, 0, 1, 0)
-        grouped01 = weighted_on_scalar(dots01, 1, "01", X_AT[1, 1] + GROUP)
-        codes00, scale00 = quantize(grouped00, "h00")
-        codes01, scale01 = quantize(grouped01, "h01", CODES)
-        dots11 = [dots_of_quarter(g, bank_no) for g, bank_no in enumerate((4, 0))]
+        def weigh(dots, cols, name, grouped):
+            squares = kept("squares" + name, [PACK, cols.stop - cols.start], F32)
+            for t in range(PACK):
+                nc.scalar.activation(squares[:, t, :], dots[t][:, cols], ACT.Square, bias=cb_sb[:, 0, t : t + 1])
+            weights = cw_sb[:, 0, 0:PACK].rearrange("p (c t i) -> p c t i", c=1, i=1)
+            shape = [P, (cols.stop - cols.start) // PAIR, PACK, PAIR]
+            nc.vector.tensor_tensor(as_words(grouped), as_rows(squares[:]), weights.to_broadcast(shape), ALU.mult)
 
-        sums0 = [psum.tile([P, 2, HALF], F32, name="sum0_%d" % pair, tag="bank%d" % (6 + pair)) for pair in range(2)]
-        for pair in range(2):
-            for b, (codes, scale) in enumerate(((codes00, scale00), (codes01, scale01))):
+        def dots_by_tile(name, mx):
+            tiles = [bank("dot%s_%d" % (name, t), [HALF], t) for t in range(PACK)]
+            for a in range(2):
+                for t in range(PACK):
+                    dot_pass(tiles[t][:], 0, t, a, mx[a][0], mx[a][1], a == 0, a == 1)
+            return [tile[:] for tile in tiles]
+
+        dots00 = dots_by_tile("00", [(codes[:], scale[:]) for codes, scale in x_first])
+        grouped00 = laid("h_grouped00", [HALF, PACK], BF16, X_AT[1, 1])
+        weigh(dots00, slice(0, HALF), "00", grouped00[:])
+        dots01 = [bank("dot01_%d" % u, [2, HALF], 4 + u) for u in range(2)]
+        for u in range(2):
+            for a in (1, 0):
                 for i in range(2):
-                    start, stop = b == 0 and i == 0, b == 1 and i == 1
-                    sum_pass(sums0[pair][:, i, :], b, 2 * pair + i, codes[:], scale[:], start, stop)
+                    start, stop = a == 1 and i == 0, a == 0 and i == 1
+                    dot_pass(dots01[u][:, i, :], 1, 2 * u + i, a, x_first[a][0][:], x_first[a][1][:], start, stop)
+        x_second = [(third_mx[0][:], third_mx[1][:]), (last_codes[:], last_scale[:])]
+        dots10 = dots_by_tile("10", x_second)
+        pairs01 = square([dots01[t // 2][:, t % 2, :] for t in range(PACK)], 1, "01")
+        grouped01 = weave(pairs01, 1, laid("h_grouped01", [HALF, PACK], BF16, X_AT[1, 1] + GROUP)[:])
+        h00 = quantize(grouped00[:], "h00")
+        h01 = quantize(grouped01, "h01", CODES)
+        dots11 = []
+        for g, number in enumerate((4, 0)):
+            tile = bank("dot11_%d" % g, [PACK, P], number)
+            for a in (1, 0):
+                codes, scale = x_second[a]
+                for t in range(PACK):
+                    start, stop = a == 1 and t == 0, a == 0 and t == PACK - 1
+                    dot_pass(tile[:, t, :], 1, t, a, codes[:, quarters[g]], scale[:, quarters[g]], start, stop)
+            dots11.append([tile[:, t, :] for t in range(PACK)])
 
-        grouped10 = weighted_on_scalar(dots10, 0, "10", THIRD_PART, 2)
-        finish(sums0[0][:], res_first[0][:], "0_0", slice(0, 2), slice(0, HALF))
-        codes10, scale10 = quantize(grouped10, "h10", CODES)
-        sums1 = [psum.tile([P, tiles, P], F32, name="sum1_%d" % g, tag="bank%d" % (2 + g)) for g in range(2)]
-        for g in range(2):
-            cols = slice(P * g, P * (g + 1))
-            for c in range(tiles):
-                sum_pass(sums1[g][:, c, :], 0, c, codes10[:, cols], scale10[:, cols], c == 0, False)
-        grouped11 = [weighted_on_scalar(dots11[g], 1, "11_%d" % g, g * GROUP // 2) for g in range(2)]
-        for g in range(2):
-            codes11, scale11 = quantize(grouped11[g], "h11_%d" % g)
-            for c in range(tiles):
-                sum_pass(sums1[g][:, c, :], 1, c, codes11[:], scale11[:], False, c == tiles - 1)
-        finish(sums0[1][:], res_first[1][:], "0_1", slice(2, 4), slice(0, HALF))
-        finish(sums1[0][:], res_second[:, :, 0:P], "1_0", slice(0, tiles), slice(HALF, HALF + P))
+        sums0 = [bank("sum0_%d" % pair, [2, HALF], 6 + pair) for pair in range(2)]
         for pair in range(2):
-            rows = slice(2 * pair, 2 * pair + 2)
-            finish(sums1[1][:, rows, :], res_second[:, rows, P:HALF], "1_1_%d" % pair, rows, slice(HALF + P, M))
+            for b, mx in enumerate((h00, h01)):
+                for i in range(2):
+                    sum_pass(sums0[pair][:, i, :], b, 2 * pair + i, mx, b == 0 and i == 0, b == 1 and i == 1)
+
+        grouped10 = kept("h_grouped10", [HALF, PACK], BF16)
+        for g, cols in enumerate(quarters):
+            weave(square([tile[:, cols] for tile in dots10], 0, "10_%d" % g), 0, grouped10[:, cols, :])
+        finish(sums0[0][:], res_first[0][:], "0_0", slice(0, 2), slice(0, HALF))
+        h10 = quantize(grouped10[:], "h10", CODES)
+        sums1 = [bank("sum1_%d" % pair, [2, HALF], 2 + pair) for pair in range(2)]
+        for c in range(TILES):
+            sum_pass(sums1[c // 2][:, c % 2, :], 0, c, h10, c % 2 == 0, False)
+        grouped11 = []
+        for g in range(2):
+            name = "11_%d" % g
+            tile = laid("h_grouped" + name, [P, PACK], BF16, LAST_PART + g * GROUP // 2)
+            grouped11.append(weave(square(dots11[g], 1, name), 1, tile[:]))
+        for g, cols in enumerate(quarters):
+            h11 = quantize(grouped11[g], "h11_%d" % g)
+            for c in range(TILES):
+                sum_pass(sums1[c // 2][:, c % 2, cols], 1, c, h11, False, g == 1 and c % 2 == 1)
+        for i in range(2):
+            rows = slice(2 + i, 3 + i)
+            held = LAST_PART + (i - 1) * GROUP // 2 + GROUP // 4
+            finish(sums0[1][:, i : i + 1, :], res_first[1][:, i : i + 1, :], "0_1_%d" % i, rows, slice(0, HALF), held)
+        for c in range(TILES):
+            rows = slice(c, c + 1)
+            finish(sums1[c // 2][:, c % 2 : c % 2 + 1, :], res_second[:, rows, :], "1_%d" % c, rows, slice(HALF, M))

@@ -1,6 +1,7 @@
 from contextlib import ExitStack
 
 import concourse.mybir as mybir
+from concourse.masks import make_identity
 
 K, M, N, J, T = 1024, 512, 512, 1024, 4096
 FLOPS = 2 * K * J * M + 2 * J * N * M
@@ -24,7 +25,6 @@ TILES = N // P
 LIST_COLS = PASS // 16
 PAIR = 2
 RUN = 4
-BLOCK = 8
 TINY = 1e-36
 
 WARM_UP = (HALF, HALF, HALF, HALF, P)
@@ -37,6 +37,9 @@ STAGED = 5 * SLOT
 CODES = STAGED + J
 LATE = 6 * SLOT
 LAST_PART = SLOT // 2
+FIRST = 8 * SLOT
+ROWS_AT = P - 4
+SCALES_AT = P - 32
 
 
 def tile_list_kernl_poly2_mix_res_kernel(
@@ -59,15 +62,18 @@ def tile_list_kernl_poly2_mix_res_kernel(
 
         offsets = keep.tile([P, J // 16], U16, name="offsets")
         scale_rows = kept("scale_rows", [T], U8)
-        nc.sync.dma_start(scale_rows[0:32, :].bitcast(I32), tab_scales.rearrange("a q t -> q a t").bitcast(I32))
+        nc.sync.dma_start(scale_rows[SCALES_AT:P, :].bitcast(I32), tab_scales.rearrange("a q t -> q a t").bitcast(I32))
         nc.sync.dma_start(offsets[:], offs)
-        nc.vector.memset(scale_rows[64:128, :].bitcast(I32), 0)
-        nc.vector.memset(scale_rows[32:64, :].bitcast(I32), 0)
+        nc.vector.memset(scale_rows[0:SCALES_AT, :].bitcast(I32), 0)
 
-        cw_sb = kept("cw_sb", [2, BLOCK], F32)
-        nc.scalar.dma_start(cw_sb[:, :, 0:PACK], cw.rearrange("(b p t) -> p b t", b=2, t=PACK))
-        cb_sb = kept("cb_sb", [2, BLOCK], F32)
-        nc.scalar.dma_start(cb_sb[:, :, 0:PACK], cb.rearrange("(b p t) -> p b t", b=2, t=PACK))
+        placed = kept("placed", [2, J], U8)
+        nc.gpsimd.memset(placed[:].rearrange("p a n -> p (a n)").bitcast(I32), 0)
+        identity = kept("identity", [P], F32)
+        make_identity(nc, identity[:])
+        vector_rows = kept("vector_rows", [PASS], F32)
+        nc.scalar.dma_start(vector_rows[ROWS_AT : ROWS_AT + 2, :], cw.rearrange("(b c) -> b c", b=2))
+        nc.scalar.dma_start(vector_rows[ROWS_AT + 2 : ROWS_AT + 4, :], cb.rearrange("(b c) -> b c", b=2))
+        nc.vector.memset(vector_rows[0:ROWS_AT, :].bitcast(I32), 0)
 
         table = kept("table", [T], I32)
         nc.sync.dma_start(table[:], tab_words[0].rearrange("p t f -> p (t f)").bitcast(I32))
@@ -82,20 +88,25 @@ def tile_list_kernl_poly2_mix_res_kernel(
         load_x(0, 0)
         load_x(0, 1)
 
-        placed = kept("placed", [2, J], U8)
-        nc.gpsimd.memset(placed[:].rearrange("p a n -> p (a n)").bitcast(I32), 0)
         al_placed = kept("al_placed", [2, N], U8)
         nc.gpsimd.memset(al_placed[:].rearrange("p a n -> p (a n)").bitcast(I32), 0)
 
         def small(name, dtype=F32):
             return keep.tile([P, 2, PACK], dtype, name=name)
 
-        guess = small("guess")
-        nc.scalar.activation(guess[:], cw_sb[:, :, 0:PACK], ACT.Abs_reciprocal_sqrt, bias=TINY)
-        size = small("size")
-        nc.scalar.activation(size[:], cw_sb[:, :, 0:PACK], ACT.Abs)
+        turned = bank("turned", [PACK, P], 7)
+        for t in range(PACK):
+            nc.tensor.transpose(turned[:, t, :], vector_rows[:, t:PASS:PACK], identity[:])
+        by_row = turned[:, :, ROWS_AT : ROWS_AT + 4].rearrange("p t r -> p r t")
+        guess = laid("guess", [2, PACK], F32, FIRST + GROUP)
+        nc.scalar.activation(guess[:], by_row[:, 0:2, :], ACT.Abs_reciprocal_sqrt, bias=TINY)
+        vectors = kept("vectors", [4, PACK], F32)
+        nc.scalar.copy(vectors[:], by_row)
+        cw_sb, cb_sb = vectors[:, 0:2, :], vectors[:, 2:4, :]
         sign = small("sign", BF16)
-        nc.scalar.activation(sign[:], cw_sb[:, :, 0:PACK], ACT.Sign)
+        nc.scalar.activation(sign[:], by_row[:, 0:2, :], ACT.Sign)
+        size = laid("size", [2, PACK], F32, FIRST)
+        nc.scalar.activation(size[:], by_row[:, 0:2, :], ACT.Abs)
         rough = small("rough")
         nc.gpsimd.tensor_tensor(rough[:], size[:], guess[:], ALU.mult)
         near_one = small("near_one")
@@ -115,14 +126,14 @@ def tile_list_kernl_poly2_mix_res_kernel(
             picked_scales[:].rearrange("p (b m t) -> p b t m", b=2, t=PACK),
         )
 
-        def place_rows(dst, src):
+        def place_rows(dst, src, first_row):
             for quad in (0, 2, 1, 3):
                 nc.sync.dma_start(
                     dst[32 * quad : 32 * quad + 4].rearrange("p a n -> p (a n)").bitcast(I32),
-                    src[8 * quad : 8 * quad + 8, :].bitcast(I32),
+                    src[first_row + 8 * quad : first_row + 8 * quad + 8, :].bitcast(I32),
                 )
 
-        place_rows(placed, staged)
+        place_rows(placed, staged, SCALES_AT)
         load_x(1, 0)
         load_x(1, 1)
         al_staged = laid("al_staged", [N], U8, AL_STAGED)
@@ -175,7 +186,7 @@ def tile_list_kernl_poly2_mix_res_kernel(
 
         centres = [kept("centres0", [2, 2 * PASS], U8)]
         part_words(picked[0], centres[0])
-        first = [kept("x_grouped0_%d" % a, [HALF, PACK], BF16) for a in range(2)]
+        first = [laid("x_grouped0_%d" % a, [HALF, PACK], BF16, FIRST + a * GROUP) for a in range(2)]
         for a in range(2):
             nc.scalar.activation(as_words(first[a][:]), as_rows(x_raw[0, a][:]), ACT.Copy)
         x_first = [quantize(first[0][:], "x0_0")]
@@ -183,7 +194,7 @@ def tile_list_kernl_poly2_mix_res_kernel(
         part_words(picked[1], centres[1])
         x_first.append(quantize(first[1][:], "x0_1"))
 
-        third = laid("x_grouped1_0", [HALF, PACK], BF16, LATE)
+        third = laid("x_grouped1_0", [HALF, PACK], BF16, FIRST + GROUP)
         nc.vector.tensor_copy(as_words(third[:]), as_rows(x_raw[1, 0][:]))
         third_mx = quantize(third[:], "x1_0")
         last = laid("x_grouped1_1", [HALF, PACK], BF16, LATE + GROUP)
@@ -209,7 +220,7 @@ def tile_list_kernl_poly2_mix_res_kernel(
         nc.sync.dma_start(al8[:], al8_words[0].rearrange("p n f -> p (n f)").bitcast(I32))
         al4 = laid("al4", [2 * N], U8, X_AT[1, 0])
         nc.sync.dma_start(al4[:].bitcast(I32), al4_words[0].bitcast(I32))
-        place_rows(al_placed, al_staged)
+        place_rows(al_placed, al_staged, 0)
         res_second = laid("res1", [TILES, HALF], F32, LATE + GROUP)
         nc.sync.dma_start(res_second[:], res_rows[:, :, HALF:M])
         out_rows = out.rearrange("(c p) m -> p c m", p=P)

@@ -187,28 +187,35 @@ def tile_list_kernl_poly2_mix_res_kernel(
         centres = [kept("centres0", [2, 2 * PASS], U8)]
         part_words(picked[0], centres[0])
         first = [laid("x_grouped0_%d" % a, [HALF, PACK], BF16, FIRST + a * GROUP) for a in range(2)]
-        for a in range(2):
-            nc.scalar.activation(as_words(first[a][:]), as_rows(x_raw[0, a][:]), ACT.Copy)
+        quarters = [slice(P * g, P * (g + 1)) for g in range(2)]
+        nc.scalar.activation(as_words(first[0][:]), as_rows(x_raw[0, 0][:]), ACT.Copy)
+        for cols in quarters:
+            nc.scalar.activation(as_words(first[1][:, cols, :]), as_rows(x_raw[0, 1][:, :, cols]), ACT.Copy)
         x_first = [quantize(first[0][:], "x0_0")]
-        centres.append(laid("centres1", [2, 2 * PASS], U8, X_AT[0, 0]))
+        x_first.append((kept("x0_1_codes", [HALF], U32), kept("x0_1_scale", [HALF], U8)))
+
+        def quantize_quarter(grouped, mx, cols):
+            nc.vector.quantize_mx(
+                out=mx[0][:, cols].bitcast(E4M3),
+                scales=mx[1][:, cols],
+                in_=grouped[:, cols, :].rearrange("p m t -> p (m t)"),
+            )
+
+        quantize_quarter(first[1], x_first[1], quarters[0])
+        quantize_quarter(first[1], x_first[1], quarters[1])
+        centres.append(laid("centres1", [2, 2 * PASS], U8, X_AT[0, 1]))
         part_words(picked[1], centres[1])
-        x_first.append(quantize(first[1][:], "x0_1"))
 
         third = laid("x_grouped1_0", [HALF, PACK], BF16, FIRST + GROUP)
         nc.vector.tensor_copy(as_words(third[:]), as_rows(x_raw[1, 0][:]))
         third_mx = quantize(third[:], "x1_0")
         last = laid("x_grouped1_1", [HALF, PACK], BF16, LATE + GROUP)
-        quarters = [slice(P * g, P * (g + 1)) for g in range(2)]
         for cols in reversed(quarters):
             nc.vector.tensor_copy(as_words(last[:, cols, :]), as_rows(x_raw[1, 1][:, :, cols]))
         last_codes = kept("x1_1_codes", [HALF], U32)
         last_scale = kept("x1_1_scale", [HALF], U8)
         for cols in reversed(quarters):
-            nc.vector.quantize_mx(
-                out=last_codes[:, cols].bitcast(E4M3),
-                scales=last_scale[:, cols],
-                in_=last[:, cols, :].rearrange("p m t -> p (m t)"),
-            )
+            quantize_quarter(last, (last_codes, last_scale), cols)
 
         res_rows = res.rearrange("(c p) m -> p c m", p=P)
         res_first = []
@@ -216,7 +223,7 @@ def tile_list_kernl_poly2_mix_res_kernel(
             rows = laid("res0_%d" % pair, [2, HALF], F32, SLOT // 2 + pair * SLOT)
             nc.sync.dma_start(rows[:], res_rows[:, 2 * pair : 2 * pair + 2, 0:HALF])
             res_first.append(rows)
-        al8 = laid("al8", [N], I32, SLOT)
+        al8 = laid("al8", [N], I32, X_AT[0, 0])
         nc.sync.dma_start(al8[:], al8_words[0].rearrange("p n f -> p (n f)").bitcast(I32))
         al4 = laid("al4", [2 * N], U8, X_AT[1, 0])
         nc.sync.dma_start(al4[:].bitcast(I32), al4_words[0].bitcast(I32))
@@ -285,38 +292,44 @@ def tile_list_kernl_poly2_mix_res_kernel(
             nc.vector.tensor_tensor(result[:], sums, residual, ALU.add)
             nc.sync.dma_start(out_rows[:, rows, cols], result[:])
 
-        def weigh(dots, cols, name, grouped):
+        def weigh(dots, b, cols, name, grouped):
             squares = kept("squares" + name, [PACK, cols.stop - cols.start], F32)
             for t in range(PACK):
-                nc.scalar.activation(squares[:, t, :], dots[t][:, cols], ACT.Square, bias=cb_sb[:, 0, t : t + 1])
-            weights = cw_sb[:, 0, 0:PACK].rearrange("p (c t i) -> p c t i", c=1, i=1)
+                nc.scalar.activation(squares[:, t, :], dots[t][:, cols], ACT.Square, bias=cb_sb[:, b, t : t + 1])
+            weights = cw_sb[:, b, 0:PACK].rearrange("p (c t i) -> p c t i", c=1, i=1)
             shape = [P, (cols.stop - cols.start) // PAIR, PACK, PAIR]
             nc.vector.tensor_tensor(as_words(grouped), as_rows(squares[:]), weights.to_broadcast(shape), ALU.mult)
 
-        def dots_by_tile(name, mx):
-            tiles = [bank("dot%s_%d" % (name, t), [HALF], t) for t in range(PACK)]
+        def dots_by_tile(name, mx, first_bank):
+            width = mx[0][0].shape[1]
+            tiles = [bank("dot%s_%d" % (name, t), [width], first_bank + t) for t in range(PACK)]
             for a in range(2):
                 for t in range(PACK):
                     dot_pass(tiles[t][:], 0, t, a, mx[a][0], mx[a][1], a == 0, a == 1)
             return [tile[:] for tile in tiles]
 
-        dots00 = dots_by_tile("00", [(codes[:], scale[:]) for codes, scale in x_first])
         grouped00 = laid("h_grouped00", [HALF, PACK], BF16, X_AT[1, 1])
-        weigh(dots00, slice(0, HALF), "00", grouped00[:])
-        dots01 = [bank("dot01_%d" % u, [2, HALF], 4 + u) for u in range(2)]
+        for g, cols in enumerate(quarters):
+            mx = [(codes[:, cols], scale[:, cols]) for codes, scale in x_first]
+            dots = dots_by_tile("00_%d" % g, mx, PACK * g)
+            if g == 0:
+                weigh(dots, 0, slice(0, P), "00_0", grouped00[:, cols, :])
+            else:
+                weave(square(dots, 0, "00_1"), 0, grouped00[:, cols, :])
+        dots01 = [bank("dot01_%d" % u, [2, HALF], u) for u in range(2)]
         for u in range(2):
             for a in (1, 0):
                 for i in range(2):
                     start, stop = a == 1 and i == 0, a == 0 and i == 1
                     dot_pass(dots01[u][:, i, :], 1, 2 * u + i, a, x_first[a][0][:], x_first[a][1][:], start, stop)
         x_second = [(third_mx[0][:], third_mx[1][:]), (last_codes[:], last_scale[:])]
-        dots10 = dots_by_tile("10", x_second)
+        dots10 = dots_by_tile("10", x_second, 2)
         pairs01 = square([dots01[t // 2][:, t % 2, :] for t in range(PACK)], 1, "01")
         grouped01 = weave(pairs01, 1, laid("h_grouped01", [HALF, PACK], BF16, X_AT[1, 1] + GROUP)[:])
         h00 = quantize(grouped00[:], "h00")
         h01 = quantize(grouped01, "h01", CODES)
         dots11 = []
-        for g, number in enumerate((4, 0)):
+        for g, number in enumerate((0, 2)):
             tile = bank("dot11_%d" % g, [PACK, P], number)
             for a in (1, 0):
                 codes, scale = x_second[a]
@@ -336,7 +349,7 @@ def tile_list_kernl_poly2_mix_res_kernel(
             weave(square([tile[:, cols] for tile in dots10], 0, "10_%d" % g), 0, grouped10[:, cols, :])
         finish(sums0[0][:], res_first[0][:], "0_0", slice(0, 2), slice(0, HALF))
         h10 = quantize(grouped10[:], "h10", CODES)
-        sums1 = [bank("sum1_%d" % pair, [2, HALF], 2 + pair) for pair in range(2)]
+        sums1 = [bank("sum1_%d" % pair, [2, HALF], 4 + pair) for pair in range(2)]
         for c in range(TILES):
             sum_pass(sums1[c // 2][:, c % 2, :], 0, c, h10, c % 2 == 0, False)
         grouped11 = []

@@ -300,36 +300,34 @@ def tile_list_kernl_poly2_mix_res_kernel(
             shape = [P, (cols.stop - cols.start) // PAIR, PACK, PAIR]
             nc.vector.tensor_tensor(as_words(grouped), as_rows(squares[:]), weights.to_broadcast(shape), ALU.mult)
 
-        def dots_by_tile(name, mx, first_bank):
+        def dots_by_tile(name, b, mx, first_bank, opening):
             width = mx[0][0].shape[1]
             tiles = [bank("dot%s_%d" % (name, t), [width], first_bank + t) for t in range(PACK)]
-            for a in range(2):
-                for t in range(PACK):
-                    dot_pass(tiles[t][:], 0, t, a, mx[a][0], mx[a][1], a == 0, a == 1)
+            if opening == 0:
+                order = [(t, a) for a in (0, 1) for t in range(PACK)]
+            else:
+                order = [(t, a) for t in range(PACK) for a in (1, 0)]
+            for t, a in order:
+                dot_pass(tiles[t][:], b, t, a, mx[a][0], mx[a][1], a == opening, a != opening)
             return [tile[:] for tile in tiles]
 
         grouped00 = laid("h_grouped00", [HALF, PACK], BF16, X_AT[1, 1])
         for g, cols in enumerate(quarters):
             mx = [(codes[:, cols], scale[:, cols]) for codes, scale in x_first]
-            dots = dots_by_tile("00_%d" % g, mx, PACK * g)
+            dots = dots_by_tile("00_%d" % g, 0, mx, PACK * g, g)
             if g == 0:
                 weigh(dots, 0, slice(0, P), "00_0", grouped00[:, cols, :])
             else:
                 weave(square(dots, 0, "00_1"), 0, grouped00[:, cols, :])
-        dots01 = [bank("dot01_%d" % u, [2, HALF], u) for u in range(2)]
-        for u in range(2):
-            for a in (1, 0):
-                for i in range(2):
-                    start, stop = a == 1 and i == 0, a == 0 and i == 1
-                    dot_pass(dots01[u][:, i, :], 1, 2 * u + i, a, x_first[a][0][:], x_first[a][1][:], start, stop)
+        dots01 = dots_by_tile("01", 1, [(codes[:], scale[:]) for codes, scale in x_first], 0, 1)
         x_second = [(third_mx[0][:], third_mx[1][:]), (last_codes[:], last_scale[:])]
-        dots10 = dots_by_tile("10", x_second, 2)
-        pairs01 = square([dots01[t // 2][:, t % 2, :] for t in range(PACK)], 1, "01")
+        dots10 = dots_by_tile("10", 0, x_second, PACK, 0)
+        pairs01 = square(dots01, 1, "01")
         grouped01 = weave(pairs01, 1, laid("h_grouped01", [HALF, PACK], BF16, X_AT[1, 1] + GROUP)[:])
         h00 = quantize(grouped00[:], "h00")
         h01 = quantize(grouped01, "h01", CODES)
         dots11 = []
-        for g, number in enumerate((0, 2)):
+        for g, number in enumerate((2, 4)):
             tile = bank("dot11_%d" % g, [PACK, P], number)
             for a in (1, 0):
                 codes, scale = x_second[a]
@@ -338,7 +336,7 @@ def tile_list_kernl_poly2_mix_res_kernel(
                     dot_pass(tile[:, t, :], 1, t, a, codes[:, quarters[g]], scale[:, quarters[g]], start, stop)
             dots11.append([tile[:, t, :] for t in range(PACK)])
 
-        sums0 = [bank("sum0_%d" % pair, [2, HALF], 6 + pair) for pair in range(2)]
+        sums0 = [bank("sum0_%d" % pair, [2, HALF], pair) for pair in range(2)]
         for pair in range(2):
             for b, mx in enumerate((h00, h01)):
                 for i in range(2):
@@ -349,7 +347,7 @@ def tile_list_kernl_poly2_mix_res_kernel(
             weave(square([tile[:, cols] for tile in dots10], 0, "10_%d" % g), 0, grouped10[:, cols, :])
         finish(sums0[0][:], res_first[0][:], "0_0", slice(0, 2), slice(0, HALF))
         h10 = quantize(grouped10[:], "h10", CODES)
-        sums1 = [bank("sum1_%d" % pair, [2, HALF], 4 + pair) for pair in range(2)]
+        sums1 = [bank("sum1_%d" % pair, [2, HALF], 6 + pair) for pair in range(2)]
         for c in range(TILES):
             sum_pass(sums1[c // 2][:, c % 2, :], 0, c, h10, c % 2 == 0, False)
         grouped11 = []

@@ -38,6 +38,7 @@ CODES = STAGED + J
 LATE = 6 * SLOT
 LAST_PART = SLOT // 2
 FIRST = 8 * SLOT
+ROOTS = 9 * SLOT
 ROWS_AT = P - 4
 SCALES_AT = P - 32
 
@@ -113,7 +114,7 @@ def tile_list_kernl_poly2_mix_res_kernel(
         nc.gpsimd.tensor_tensor(near_one[:], rough[:], guess[:], ALU.mult)
         factor = small("factor")
         nc.gpsimd.tensor_scalar(factor[:], near_one[:], -0.5, 1.5, ALU.mult, ALU.add)
-        root = small("root")
+        root = laid("root", [2, PACK], F32, ROOTS)
         nc.gpsimd.tensor_tensor(root[:], rough[:], factor[:], ALU.mult)
         shift = small("shift")
         nc.gpsimd.tensor_tensor(shift[:], root[:], cb_sb[:, :, 0:PACK], ALU.mult)
@@ -292,14 +293,6 @@ def tile_list_kernl_poly2_mix_res_kernel(
             nc.vector.tensor_tensor(result[:], sums, residual, ALU.add)
             nc.sync.dma_start(out_rows[:, rows, cols], result[:])
 
-        def weigh(dots, b, cols, name, grouped):
-            squares = kept("squares" + name, [PACK, cols.stop - cols.start], F32)
-            for t in range(PACK):
-                nc.scalar.activation(squares[:, t, :], dots[t][:, cols], ACT.Square, bias=cb_sb[:, b, t : t + 1])
-            weights = cw_sb[:, b, 0:PACK].rearrange("p (c t i) -> p c t i", c=1, i=1)
-            shape = [P, (cols.stop - cols.start) // PAIR, PACK, PAIR]
-            nc.vector.tensor_tensor(as_words(grouped), as_rows(squares[:]), weights.to_broadcast(shape), ALU.mult)
-
         def dots_by_tile(name, b, mx, first_bank, opening):
             width = mx[0][0].shape[1]
             tiles = [bank("dot%s_%d" % (name, t), [width], first_bank + t) for t in range(PACK)]
@@ -315,10 +308,7 @@ def tile_list_kernl_poly2_mix_res_kernel(
         for g, cols in enumerate(quarters):
             mx = [(codes[:, cols], scale[:, cols]) for codes, scale in x_first]
             dots = dots_by_tile("00_%d" % g, 0, mx, PACK * g, g)
-            if g == 0:
-                weigh(dots, 0, slice(0, P), "00_0", grouped00[:, cols, :])
-            else:
-                weave(square(dots, 0, "00_1"), 0, grouped00[:, cols, :])
+            weave(square(dots, 0, "00_%d" % g), 0, grouped00[:, cols, :])
         dots01 = dots_by_tile("01", 1, [(codes[:], scale[:]) for codes, scale in x_first], 0, 1)
         x_second = [(third_mx[0][:], third_mx[1][:]), (last_codes[:], last_scale[:])]
         dots10 = dots_by_tile("10", 0, x_second, PACK, 0)
@@ -346,23 +336,35 @@ def tile_list_kernl_poly2_mix_res_kernel(
         for g, cols in enumerate(quarters):
             weave(square([tile[:, cols] for tile in dots10], 0, "10_%d" % g), 0, grouped10[:, cols, :])
         finish(sums0[0][:], res_first[0][:], "0_0", slice(0, 2), slice(0, HALF))
-        h10 = quantize(grouped10[:], "h10", CODES)
-        sums1 = [bank("sum1_%d" % pair, [2, HALF], 6 + pair) for pair in range(2)]
-        for c in range(TILES):
-            sum_pass(sums1[c // 2][:, c % 2, :], 0, c, h10, c % 2 == 0, False)
-        grouped11 = []
-        for g in range(2):
+
+        def weave_last(g):
             name = "11_%d" % g
             tile = laid("h_grouped" + name, [P, PACK], BF16, LAST_PART + g * GROUP // 2)
-            grouped11.append(weave(square(dots11[g], 1, name), 1, tile[:]))
-        for g, cols in enumerate(quarters):
-            h11 = quantize(grouped11[g], "h11_%d" % g)
-            for c in range(TILES):
-                sum_pass(sums1[c // 2][:, c % 2, cols], 1, c, h11, False, g == 1 and c % 2 == 1)
-        for i in range(2):
+            return weave(square(dots11[g], 1, name), 1, tile[:])
+
+        def finish_tile(i, offset=None):
             rows = slice(2 + i, 3 + i)
-            held = LAST_PART + (i - 1) * GROUP // 2 + GROUP // 4
-            finish(sums0[1][:, i : i + 1, :], res_first[1][:, i : i + 1, :], "0_1_%d" % i, rows, slice(0, HALF), held)
-        for c in range(TILES):
-            rows = slice(c, c + 1)
-            finish(sums1[c // 2][:, c % 2 : c % 2 + 1, :], res_second[:, rows, :], "1_%d" % c, rows, slice(HALF, M))
+            finish(sums0[1][:, i : i + 1, :], res_first[1][:, i : i + 1, :], "0_1_%d" % i, rows, slice(0, HALF), offset)
+
+        sums1 = [bank("sum1_%d" % g, [TILES, P], 6 + g) for g in range(2)]
+
+        def last_passes(g, grouped):
+            h11 = quantize(grouped, "h11_%d" % g)
+            for c in range(TILES):
+                sum_pass(sums1[g][:, c, :], 1, c, h11, False, c == TILES - 1)
+
+        grouped = weave_last(0)
+        h10 = quantize(grouped10[:], "h10", CODES)
+        for g, cols in enumerate(quarters):
+            for c in range(TILES):
+                sum_pass(sums1[g][:, c, :], 0, c, (h10[0][:, cols], h10[1][:, cols]), c == 0, False)
+        last_passes(0, grouped)
+        finish_tile(0)
+        grouped = weave_last(1)
+        finish_tile(1, ROOTS)
+        last_passes(1, grouped)
+        for g, cols in enumerate(quarters):
+            for pair in range(2):
+                rows = slice(2 * pair, 2 * pair + 2)
+                stored = slice(HALF + cols.start, HALF + cols.stop)
+                finish(sums1[g][:, rows, :], res_second[:, rows, cols], "1_%d_%d" % (g, pair), rows, stored)

@@ -293,6 +293,14 @@ def tile_list_kernl_poly2_mix_res_kernel(
             nc.vector.tensor_tensor(result[:], sums, residual, ALU.add)
             nc.sync.dma_start(out_rows[:, rows, cols], result[:])
 
+        def weigh(dots, b, cols, name, grouped):
+            squares = kept("squares" + name, [PACK, cols.stop - cols.start], F32)
+            for t in range(PACK):
+                nc.scalar.activation(squares[:, t, :], dots[t][:, cols], ACT.Square, bias=cb_sb[:, b, t : t + 1])
+            weights = cw_sb[:, b, 0:PACK].rearrange("p (c t i) -> p c t i", c=1, i=1)
+            shape = [P, (cols.stop - cols.start) // PAIR, PACK, PAIR]
+            nc.vector.tensor_tensor(as_words(grouped), as_rows(squares[:]), weights.to_broadcast(shape), ALU.mult)
+
         def dots_by_tile(name, b, mx, first_bank, opening):
             width = mx[0][0].shape[1]
             tiles = [bank("dot%s_%d" % (name, t), [width], first_bank + t) for t in range(PACK)]
@@ -308,7 +316,10 @@ def tile_list_kernl_poly2_mix_res_kernel(
         for g, cols in enumerate(quarters):
             mx = [(codes[:, cols], scale[:, cols]) for codes, scale in x_first]
             dots = dots_by_tile("00_%d" % g, 0, mx, PACK * g, g)
-            weave(square(dots, 0, "00_%d" % g), 0, grouped00[:, cols, :])
+            if g == 0:
+                weigh(dots, 0, slice(0, P), "00_0", grouped00[:, cols, :])
+            else:
+                weave(square(dots, 0, "00_1"), 0, grouped00[:, cols, :])
         dots01 = dots_by_tile("01", 1, [(codes[:], scale[:]) for codes, scale in x_first], 0, 1)
         x_second = [(third_mx[0][:], third_mx[1][:]), (last_codes[:], last_scale[:])]
         dots10 = dots_by_tile("10", 0, x_second, PACK, 0)

@@ -208,8 +208,11 @@ def tile_list_kernl_poly2_mix_res_kernel(
         part_words(picked[1], centres[1])
 
         third = laid("x_grouped1_0", [HALF, PACK], BF16, FIRST + GROUP)
-        nc.vector.tensor_copy(as_words(third[:]), as_rows(x_raw[1, 0][:]))
-        third_mx = quantize(third[:], "x1_0")
+        for cols in quarters:
+            nc.vector.tensor_copy(as_words(third[:, cols, :]), as_rows(x_raw[1, 0][:, :, cols]))
+        third_mx = (kept("x1_0_codes", [HALF], U32), kept("x1_0_scale", [HALF], U8))
+        for cols in quarters:
+            quantize_quarter(third, third_mx, cols)
         last = laid("x_grouped1_1", [HALF, PACK], BF16, LATE + GROUP)
         for cols in reversed(quarters):
             nc.vector.tensor_copy(as_words(last[:, cols, :]), as_rows(x_raw[1, 1][:, :, cols]))

@@ -119,12 +119,12 @@ def tile_list_kernl_poly2_mix_res_kernel(
         shift = small("shift")
         nc.gpsimd.tensor_tensor(shift[:], root[:], cb_sb[:, :, 0:PACK], ALU.mult)
 
-        picked_scales = laid("picked_scales", [J], U8, AL_STAGED - N // 2)
+        picked_scales = laid("picked_scales", [SLOT], U8, AL_STAGED - N // 2)
         staged = laid("staged", [J], U8, STAGED)
-        nc.vector.tensor_copy(picked_scales[:], scale_rows[:].indirect(offsets[:]))
+        nc.vector.tensor_copy(picked_scales[:, 0:J], scale_rows[:].indirect(offsets[:]))
         nc.vector.tensor_copy(
             staged[:].rearrange("p (b t m) -> p b t m", b=2, t=PACK),
-            picked_scales[:].rearrange("p (b m t) -> p b t m", b=2, t=PACK),
+            picked_scales[:, 0:J].rearrange("p (b m t) -> p b t m", b=2, t=PACK),
         )
 
         def place_rows(dst, src, first_row):
@@ -136,7 +136,10 @@ def tile_list_kernl_poly2_mix_res_kernel(
 
         place_rows(placed, staged, SCALES_AT)
         load_x(1, 0)
-        load_x(1, 1)
+        x_last = []
+        for g in range(2):
+            x_last.append(laid("x_raw1_1_%d" % g, [PACK, P], F32, X_AT[1, 1] + g * GROUP))
+            nc.sync.dma_start(x_last[g][:], x_rows[1][:, :, HALF + P * g : HALF + P * (g + 1)])
         al_staged = laid("al_staged", [N], U8, AL_STAGED)
         for a, scales in enumerate((al8_scales, al4_scales)):
             nc.sync.dma_start(al_staged[a:32:2, :].bitcast(I32), scales[0].bitcast(I32))
@@ -208,18 +211,12 @@ def tile_list_kernl_poly2_mix_res_kernel(
         part_words(picked[1], centres[1])
 
         third = laid("x_grouped1_0", [HALF, PACK], BF16, FIRST + GROUP)
-        for cols in quarters:
-            nc.vector.tensor_copy(as_words(third[:, cols, :]), as_rows(x_raw[1, 0][:, :, cols]))
-        third_mx = (kept("x1_0_codes", [HALF], U32), kept("x1_0_scale", [HALF], U8))
-        for cols in quarters:
-            quantize_quarter(third, third_mx, cols)
+        nc.vector.tensor_copy(as_words(third[:]), as_rows(x_raw[1, 0][:]))
         last = laid("x_grouped1_1", [HALF, PACK], BF16, LATE + GROUP)
-        for cols in reversed(quarters):
-            nc.vector.tensor_copy(as_words(last[:, cols, :]), as_rows(x_raw[1, 1][:, :, cols]))
-        last_codes = kept("x1_1_codes", [HALF], U32)
-        last_scale = kept("x1_1_scale", [HALF], U8)
-        for cols in reversed(quarters):
-            quantize_quarter(last, (last_codes, last_scale), cols)
+        for cols, raw in zip(quarters, x_last):
+            nc.vector.tensor_copy(as_words(last[:, cols, :]), as_rows(raw[:]))
+        third_mx = quantize(third[:], "x1_0", X_AT[1, 1])
+        last_codes, last_scale = quantize(last[:], "x1_1")
 
         res_rows = res.rearrange("(c p) m -> p c m", p=P)
         res_first = []
@@ -315,7 +312,7 @@ def tile_list_kernl_poly2_mix_res_kernel(
                 dot_pass(tiles[t][:], b, t, a, mx[a][0], mx[a][1], a == opening, a != opening)
             return [tile[:] for tile in tiles]
 
-        grouped00 = laid("h_grouped00", [HALF, PACK], BF16, X_AT[1, 1])
+        grouped00 = laid("h_grouped00", [HALF, PACK], BF16, X_AT[1, 1] + J + GROUP)
         for g, cols in enumerate(quarters):
             mx = [(codes[:, cols], scale[:, cols]) for codes, scale in x_first]
             dots = dots_by_tile("00_%d" % g, 0, mx, PACK * g, g)
@@ -327,8 +324,10 @@ def tile_list_kernl_poly2_mix_res_kernel(
         x_second = [(third_mx[0][:], third_mx[1][:]), (last_codes[:], last_scale[:])]
         dots10 = dots_by_tile("10", 0, x_second, PACK, 0)
         pairs01 = square(dots01, 1, "01")
-        grouped01 = weave(pairs01, 1, laid("h_grouped01", [HALF, PACK], BF16, X_AT[1, 1] + GROUP)[:])
-        h00 = quantize(grouped00[:], "h00")
+        h00 = (kept("h00_codes", [HALF], U32), kept("h00_scale", [HALF], U8))
+        quantize_quarter(grouped00, h00, quarters[0])
+        grouped01 = weave(pairs01, 1, laid("h_grouped01", [HALF, PACK], BF16, X_AT[1, 1] + J)[:])
+        quantize_quarter(grouped00, h00, quarters[1])
         h01 = quantize(grouped01, "h01", CODES)
         dots11 = []
         for g, number in enumerate((2, 4)):
@@ -360,18 +359,22 @@ def tile_list_kernl_poly2_mix_res_kernel(
             rows = slice(2 + i, 3 + i)
             finish(sums0[1][:, i : i + 1, :], res_first[1][:, i : i + 1, :], "0_1_%d" % i, rows, slice(0, HALF), offset)
 
-        sums1 = [bank("sum1_%d" % g, [TILES, P], 6 + g) for g in range(2)]
+        whole = bank("sum1_0", [TILES, P], 6)
+        parts = [bank("sum1_1_%d" % pair, [2, P], number) for pair, number in enumerate((7, 3))]
+        sums1 = [[whole[:, 0:2, :], whole[:, 2:4, :]], [part[:] for part in parts]]
+        closing = [(TILES - 1,), (1, TILES - 1)]
+        opening = [(0,), (0, 2)]
 
         def last_passes(g, grouped):
             h11 = quantize(grouped, "h11_%d" % g)
             for c in range(TILES):
-                sum_pass(sums1[g][:, c, :], 1, c, h11, False, c == TILES - 1)
+                sum_pass(sums1[g][c // 2][:, c % 2, :], 1, c, h11, False, c in closing[g])
 
         grouped = weave_last(0)
         h10 = quantize(grouped10[:], "h10", CODES)
         for g, cols in enumerate(quarters):
             for c in range(TILES):
-                sum_pass(sums1[g][:, c, :], 0, c, (h10[0][:, cols], h10[1][:, cols]), c == 0, False)
+                sum_pass(sums1[g][c // 2][:, c % 2, :], 0, c, (h10[0][:, cols], h10[1][:, cols]), c in opening[g], False)
         last_passes(0, grouped)
         finish_tile(0)
         grouped = weave_last(1)
@@ -381,4 +384,4 @@ def tile_list_kernl_poly2_mix_res_kernel(
             for pair in range(2):
                 rows = slice(2 * pair, 2 * pair + 2)
                 stored = slice(HALF + cols.start, HALF + cols.stop)
-                finish(sums1[g][:, rows, :], res_second[:, rows, cols], "1_%d_%d" % (g, pair), rows, stored)
+                finish(sums1[g][pair], res_second[:, rows, cols], "1_%d_%d" % (g, pair), rows, stored)

@@ -24,7 +24,6 @@ HALF = M // 2
 TILES = N // P
 LIST_COLS = PASS // 16
 PAIR = 2
-RUN = 4
 TINY = 1e-36
 
 WARM_UP = (HALF, HALF, HALF, HALF, P)
@@ -162,8 +161,8 @@ def tile_list_kernl_poly2_mix_res_kernel(
 
         def part_words(words, parted):
             nc.vector.tensor_copy(
-                parted[:].bitcast(U16).rearrange("p a (t c i) -> p a c t i", t=PACK, i=RUN),
-                words[:].bitcast(U16).rearrange("p (c i t a) -> p a c t i", i=RUN, t=PACK, a=2),
+                parted[:].bitcast(U16).rearrange("p a (t m) -> p a m t", t=PACK),
+                words[:].bitcast(U16).rearrange("p (m t a) -> p a m t", t=PACK, a=2),
             )
 
         idle = kept("idle", [HALF, PACK], BF16)

@@ -34,7 +34,7 @@ X_AT = {(0, 0): 0, (0, 1): SLOT, (1, 0): 2 * SLOT, (1, 1): 3 * SLOT + N}
 AL_STAGED = X_AT[1, 1] - N
 STAGED = 5 * SLOT
 CODES = STAGED + J
-LATE = 6 * SLOT
+LATE = 6 * SLOT + GROUP
 LAST_PART = SLOT // 2
 FIRST = 8 * SLOT
 ROOTS = 9 * SLOT
@@ -146,8 +146,8 @@ def tile_list_kernl_poly2_mix_res_kernel(
         def as_words(grouped):
             return grouped.rearrange("p (c i) t -> p c t i", i=PAIR)
 
-        def as_rows(rows):
-            return rows.rearrange("p t (c i) -> p c t i", i=PAIR)
+        def as_rows(planes):
+            return planes.rearrange("p t (c i) -> p c t i", i=PAIR)
 
         def quantize(grouped, name, offset=None):
             width = grouped.shape[1]
@@ -156,7 +156,8 @@ def tile_list_kernl_poly2_mix_res_kernel(
             else:
                 codes = laid(name + "_codes", [width], U32, offset)
             scale = kept(name + "_scale", [width], U8)
-            nc.vector.quantize_mx(out=codes[:].bitcast(E4M3), scales=scale[:], in_=grouped.rearrange("p m t -> p (m t)"))
+            values = grouped.rearrange("p m t -> p (m t)")
+            nc.vector.quantize_mx(out=codes[:].bitcast(E4M3), scales=scale[:], in_=values)
             return codes, scale
 
         def part_words(words, parted):
@@ -211,7 +212,7 @@ def tile_list_kernl_poly2_mix_res_kernel(
 
         third = laid("x_grouped1_0", [HALF, PACK], BF16, FIRST + GROUP)
         nc.vector.tensor_copy(as_words(third[:]), as_rows(x_raw[1, 0][:]))
-        last = laid("x_grouped1_1", [HALF, PACK], BF16, LATE + GROUP)
+        last = laid("x_grouped1_1", [HALF, PACK], BF16, LATE)
         for cols, raw in zip(quarters, x_last):
             nc.vector.tensor_copy(as_words(last[:, cols, :]), as_rows(raw[:]))
         third_mx = quantize(third[:], "x1_0", X_AT[1, 1])
@@ -219,16 +220,15 @@ def tile_list_kernl_poly2_mix_res_kernel(
 
         res_rows = res.rearrange("(c p) m -> p c m", p=P)
         res_first = []
-        for pair in range(2):
-            rows = laid("res0_%d" % pair, [2, HALF], F32, SLOT // 2 + pair * SLOT)
-            nc.sync.dma_start(rows[:], res_rows[:, 2 * pair : 2 * pair + 2, 0:HALF])
-            res_first.append(rows)
+        for side in range(2):
+            res_first.append(laid("res0_%d" % side, [2, HALF], F32, LAST_PART + side * SLOT))
+            nc.sync.dma_start(res_first[side][:], res_rows[:, 2 * side : 2 * side + 2, 0:HALF])
         al8 = laid("al8", [N], I32, X_AT[0, 0])
         nc.sync.dma_start(al8[:], al8_words[0].rearrange("p n f -> p (n f)").bitcast(I32))
         al4 = laid("al4", [2 * N], U8, X_AT[1, 0])
         nc.sync.dma_start(al4[:].bitcast(I32), al4_words[0].bitcast(I32))
         place_rows(al_placed, al_staged, 0)
-        res_second = laid("res1", [TILES, HALF], F32, LATE + GROUP)
+        res_second = laid("res1", [TILES, HALF], F32, LATE)
         nc.sync.dma_start(res_second[:], res_rows[:, :, HALF:M])
         out_rows = out.rearrange("(c p) m -> p c m", p=P)
 
@@ -292,41 +292,39 @@ def tile_list_kernl_poly2_mix_res_kernel(
             nc.vector.tensor_tensor(result[:], sums, residual, ALU.add)
             nc.sync.dma_start(out_rows[:, rows, cols], result[:])
 
-        def weigh(dots, b, cols, name, grouped):
-            squares = kept("squares" + name, [PACK, cols.stop - cols.start], F32)
+        def weigh(dots, b, name, grouped):
+            width = dots[0].shape[1]
+            squares = kept("squares" + name, [PACK, width], F32)
             for t in range(PACK):
-                nc.scalar.activation(squares[:, t, :], dots[t][:, cols], ACT.Square, bias=cb_sb[:, b, t : t + 1])
+                nc.scalar.activation(squares[:, t, :], dots[t], ACT.Square, bias=cb_sb[:, b, t : t + 1])
             weights = cw_sb[:, b, 0:PACK].rearrange("p (c t i) -> p c t i", c=1, i=1)
-            shape = [P, (cols.stop - cols.start) // PAIR, PACK, PAIR]
+            shape = [P, width // PAIR, PACK, PAIR]
             nc.vector.tensor_tensor(as_words(grouped), as_rows(squares[:]), weights.to_broadcast(shape), ALU.mult)
 
-        def dots_by_tile(name, b, mx, first_bank, opening):
+        def dots_by_tile(name, b, mx, first_bank, ahead):
             width = mx[0][0].shape[1]
             tiles = [bank("dot%s_%d" % (name, t), [width], first_bank + t) for t in range(PACK)]
-            if opening == 0:
-                order = [(t, a) for a in (0, 1) for t in range(PACK)]
-            else:
-                order = [(t, a) for t in range(PACK) for a in (1, 0)]
+            order = [(t, 0) for t in range(ahead)] + [(t, 1) for t in range(ahead)]
+            order = order + [(t, a) for t in range(ahead, PACK) for a in (1, 0)]
             for t, a in order:
-                dot_pass(tiles[t][:], b, t, a, mx[a][0], mx[a][1], a == opening, a != opening)
+                opens = a == (0 if t < ahead else 1)
+                dot_pass(tiles[t][:], b, t, a, mx[a][0], mx[a][1], opens, not opens)
             return [tile[:] for tile in tiles]
 
         grouped00 = laid("h_grouped00", [HALF, PACK], BF16, X_AT[1, 1] + J + GROUP)
         for g, cols in enumerate(quarters):
             mx = [(codes[:, cols], scale[:, cols]) for codes, scale in x_first]
-            dots = dots_by_tile("00_%d" % g, 0, mx, PACK * g, g)
+            dots = dots_by_tile("00_%d" % g, 0, mx, PACK * g, 1 - g)
             if g == 0:
-                weigh(dots, 0, slice(0, P), "00_0", grouped00[:, cols, :])
+                weigh(dots, 0, "00_0", grouped00[:, cols, :])
             else:
                 weave(square(dots, 0, "00_1"), 0, grouped00[:, cols, :])
-        dots01 = dots_by_tile("01", 1, [(codes[:], scale[:]) for codes, scale in x_first], 0, 1)
+        dots01 = dots_by_tile("01", 1, [(codes[:], scale[:]) for codes, scale in x_first], 0, 0)
         x_second = [(third_mx[0][:], third_mx[1][:]), (last_codes[:], last_scale[:])]
-        dots10 = dots_by_tile("10", 0, x_second, PACK, 0)
+        dots10 = dots_by_tile("10", 0, x_second, PACK, PACK)
         pairs01 = square(dots01, 1, "01")
-        h00 = (kept("h00_codes", [HALF], U32), kept("h00_scale", [HALF], U8))
-        quantize_quarter(grouped00, h00, quarters[0])
         grouped01 = weave(pairs01, 1, laid("h_grouped01", [HALF, PACK], BF16, X_AT[1, 1] + J)[:])
-        quantize_quarter(grouped00, h00, quarters[1])
+        h00 = quantize(grouped00[:], "h00")
         h01 = quantize(grouped01, "h01", CODES)
         dots11 = []
         for g, number in enumerate((2, 4)):
@@ -338,11 +336,11 @@ def tile_list_kernl_poly2_mix_res_kernel(
                     dot_pass(tile[:, t, :], 1, t, a, codes[:, quarters[g]], scale[:, quarters[g]], start, stop)
             dots11.append([tile[:, t, :] for t in range(PACK)])
 
-        sums0 = [bank("sum0_%d" % pair, [2, HALF], pair) for pair in range(2)]
-        for pair in range(2):
+        sums0 = [bank("sum0_%d" % side, [2, HALF], side) for side in range(2)]
+        for side in range(2):
             for b, mx in enumerate((h00, h01)):
                 for i in range(2):
-                    sum_pass(sums0[pair][:, i, :], b, 2 * pair + i, mx, b == 0 and i == 0, b == 1 and i == 1)
+                    sum_pass(sums0[side][:, i, :], b, 2 * side + i, mx, b == 0 and i == 0, b == 1 and i == 1)
 
         grouped10 = kept("h_grouped10", [HALF, PACK], BF16)
         for g, cols in enumerate(quarters):
@@ -359,28 +357,28 @@ def tile_list_kernl_poly2_mix_res_kernel(
             finish(sums0[1][:, i : i + 1, :], res_first[1][:, i : i + 1, :], "0_1_%d" % i, rows, slice(0, HALF), offset)
 
         whole = bank("sum1_0", [TILES, P], 6)
-        parts = [bank("sum1_1_%d" % pair, [2, P], number) for pair, number in enumerate((7, 3))]
-        sums1 = [[whole[:, 0:2, :], whole[:, 2:4, :]], [part[:] for part in parts]]
-        closing = [(TILES - 1,), (1, TILES - 1)]
-        opening = [(0,), (0, 2)]
+        sides = [bank("sum1_1_%d" % side, [2, P], number) for side, number in enumerate((7, 3))]
+        sums1 = [[whole[:, 0:2, :], whole[:, 2:4, :]], [tile[:] for tile in sides]]
+        tiles_a_bank = (TILES, 2)
 
         def last_passes(g, grouped):
             h11 = quantize(grouped, "h11_%d" % g)
             for c in range(TILES):
-                sum_pass(sums1[g][c // 2][:, c % 2, :], 1, c, h11, False, c in closing[g])
+                sum_pass(sums1[g][c // 2][:, c % 2, :], 1, c, h11, False, (c + 1) % tiles_a_bank[g] == 0)
 
         grouped = weave_last(0)
         h10 = quantize(grouped10[:], "h10", CODES)
         for g, cols in enumerate(quarters):
+            mx = (h10[0][:, cols], h10[1][:, cols])
             for c in range(TILES):
-                sum_pass(sums1[g][c // 2][:, c % 2, :], 0, c, (h10[0][:, cols], h10[1][:, cols]), c in opening[g], False)
+                sum_pass(sums1[g][c // 2][:, c % 2, :], 0, c, mx, c % tiles_a_bank[g] == 0, False)
         last_passes(0, grouped)
         finish_tile(0)
         grouped = weave_last(1)
         finish_tile(1, ROOTS)
         last_passes(1, grouped)
         for g, cols in enumerate(quarters):
-            for pair in range(2):
-                rows = slice(2 * pair, 2 * pair + 2)
+            for side in range(2):
+                rows = slice(2 * side, 2 * side + 2)
                 stored = slice(HALF + cols.start, HALF + cols.stop)
-                finish(sums1[g][pair], res_second[:, rows, cols], "1_%d_%d" % (g, pair), rows, stored)
+                finish(sums1[g][side], res_second[:, rows, cols], "1_%d_%d" % (g, side), rows, stored)

@@ -160,10 +160,10 @@ def tile_list_kernl_poly2_mix_res_kernel(
             nc.vector.quantize_mx(out=codes[:].bitcast(E4M3), scales=scale[:], in_=values)
             return codes, scale
 
-        def part_words(words, parted):
+        def part_words(words, parted, passes):
             nc.vector.tensor_copy(
                 parted[:].bitcast(U16).rearrange("p a (t m) -> p a m t", t=PACK),
-                words[:].bitcast(U16).rearrange("p (m t a) -> p a m t", t=PACK, a=2),
+                words[:].bitcast(U16).rearrange("p (m t a) -> p a m t", t=PACK, a=2)[:, passes],
             )
 
         idle = kept("idle", [HALF, PACK], BF16)
@@ -188,14 +188,17 @@ def tile_list_kernl_poly2_mix_res_kernel(
                 stop=i == len(WARM_UP) - 1,
             )
 
-        centres = [kept("centres0", [2, 2 * PASS], U8)]
-        part_words(picked[0], centres[0])
+        early = kept("centres0_0", [1, 2 * PASS], U8)
+        part_words(picked[0], early, slice(0, 1))
         first = [laid("x_grouped0_%d" % a, [HALF, PACK], BF16, FIRST + a * GROUP) for a in range(2)]
         quarters = [slice(P * g, P * (g + 1)) for g in range(2)]
         nc.scalar.activation(as_words(first[0][:]), as_rows(x_raw[0, 0][:]), ACT.Copy)
         for cols in quarters:
             nc.scalar.activation(as_words(first[1][:, cols, :]), as_rows(x_raw[0, 1][:, :, cols]), ACT.Copy)
         x_first = [quantize(first[0][:], "x0_0")]
+        late = laid("centres0_1", [1, 2 * PASS], U8, X_AT[0, 0])
+        part_words(picked[0], late, slice(1, 2))
+        centres = [(early[:, 0, :], late[:, 0, :])]
         x_first.append((kept("x0_1_codes", [HALF], U32), kept("x0_1_scale", [HALF], U8)))
 
         def quantize_quarter(grouped, mx, cols):
@@ -207,8 +210,9 @@ def tile_list_kernl_poly2_mix_res_kernel(
 
         quantize_quarter(first[1], x_first[1], quarters[0])
         quantize_quarter(first[1], x_first[1], quarters[1])
-        centres.append(laid("centres1", [2, 2 * PASS], U8, X_AT[0, 1]))
-        part_words(picked[1], centres[1])
+        both = laid("centres1", [2, 2 * PASS], U8, X_AT[0, 1])
+        part_words(picked[1], both, slice(0, 2))
+        centres.append((both[:, 0, :], both[:, 1, :]))
 
         third = laid("x_grouped1_0", [HALF, PACK], BF16, FIRST + GROUP)
         nc.vector.tensor_copy(as_words(third[:]), as_rows(x_raw[1, 0][:]))
@@ -223,7 +227,7 @@ def tile_list_kernl_poly2_mix_res_kernel(
         for side in range(2):
             res_first.append(laid("res0_%d" % side, [2, HALF], F32, LAST_PART + side * SLOT))
             nc.sync.dma_start(res_first[side][:], res_rows[:, 2 * side : 2 * side + 2, 0:HALF])
-        al8 = laid("al8", [N], I32, X_AT[0, 0])
+        al8 = laid("al8", [N], I32, X_AT[1, 0] + GROUP)
         nc.sync.dma_start(al8[:], al8_words[0].rearrange("p n f -> p (n f)").bitcast(I32))
         al4 = laid("al4", [2 * N], U8, X_AT[1, 0])
         nc.sync.dma_start(al4[:].bitcast(I32), al4_words[0].bitcast(I32))
@@ -236,7 +240,7 @@ def tile_list_kernl_poly2_mix_res_kernel(
             col = PASS * b + P * t
             nc.tensor.matmul_mx(
                 out=dst,
-                lhsT=centres[b][:, a, 2 * P * t : 2 * P * (t + 1)].bitcast(E2M1),
+                lhsT=centres[b][a][:, 2 * P * t : 2 * P * (t + 1)].bitcast(E2M1),
                 lhsT_scale=placed[:, a, col : col + P],
                 rhs=codes.bitcast(E4M3),
                 rhs_scale=scale,
@@ -314,7 +318,7 @@ def tile_list_kernl_poly2_mix_res_kernel(
         grouped00 = laid("h_grouped00", [HALF, PACK], BF16, X_AT[1, 1] + J + GROUP)
         for g, cols in enumerate(quarters):
             mx = [(codes[:, cols], scale[:, cols]) for codes, scale in x_first]
-            dots = dots_by_tile("00_%d" % g, 0, mx, PACK * g, 1 - g)
+            dots = dots_by_tile("00_%d" % g, 0, mx, PACK * g, PACK - 2 * g)
             if g == 0:
                 weigh(dots, 0, "00_0", grouped00[:, cols, :])
             else:

@@ -318,7 +318,7 @@ def tile_list_kernl_poly2_mix_res_kernel(
         grouped00 = laid("h_grouped00", [HALF, PACK], BF16, X_AT[1, 1] + J + GROUP)
         for g, cols in enumerate(quarters):
             mx = [(codes[:, cols], scale[:, cols]) for codes, scale in x_first]
-            dots = dots_by_tile("00_%d" % g, 0, mx, PACK * g, PACK - 2 * g)
+            dots = dots_by_tile("00_%d" % g, 0, mx, PACK * g, PACK * (1 - g))
             if g == 0:
                 weigh(dots, 0, "00_0", grouped00[:, cols, :])
             else:

from contextlib import ExitStack

import concourse.mybir as mybir
from concourse.masks import make_identity

K, M, N, J, T = 1024, 512, 512, 1024, 4096
FLOPS = 2 * K * J * M + 2 * J * N * M

F32 = mybir.dt.float32
BF16 = mybir.dt.bfloat16
I32 = mybir.dt.int32
U32 = mybir.dt.uint32
U16 = mybir.dt.uint16
U8 = mybir.dt.uint8
E4M3 = mybir.dt.float8_e4m3fn_x4
E2M1 = mybir.dt.float4_e2m1fn_x4
ACT = mybir.ActivationFunctionType
ALU = mybir.AluOpType

P = 128
PACK = 4
PASS = P * PACK
HALF = M // 2
TILES = N // P
LIST_COLS = PASS // 16
PAIR = 2
TINY = 1e-36

WARM_UP = (HALF, HALF, HALF, HALF, P)

SLOT = PACK * HALF * 4
GROUP = PACK * HALF * 2
X_AT = {(0, 0): 0, (0, 1): SLOT, (1, 0): 2 * SLOT, (1, 1): 3 * SLOT + N}
AL_STAGED = X_AT[1, 1] - N
STAGED = 5 * SLOT
CODES = STAGED + J
LATE = 6 * SLOT + GROUP
LAST_PART = SLOT // 2
FIRST = 8 * SLOT
ROOTS = 9 * SLOT
ROWS_AT = P - 4
SCALES_AT = P - 32


def tile_list_kernl_poly2_mix_res_kernel(
    tc, x, tab_words, tab_scales, cw, cb, al8_words, al8_scales, al4_words, al4_scales, res, offs, out
):
    nc = tc.nc
    with ExitStack() as ctx:
        keep = ctx.enter_context(tc.tile_pool(name="keep", bufs=1))
        stage = ctx.enter_context(tc.tile_pool(name="stage", bufs=1))
        psum = ctx.enter_context(tc.psum_pool(name="psum", bufs=1))

        def kept(name, shape, dtype):
            return keep.tile([P] + shape, dtype, name=name, align_bytes=64)

        def laid(name, shape, dtype, offset):
            return stage.tile([P] + shape, dtype, name=name, offset=offset, align_bytes=64)

        def bank(name, shape, number):
            return psum.tile([P] + shape, F32, name=name, tag="bank%d" % number)

        offsets = keep.tile([P, J // 16], U16, name="offsets")
        scale_rows = kept("scale_rows", [T], U8)
        nc.sync.dma_start(scale_rows[SCALES_AT:P, :].bitcast(I32), tab_scales.rearrange("a q t -> q a t").bitcast(I32))
        nc.sync.dma_start(offsets[:], offs)
        nc.vector.memset(scale_rows[0:SCALES_AT, :].bitcast(I32), 0)

        placed = kept("placed", [2, J], U8)
        nc.gpsimd.memset(placed[:].rearrange("p a n -> p (a n)").bitcast(I32), 0)
        identity = kept("identity", [P], F32)
        make_identity(nc, identity[:])
        vector_rows = kept("vector_rows", [PASS], F32)
        nc.scalar.dma_start(vector_rows[ROWS_AT : ROWS_AT + 2, :], cw.rearrange("(b c) -> b c", b=2))
        nc.scalar.dma_start(vector_rows[ROWS_AT + 2 : ROWS_AT + 4, :], cb.rearrange("(b c) -> b c", b=2))
        nc.vector.memset(vector_rows[0:ROWS_AT, :].bitcast(I32), 0)

        table = kept("table", [T], I32)
        nc.sync.dma_start(table[:], tab_words[0].rearrange("p t f -> p (t f)").bitcast(I32))

        x_rows = x.rearrange("(a p t) m -> a p t m", a=2, t=PACK)
        x_raw = {}

        def load_x(half, a):
            x_raw[half, a] = laid("x_raw%d_%d" % (half, a), [PACK, HALF], F32, X_AT[half, a])
            nc.sync.dma_start(x_raw[half, a][:], x_rows[a][:, :, HALF * half : HALF * (half + 1)])

        load_x(0, 0)
        load_x(0, 1)

        al_placed = kept("al_placed", [2, N], U8)
        nc.gpsimd.memset(al_placed[:].rearrange("p a n -> p (a n)").bitcast(I32), 0)

        def small(name, dtype=F32):
            return keep.tile([P, 2, PACK], dtype, name=name)

        turned = bank("turned", [PACK, P], 7)
        for t in range(PACK):
            nc.tensor.transpose(turned[:, t, :], vector_rows[:, t:PASS:PACK], identity[:])
        by_row = turned[:, :, ROWS_AT : ROWS_AT + 4].rearrange("p t r -> p r t")
        guess = laid("guess", [2, PACK], F32, FIRST + GROUP)
        nc.scalar.activation(guess[:], by_row[:, 0:2, :], ACT.Abs_reciprocal_sqrt, bias=TINY)
        vectors = kept("vectors", [4, PACK], F32)
        nc.scalar.copy(vectors[:], by_row)
        cw_sb, cb_sb = vectors[:, 0:2, :], vectors[:, 2:4, :]
        sign = small("sign", BF16)
        nc.scalar.activation(sign[:], by_row[:, 0:2, :], ACT.Sign)
        size = laid("size", [2, PACK], F32, FIRST)
        nc.scalar.activation(size[:], by_row[:, 0:2, :], ACT.Abs)
        rough = small("rough")
        nc.gpsimd.tensor_tensor(rough[:], size[:], guess[:], ALU.mult)
        near_one = small("near_one")
        nc.gpsimd.tensor_tensor(near_one[:], rough[:], guess[:], ALU.mult)
        factor = small("factor")
        nc.gpsimd.tensor_scalar(factor[:], near_one[:], -0.5, 1.5, ALU.mult, ALU.add)
        root = laid("root", [2, PACK], F32, ROOTS)
        nc.gpsimd.tensor_tensor(root[:], rough[:], factor[:], ALU.mult)
        shift = small("shift")
        nc.gpsimd.tensor_tensor(shift[:], root[:], cb_sb[:, :, 0:PACK], ALU.mult)

        picked_scales = laid("picked_scales", [SLOT], U8, AL_STAGED - N // 2)
        staged = laid("staged", [J], U8, STAGED)
        nc.vector.tensor_copy(picked_scales[:, 0:J], scale_rows[:].indirect(offsets[:]))
        nc.vector.tensor_copy(
            staged[:].rearrange("p (b t m) -> p b t m", b=2, t=PACK),
            picked_scales[:, 0:J].rearrange("p (b m t) -> p b t m", b=2, t=PACK),
        )

        def place_rows(dst, src, first_row):
            for quad in (0, 2, 1, 3):
                nc.sync.dma_start(
                    dst[32 * quad : 32 * quad + 4].rearrange("p a n -> p (a n)").bitcast(I32),
                    src[first_row + 8 * quad : first_row + 8 * quad + 8, :].bitcast(I32),
                )

        place_rows(placed, staged, SCALES_AT)
        load_x(1, 0)
        x_last = []
        for g in range(2):
            x_last.append(laid("x_raw1_1_%d" % g, [PACK, P], F32, X_AT[1, 1] + g * GROUP))
            nc.sync.dma_start(x_last[g][:], x_rows[1][:, :, HALF + P * g : HALF + P * (g + 1)])
        al_staged = laid("al_staged", [N], U8, AL_STAGED)
        for a, scales in enumerate((al8_scales, al4_scales)):
            nc.sync.dma_start(al_staged[a:32:2, :].bitcast(I32), scales[0].bitcast(I32))

        def as_words(grouped):
            return grouped.rearrange("p (c i) t -> p c t i", i=PAIR)

        def as_rows(planes):
            return planes.rearrange("p t (c i) -> p c t i", i=PAIR)

        def quantize(grouped, name, offset=None):
            width = grouped.shape[1]
            if offset is None:
                codes = kept(name + "_codes", [width], U32)
            else:
                codes = laid(name + "_codes", [width], U32, offset)
            scale = kept(name + "_scale", [width], U8)
            values = grouped.rearrange("p m t -> p (m t)")
            nc.vector.quantize_mx(out=codes[:].bitcast(E4M3), scales=scale[:], in_=values)
            return codes, scale

        def part_words(words, parted, passes):
            nc.vector.tensor_copy(
                parted[:].bitcast(U16).rearrange("p a (t m) -> p a m t", t=PACK),
                words[:].bitcast(U16).rearrange("p (m t a) -> p a m t", t=PACK, a=2)[:, passes],
            )

        idle = kept("idle", [HALF, PACK], BF16)
        nc.vector.memset(idle[:].rearrange("p m t -> p (m t)").bitcast(I32), 0)
        idle_codes, idle_scale = quantize(idle[:], "idle")

        picked = [kept("picked%d" % b, [PASS], U32) for b in range(2)]
        for b in range(2):
            nc.vector.tensor_copy(
                picked[b][:], table[:].bitcast(U32).indirect(offsets[:, LIST_COLS * b : LIST_COLS * (b + 1)])
            )

        warm = bank("warm", [HALF], 7)
        for i, width in enumerate(WARM_UP):
            nc.tensor.matmul_mx(
                out=warm[:, 0:width],
                lhsT=picked[0][:, 0 : P // 2].bitcast(U8).bitcast(E2M1),
                lhsT_scale=staged[:, 0:P],
                rhs=idle_codes[:, 0:width].bitcast(E4M3),
                rhs_scale=idle_scale[:, 0:width],
                start=i == 0,
                stop=i == len(WARM_UP) - 1,
            )

        early = kept("centres0_0", [1, 2 * PASS], U8)
        part_words(picked[0], early, slice(0, 1))
        first = [laid("x_grouped0_%d" % a, [HALF, PACK], BF16, FIRST + a * GROUP) for a in range(2)]
        quarters = [slice(P * g, P * (g + 1)) for g in range(2)]
        nc.scalar.activation(as_words(first[0][:]), as_rows(x_raw[0, 0][:]), ACT.Copy)
        for cols in quarters:
            nc.scalar.activation(as_words(first[1][:, cols, :]), as_rows(x_raw[0, 1][:, :, cols]), ACT.Copy)
        x_first = [quantize(first[0][:], "x0_0")]
        late = laid("centres0_1", [1, 2 * PASS], U8, X_AT[0, 0])
        part_words(picked[0], late, slice(1, 2))
        centres = [(early[:, 0, :], late[:, 0, :])]
        x_first.append((kept("x0_1_codes", [HALF], U32), kept("x0_1_scale", [HALF], U8)))

        def quantize_quarter(grouped, mx, cols):
            nc.vector.quantize_mx(
                out=mx[0][:, cols].bitcast(E4M3),
                scales=mx[1][:, cols],
                in_=grouped[:, cols, :].rearrange("p m t -> p (m t)"),
            )

        quantize_quarter(first[1], x_first[1], quarters[0])
        quantize_quarter(first[1], x_first[1], quarters[1])
        both = laid("centres1", [2, 2 * PASS], U8, X_AT[0, 1])
        part_words(picked[1], both, slice(0, 2))
        centres.append((both[:, 0, :], both[:, 1, :]))

        third = laid("x_grouped1_0", [HALF, PACK], BF16, FIRST + GROUP)
        nc.vector.tensor_copy(as_words(third[:]), as_rows(x_raw[1, 0][:]))
        last = laid("x_grouped1_1", [HALF, PACK], BF16, LATE)
        for cols, raw in zip(quarters, x_last):
            nc.vector.tensor_copy(as_words(last[:, cols, :]), as_rows(raw[:]))
        third_mx = quantize(third[:], "x1_0", X_AT[1, 1])
        last_codes, last_scale = quantize(last[:], "x1_1")

        res_rows = res.rearrange("(c p) m -> p c m", p=P)
        res_first = []
        for side in range(2):
            res_first.append(laid("res0_%d" % side, [2, HALF], F32, LAST_PART + side * SLOT))
            nc.sync.dma_start(res_first[side][:], res_rows[:, 2 * side : 2 * side + 2, 0:HALF])
        al8 = laid("al8", [N], I32, X_AT[1, 0] + GROUP)
        nc.sync.dma_start(al8[:], al8_words[0].rearrange("p n f -> p (n f)").bitcast(I32))
        al4 = laid("al4", [2 * N], U8, X_AT[1, 0])
        nc.sync.dma_start(al4[:].bitcast(I32), al4_words[0].bitcast(I32))
        place_rows(al_placed, al_staged, 0)
        res_second = laid("res1", [TILES, HALF], F32, LATE)
        nc.sync.dma_start(res_second[:], res_rows[:, :, HALF:M])
        out_rows = out.rearrange("(c p) m -> p c m", p=P)

        def dot_pass(dst, b, t, a, codes, scale, start, stop):
            col = PASS * b + P * t
            nc.tensor.matmul_mx(
                out=dst,
                lhsT=centres[b][a][:, 2 * P * t : 2 * P * (t + 1)].bitcast(E2M1),
                lhsT_scale=placed[:, a, col : col + P],
                rhs=codes.bitcast(E4M3),
                rhs_scale=scale,
                start=start,
                stop=stop,
            )

        def sum_pass(dst, b, c, mx, start, stop):
            if b == 0:
                weights = al8[:, P * c : P * (c + 1)].bitcast(E4M3)
            else:
                weights = al4[:, 2 * P * c : 2 * P * (c + 1)].bitcast(E2M1)
            nc.tensor.matmul_mx(
                out=dst,
                lhsT=weights,
                lhsT_scale=al_placed[:, b, P * c : P * (c + 1)],
                rhs=mx[0][:].bitcast(E4M3),
                rhs_scale=mx[1][:],
                start=start,
                stop=stop,
            )

        def square(dots, b, name):
            width = dots[0].shape[1]
            pairs = kept("pairs" + name, [2, width, 2], BF16)
            for t in range(PACK):
                nc.scalar.activation(
                    pairs[:, t // 2, :, t % 2],
                    dots[t],
                    ACT.Square,
                    bias=shift[:, b, t : t + 1],
                    scale=root[:, b, t : t + 1],
                )
            return pairs

        def weave(pairs, b, grouped):
            width = pairs.shape[2]
            signs = sign[:, b, :].rearrange("p (m u e) -> p m u e", m=1, u=2)
            nc.vector.tensor_tensor(
                grouped.rearrange("p m (u e) -> p m u e", u=2),
                pairs[:].rearrange("p u m e -> p m u e"),
                signs.to_broadcast([P, width, 2, 2]),
                ALU.mult,
            )
            return grouped

        def finish(sums, residual, name, rows, cols, offset=None):
            shape = [rows.stop - rows.start, cols.stop - cols.start]
            if offset is None:
                result = kept("result" + name, shape, F32)
            else:
                result = laid("result" + name, shape, F32, offset)
            nc.vector.tensor_tensor(result[:], sums, residual, ALU.add)
            nc.sync.dma_start(out_rows[:, rows, cols], result[:])

        def weigh(dots, b, name, grouped):
            width = dots[0].shape[1]
            squares = kept("squares" + name, [PACK, width], F32)
            for t in range(PACK):
                nc.scalar.activation(squares[:, t, :], dots[t], ACT.Square, bias=cb_sb[:, b, t : t + 1])
            weights = cw_sb[:, b, 0:PACK].rearrange("p (c t i) -> p c t i", c=1, i=1)
            shape = [P, width // PAIR, PACK, PAIR]
            nc.vector.tensor_tensor(as_words(grouped), as_rows(squares[:]), weights.to_broadcast(shape), ALU.mult)

        def dots_by_tile(name, b, mx, first_bank, ahead):
            width = mx[0][0].shape[1]
            tiles = [bank("dot%s_%d" % (name, t), [width], first_bank + t) for t in range(PACK)]
            order = [(t, 0) for t in range(ahead)] + [(t, 1) for t in range(ahead)]
            order = order + [(t, a) for t in range(ahead, PACK) for a in (1, 0)]
            for t, a in order:
                opens = a == (0 if t < ahead else 1)
                dot_pass(tiles[t][:], b, t, a, mx[a][0], mx[a][1], opens, not opens)
            return [tile[:] for tile in tiles]

        grouped00 = laid("h_grouped00", [HALF, PACK], BF16, X_AT[1, 1] + J + GROUP)
        for g, cols in enumerate(quarters):
            mx = [(codes[:, cols], scale[:, cols]) for codes, scale in x_first]
            dots = dots_by_tile("00_%d" % g, 0, mx, PACK * g, PACK * (1 - g))
            if g == 0:
                weigh(dots, 0, "00_0", grouped00[:, cols, :])
            else:
                weave(square(dots, 0, "00_1"), 0, grouped00[:, cols, :])
        dots01 = dots_by_tile("01", 1, [(codes[:], scale[:]) for codes, scale in x_first], 0, 0)
        x_second = [(third_mx[0][:], third_mx[1][:]), (last_codes[:], last_scale[:])]
        dots10 = dots_by_tile("10", 0, x_second, PACK, PACK)
        pairs01 = square(dots01, 1, "01")
        grouped01 = weave(pairs01, 1, laid("h_grouped01", [HALF, PACK], BF16, X_AT[1, 1] + J)[:])
        h00 = quantize(grouped00[:], "h00")
        h01 = quantize(grouped01, "h01", CODES)
        dots11 = []
        for g, number in enumerate((2, 4)):
            tile = bank("dot11_%d" % g, [PACK, P], number)
            for a in (1, 0):
                codes, scale = x_second[a]
                for t in range(PACK):
                    start, stop = a == 1 and t == 0, a == 0 and t == PACK - 1
                    dot_pass(tile[:, t, :], 1, t, a, codes[:, quarters[g]], scale[:, quarters[g]], start, stop)
            dots11.append([tile[:, t, :] for t in range(PACK)])

        sums0 = [bank("sum0_%d" % side, [2, HALF], side) for side in range(2)]
        for side in range(2):
            for b, mx in enumerate((h00, h01)):
                for i in range(2):
                    sum_pass(sums0[side][:, i, :], b, 2 * side + i, mx, b == 0 and i == 0, b == 1 and i == 1)

        grouped10 = kept("h_grouped10", [HALF, PACK], BF16)
        for g, cols in enumerate(quarters):
            weave(square([tile[:, cols] for tile in dots10], 0, "10_%d" % g), 0, grouped10[:, cols, :])
        finish(sums0[0][:], res_first[0][:], "0_0", slice(0, 2), slice(0, HALF))

        def weave_last(g):
            name = "11_%d" % g
            tile = laid("h_grouped" + name, [P, PACK], BF16, LAST_PART + g * GROUP // 2)
            return weave(square(dots11[g], 1, name), 1, tile[:])

        def finish_tile(i, offset=None):
            rows = slice(2 + i, 3 + i)
            finish(sums0[1][:, i : i + 1, :], res_first[1][:, i : i + 1, :], "0_1_%d" % i, rows, slice(0, HALF), offset)

        whole = bank("sum1_0", [TILES, P], 6)
        sides = [bank("sum1_1_%d" % side, [2, P], number) for side, number in enumerate((7, 3))]
        sums1 = [[whole[:, 0:2, :], whole[:, 2:4, :]], [tile[:] for tile in sides]]
        tiles_a_bank = (TILES, 2)

        def last_passes(g, grouped):
            h11 = quantize(grouped, "h11_%d" % g)
            for c in range(TILES):
                sum_pass(sums1[g][c // 2][:, c % 2, :], 1, c, h11, False, (c + 1) % tiles_a_bank[g] == 0)

        grouped = weave_last(0)
        h10 = quantize(grouped10[:], "h10", CODES)
        for g, cols in enumerate(quarters):
            mx = (h10[0][:, cols], h10[1][:, cols])
            for c in range(TILES):
                sum_pass(sums1[g][c // 2][:, c % 2, :], 0, c, mx, c % tiles_a_bank[g] == 0, False)
        last_passes(0, grouped)
        finish_tile(0)
        grouped = weave_last(1)
        finish_tile(1, ROOTS)
        last_passes(1, grouped)
        for g, cols in enumerate(quarters):
            for side in range(2):
                rows = slice(2 * side, 2 * side + 2)
                stored = slice(HALF + cols.start, HALF + cols.stop)
                finish(sums1[g][side], res_second[:, rows, cols], "1_%d_%d" % (g, side), rows, stored)
